import numpy as np
import ml_dtypes


def mxq(x, axis, fmt="e4m3"):
    dtype, down = {"e4m3": (ml_dtypes.float8_e4m3fn, 7), "e5m2": (ml_dtypes.float8_e5m2, 14)}[fmt]
    v = np.moveaxis(np.asarray(x, np.float32).astype(ml_dtypes.bfloat16).astype(np.float64), axis, -1)
    blocks = v.reshape(v.shape[:-1] + (-1, 32))
    amax = np.abs(blocks).max(-1, keepdims=True)
    byte = np.maximum(np.where(amax > 0, np.frexp(amax)[1] - 1 + 127, 0) - down, 1)
    scale = np.exp2(byte - 127.0)
    codes = (blocks / scale).astype(np.float32).astype(dtype).astype(np.float64)
    return np.moveaxis((codes * scale).reshape(v.shape), -1, axis)


WIDE = False


def mx_kscale(k):
    if not WIDE:
        return np.ones(k)
    levels = np.array([10, -10, 5, -5, 0])
    if k % 512:
        return np.exp2(np.random.permutation(np.resize(levels, k // 32))).repeat(32)
    a = np.empty((k // 512, 16))
    for p in range(k // 512):
        a[p, :8] = np.random.permutation(np.resize(levels, 8))
        for g in range(8):
            far = levels[np.abs(levels - a[p, g]) >= 10]
            a[p, g + 8] = far[np.random.randint(len(far))]
    return np.exp2(a.ravel()).repeat(32)


BF16 = ml_dtypes.bfloat16


def bf(x):
    return np.asarray(x, np.float32).astype(BF16)


def f64(x):
    return np.asarray(x).astype(np.float64)

E4M3FN = np.array([(-1.0 if i & 128 else 1.0) * ((1.0 + (i & 7) / 8.0) * 2.0 ** (((i >> 3) & 15) - 7) if i & 120 else (i & 7) * 2.0 ** -9) for i in range(256)])


def e4m3fn_bytes(y):
    return np.clip(np.asarray(y, np.float64), -448.0, 448.0).astype(np.float32).astype(ml_dtypes.float8_e4m3fn).view(np.uint8)


def e4m3fn_values(b):
    return E4M3FN[b]


P, S, T = 4096, 512, 1024


def setup_inputs():
    s = mx_kscale(P)
    t = mx_kscale(S)
    strength = np.exp(0.5 * np.random.standard_normal((P, 1)))
    G = np.random.standard_normal((P, S)) * strength / np.sqrt(P) * s[:, None]
    G_scale = (np.max(np.abs(G), axis=1, keepdims=True) / 448).astype(np.float32)
    G_bytes = e4m3fn_bytes(G / np.repeat(f64(G_scale), S, axis=1))
    sigma = 0.4 + 0.4 * np.random.random_sample(S)
    E = np.random.standard_normal((S, T)) * sigma[:, None] * t[:, None]
    Q = np.linalg.qr(np.random.standard_normal((S, S)))[0]
    V = Q / sigma[None, :] / t[None, :]
    return {"G_bytes": G_bytes,
            "G_scale": G_scale,
            "J": bf(np.random.standard_normal((P, T)) / s[:, None]),
            "gain": bf((1 + 0.1 * np.random.standard_normal(S)) * t),
            "E": bf(E),
            "V": bf(V)}


def reference(G_bytes, G_scale, J, gain, E, V):
    G = e4m3fn_values(G_bytes) * np.repeat(f64(G_scale), S, axis=1)
    Gq = mxq(G, 0, "e4m3")
    Jq = mxq(f64(J), 0, "e4m3")
    F = Gq.T @ Jq
    B = F * f64(gain)[:, None] + f64(E)
    Y = mxq(f64(V), 1, "e4m3") @ mxq(B, 0, "e4m3")
    return Y

@@ -1,0 +1,337 @@
+from contextlib import ExitStack
+
+import concourse.mybir as mybir
+from concourse.masks import make_identity
+
+SRC, SEN, TIM = 4096, 512, 1024
+FLOPS = 2 * SRC * SEN * TIM + 2 * SEN * SEN * TIM
+
+F32 = mybir.dt.float32
+BF16 = mybir.dt.bfloat16
+U32 = mybir.dt.uint32
+U8 = mybir.dt.uint8
+FP8 = mybir.dt.float8_e4m3fn
+FP8X4 = mybir.dt.float8_e4m3fn_x4
+MULT = mybir.AluOpType.mult
+ADD = mybir.AluOpType.add
+COPY = mybir.ActivationFunctionType.Copy
+
+P = 128
+PASSES = SRC // 512
+NCH = 2
+W = TIM // NCH
+
+CFG = {'sj': ((1, 3, 4, 7), (0, 2, 4, 5, 6)), 'vw': (2, 0, 0, 1, 1, 2, 1, 0), 'jfirst': 0, 'st': (1, 4, 4, 5), 'bi': (7, 1), 'bq': 7, 'ev': 8, 'vc': 5, 'vq': 7, 'tail': (0, 0), 'evv': (2, 3, 7), 'lag': 0, 'pj': ((3, 5, 7), ()), 'late': 0, 'gfirst': 1, 'form': 0}
+
+
+def tile_meg_forward_whitened_d3_kernel(tc, g_bytes, g_scale, j_in, gain_in, e_in, v_in, out):
+    nc = tc.nc
+
+    with ExitStack() as ctx:
+        keep = ctx.enter_context(tc.tile_pool(name="keep", bufs=1))
+        work = ctx.enter_context(tc.tile_pool(name="work", bufs=3))
+        psum = ctx.enter_context(tc.psum_pool(name="psum", bufs=1))
+
+        ident_raw = keep.tile([P, P], F32, name="ident_raw")
+        make_identity(nc, ident_raw[:])
+        ident = keep.tile([P, P], F32, name="ident")
+        nc.scalar.activation(out=ident[:], in_=ident_raw[:], func=COPY)
+
+        ident_b = keep.tile([P, P], BF16, name="ident_b")
+        nc.vector.tensor_copy(out=ident_b[:], in_=ident_raw[:])
+
+        gsc = {}
+        gs_view = g_scale.rearrange("(g p t) o -> p g (t o)", p=P, t=4)
+        gb_view = g_bytes.rearrange("(g p t) s -> g p t s", p=P, t=4)
+        j_view = j_in.rearrange("(g p t) n -> g p t n", p=P, t=4)
+        gb, jr = {}, {}
+
+        def load_g(g):
+            gb[g] = keep.tile([P, 4, SEN], U8, name="gb%d" % g, align_bytes=64)
+            gsc[g] = keep.tile([P, 1, 4], F32, name="gsc%d" % g)
+            nc.sync.dma_start(out=gsc[g][:], in_=gs_view[:, g:g + 1, :])
+            for t in range(0, 4, 2) if g == 0 else ():
+                nc.sync.dma_start(out=gb[g][:, t:t + 2, :], in_=gb_view[g][:, t:t + 2, :])
+            if g > 0:
+                nc.sync.dma_start(out=gb[g][:], in_=gb_view[g])
+
+        def load_j(c, g):
+            jr[c, g] = work.tile([P, 4, W], BF16, name="jr", bufs=12, align_bytes=64)
+            nc.sync.dma_start(out=jr[c, g][:], in_=j_view[g][:, :, c * W:(c + 1) * W])
+
+        v_raw = keep.tile([P, 4, SEN], BF16, name="v_raw", align_bytes=64)
+        for g in range(CFG["gfirst"]):
+            load_g(g)
+        for g in range(PASSES):
+            if g + CFG["gfirst"] < PASSES:
+                load_g(g + CFG["gfirst"])
+            load_j(0, g)
+            if g == 3:
+                nc.sync.dma_start(out=v_raw[:], in_=v_in.rearrange("(b p) s -> p b s", p=P))
+        gain = keep.tile([P, 4], BF16, name="gain")
+        nc.sync.dma_start(out=gain[:], in_=gain_in.rearrange("(p t) -> p t", t=4))
+        for g in range(PASSES):
+            load_j(1, g)
+            if g == 3:
+                e_sb = keep.tile([P, 4, TIM], BF16, name="e_sb", align_bytes=64)
+                nc.sync.dma_start(out=e_sb[:], in_=e_in.rearrange("(p t) n -> p t n", t=4))
+
+        gw, gi, ji = {}, {}, {}
+        gc, gs, jc, js = {}, {}, {}, {}
+        acc = {}
+        bank_of = {0: 0, 1: 0 if CFG["late"] else 4}
+        turn = [0]
+
+        def widen(g, t, on_vector=False):
+            if t == 0:
+                gw[g] = work.tile([P, 4, SEN], BF16, name="gw", align_bytes=64)
+            sc = gsc[g][:, 0, t:t + 1]
+            src = gb[g][:, t, :].bitcast(FP8)
+            if on_vector:
+                nc.vector.tensor_scalar(out=gw[g][:, t, :], in0=src, scalar1=sc, scalar2=None, op0=MULT)
+            else:
+                nc.scalar.activation(out=gw[g][:, t, :], in_=src, func=COPY, scale=sc)
+
+        def g_interleave(g):
+            gi[g] = work.tile([P, SEN, 4], BF16, name="gi", align_bytes=64)
+            nc.vector.tensor_copy(
+                out=gi[g][:].rearrange("p (t m) j -> p m j t", t=4),
+                in_=gw[g][:].rearrange("p j (m t) -> p m j t", t=4),
+            )
+
+        def g_quant(g):
+            gc[g] = keep.tile([P, SEN], U32, name="gc%d" % g, align_bytes=64)
+            gs[g] = keep.tile([P, SEN], U8, name="gs%d" % g, align_bytes=64)
+            nc.vector.quantize_mx(
+                out=gc[g][:].bitcast(FP8X4), scales=gs[g][:], in_=gi[g][:].rearrange("p n t -> p (n t)")
+            )
+
+        def j_interleave(c, g, on_scalar):
+            ji[c, g] = work.tile([P, W, 4], BF16, name="ji", bufs=6, align_bytes=64)
+            dst = ji[c, g][:].rearrange("p (c i) t -> p c t i", i=4)
+            src = jr[c, g][:].rearrange("p t (c i) -> p c t i", i=4)
+            if on_scalar:
+                nc.scalar.copy(out=dst, in_=src)
+            else:
+                nc.vector.tensor_copy(out=dst, in_=src)
+
+        packed = {}
+
+        def next_bank():
+            turn[0] += 1
+            return "bank%d" % (4 + (turn[0] - 1) % 4)
+
+        def pe_pack(g):
+            for q in range(2):
+                packed[g, q] = psum.tile([P, 1024], BF16, name=next_bank())
+                for h in range(2):
+                    n0 = 256 * q + 128 * h
+                    nc.tensor.matmul(
+                        out=packed[g, q][:, 512 * h:512 * (h + 1)].rearrange("p (n t) -> p t n", t=4),
+                        lhsT=ident_b[:],
+                        rhs=jr[0, g][:, :, n0:n0 + 128],
+                        start=True,
+                        stop=True,
+                    )
+
+        def pe_fetch(g):
+            ji[0, g] = work.tile([P, W, 4], BF16, name="ji", bufs=6, align_bytes=64)
+            flat = ji[0, g][:].rearrange("p n t -> p (n t)")
+            for q in range(2):
+                nc.scalar.copy(out=flat[:, 1024 * q:1024 * (q + 1)], in_=packed[g, q][:])
+
+        def j_quant(c, g):
+            jc[c, g] = keep.tile([P, W], U32, name="jc%d_%d" % (c, g), align_bytes=64)
+            js[c, g] = keep.tile([P, W], U8, name="js%d_%d" % (c, g), align_bytes=64)
+            nc.vector.quantize_mx(
+                out=jc[c, g][:].bitcast(FP8X4), scales=js[c, g][:], in_=ji[c, g][:].rearrange("p n t -> p (n t)")
+            )
+
+        def stage1(c, g):
+            for m in range(4):
+                if g == 0:
+                    acc[c, m] = psum.tile([P, W], F32, name="bank%d" % (bank_of[c] + m))
+                nc.tensor.matmul_mx(
+                    out=acc[c, m][:],
+                    lhsT=gc[g][:, m * P:(m + 1) * P].bitcast(FP8X4),
+                    lhsT_scale=gs[g][:, m * P:(m + 1) * P],
+                    rhs=jc[c, g][:].bitcast(FP8X4),
+                    rhs_scale=js[c, g][:],
+                    start=(g == 0),
+                    stop=(g == PASSES - 1),
+                )
+
+        v_grp = keep.tile([P, SEN, 4], BF16, name="v_grp", align_bytes=64)
+        v_codes = keep.tile([P, SEN], U32, name="v_codes", align_bytes=64)
+        v_scales = keep.tile([P, SEN], U8, name="v_scales", align_bytes=64)
+        vt = {}
+
+        def v_transpose():
+            words = v_raw[:].rearrange("p b s -> p (b s)").bitcast(F32)
+            for h in range(2):
+                vt[h] = psum.tile([P, 2, 2, P], F32, name=next_bank())
+                for b in range(2):
+                    for u in range(2):
+                        w0 = (2 * h + b) * 256
+                        nc.tensor.transpose(vt[h][:, b, u, :], words[:, w0 + u:w0 + 256:2], ident[:])
+
+        def v_copy(h):
+            dst = v_grp[:].rearrange("p w t -> p (w t)").bitcast(F32)[:, 512 * h:512 * (h + 1)]
+            nc.scalar.copy(
+                out=dst.rearrange("p (b r u) -> p b r u", b=2, u=2), in_=vt[h][:].rearrange("p b u r -> p b r u")
+            )
+
+        def v_quant():
+            nc.vector.quantize_mx(
+                out=v_codes[:].bitcast(FP8X4), scales=v_scales[:], in_=v_grp[:].rearrange("p w t -> p (w t)")
+            )
+
+        bp, bi, bc, bs, y, acc2 = {}, {}, {}, {}, {}, {}
+
+        def gain_noise(c, m, h, parts):
+            n = W // parts
+            if m == 0:
+                bp[c, h] = work.tile([P, 4, n], BF16, name="bp%d" % n, bufs=parts, align_bytes=64)
+            nc.vector.scalar_tensor_tensor(
+                out=bp[c, h][:, m, :],
+                in0=acc[c, m][:, h * n:(h + 1) * n],
+                scalar=gain[:, m:m + 1],
+                in1=e_sb[:, m, c * W + h * n:c * W + (h + 1) * n],
+                op0=MULT,
+                op1=ADD,
+            )
+
+        def b_interleave(c, h, parts, on_scalar):
+            n = W // parts
+            bi[c, h] = work.tile([P, n, 4], BF16, name="bi%d" % n, bufs=parts, align_bytes=64)
+            dst = bi[c, h][:].rearrange("p (c i) t -> p c t i", i=4)
+            src = bp[c, h][:].rearrange("p t (c i) -> p c t i", i=4)
+            if on_scalar:
+                nc.scalar.copy(out=dst, in_=src)
+            else:
+                nc.vector.tensor_copy(out=dst, in_=src)
+
+        def b_quant(c, h, parts):
+            n = W // parts
+            bc[c, h] = work.tile([P, n], U32, name="bc%d" % n, bufs=parts, align_bytes=64)
+            bs[c, h] = work.tile([P, n], U8, name="bs%d" % n, bufs=parts, align_bytes=64)
+            nc.vector.quantize_mx(
+                out=bc[c, h][:].bitcast(FP8X4), scales=bs[c, h][:], in_=bi[c, h][:].rearrange("p n t -> p (n t)")
+            )
+
+        def stage2(c, h, parts):
+            n = W // parts
+            for b in range(4):
+                bank = ((4 if CFG["late"] else 0) if c == 0 else 4 * h) + b
+                if c == 1 and CFG["late"]:
+                    bank = 4 * (1 - h) + b
+                acc2[c, h, b] = psum.tile([P, n], F32, name="bank%d" % bank)
+                nc.tensor.matmul_mx(
+                    out=acc2[c, h, b][:],
+                    lhsT=v_codes[:, b * P:(b + 1) * P].bitcast(FP8X4),
+                    lhsT_scale=v_scales[:, b * P:(b + 1) * P],
+                    rhs=bc[c, h][:].bitcast(FP8X4),
+                    rhs_scale=bs[c, h][:],
+                    start=True,
+                    stop=True,
+                )
+
+        def finish(c, h, b, parts, on_scalar):
+            n = W // parts
+            y = work.tile([P, n], F32, name="y%d" % n, bufs=4 * parts)
+            if on_scalar:
+                nc.scalar.copy(out=y[:], in_=acc2[c, h, b][:])
+            else:
+                nc.vector.tensor_copy(out=y[:], in_=acc2[c, h, b][:])
+            nc.sync.dma_start(out=out[b * P:(b + 1) * P, c * W + h * n:c * W + (h + 1) * n], in_=y[:])
+
+        with tc.manual_schedule():
+            pending = []
+
+            held = []
+
+            def flush(keep_back):
+                while len(pending) > keep_back:
+                    c, g = pending.pop(0)
+                    j_quant(c, g)
+                    if CFG["late"] and c == 1 and not bp.get("done"):
+                        held.append(g)
+                    else:
+                        stage1(c, g)
+
+            def widen_all(g):
+                for t in range(4):
+                    widen(g, t, on_vector=t >= 4 - CFG["vw"][g])
+
+            widen_all(0)
+            for g in range(PASSES):
+                on_scalar = g in CFG["sj"][0]
+                on_scalar = on_scalar or g in CFG["pj"][0]
+                do_s = lambda c, g: pe_fetch(g) if g in CFG["pj"][0] else j_interleave(c, g, True)
+                if g == 0 and 0 in CFG["pj"][0]:
+                    pe_pack(0)
+                if on_scalar and CFG["jfirst"]:
+                    do_s(0, g)
+                if g + 1 < PASSES:
+                    widen_all(g + 1)
+                if on_scalar and not CFG["jfirst"]:
+                    do_s(0, g)
+                if g + 1 in CFG["pj"][0]:
+                    pe_pack(g + 1)
+                if g == CFG["vc"]:
+                    v_transpose()
+                    v_copy(0)
+                    v_copy(1)
+                g_interleave(g)
+                if not on_scalar:
+                    j_interleave(0, g, False)
+                flush(CFG["lag"])
+                g_quant(g)
+                pending.append((0, g))
+                if not on_scalar:
+                    flush(CFG["lag"])
+            for g in range(PASSES):
+                on_scalar = g in CFG["sj"][1]
+                on_scalar = on_scalar or g in CFG["pj"][1]
+                j_interleave(1, g, on_scalar)
+                flush(0 if g == 0 else CFG["lag"])
+                if g == CFG["vq"]:
+                    v_quant()
+                for m in range(4):
+                    if CFG["st"][m] == g:
+                        gain_noise(0, m, 0, 1)
+                        if m == 3:
+                            bp["done"] = True
+                            for k in held:
+                                stage1(1, k)
+                            held.clear()
+                pending.append((1, g))
+                if not on_scalar:
+                    flush(CFG["lag"])
+                if g == CFG["bi"][0]:
+                    b_interleave(0, 0, 1, CFG["bi"][1])
+                if g == CFG["bq"]:
+                    b_quant(0, 0, 1)
+                    stage2(0, 0, 1)
+                if g == CFG["ev"]:
+                    for b in range(4):
+                        finish(0, 0, b, 1, True)
+            flush(0)
+            for h in range(2):
+                for m in range(4):
+                    gain_noise(1, m, h, 2)
+                if h == 0 and CFG["bq"] == 8:
+                    b_quant(0, 0, 1)
+                    stage2(0, 0, 1)
+                if h == 0 and CFG["ev"] == 8:
+                    for b in range(4):
+                        finish(0, 0, b, 1, True)
+                if h == 1:
+                    b_quant(1, 0, 2)
+                    stage2(1, 0, 2)
+                b_interleave(1, h, 2, CFG["tail"][h])
+            b_quant(1, 1, 2)
+            stage2(1, 1, 2)
+            for h in range(2):
+                for b in range(4):
+                    finish(1, h, b, 2, (4 * h + b) not in CFG["evv"])

@@ -18,10 +18,10 @@ COPY = mybir.ActivationFunctionType.Copy
 
 P = 128
 PASSES = SRC // 512
-NCH = 2
-W = TIM // NCH
-
-CFG = {'sj': ((1, 3, 4, 7), (0, 2, 4, 5, 6)), 'vw': (2, 0, 0, 1, 1, 2, 1, 0), 'jfirst': 0, 'st': (1, 4, 4, 5), 'bi': (7, 1), 'bq': 7, 'ev': 8, 'vc': 5, 'vq': 7, 'tail': (0, 0), 'evv': (2, 3, 7), 'lag': 0, 'pj': ((3, 5, 7), ()), 'late': 0, 'gfirst': 1, 'form': 0}
+WIDE, MID, LAST = (0, 512), (512, 256), (768, 256)
+LAST_A, LAST_B = (768, 128), (896, 128)
+ROUTED = (1, 2, 3, 4, 5, 6)
+HALVED = 2
 
 
 def tile_meg_forward_whitened_d3_kernel(tc, g_bytes, g_scale, j_in, gain_in, e_in, v_in, out):
@@ -31,307 +31,329 @@ def tile_meg_forward_whitened_d3_kernel(tc, g_bytes, g_scale, j_in, gain_in, e_i
         keep = ctx.enter_context(tc.tile_pool(name="keep", bufs=1))
         work = ctx.enter_context(tc.tile_pool(name="work", bufs=3))
         psum = ctx.enter_context(tc.psum_pool(name="psum", bufs=1))
+        ctx.enter_context(tc.manual_schedule())
 
-        ident_raw = keep.tile([P, P], F32, name="ident_raw")
-        make_identity(nc, ident_raw[:])
-        ident = keep.tile([P, P], F32, name="ident")
-        nc.scalar.activation(out=ident[:], in_=ident_raw[:], func=COPY)
-
+        zeros = keep.tile([P, P], F32, name="zeros")
+        nc.vector.memset(zeros[:], 0.0)
         ident_b = keep.tile([P, P], BF16, name="ident_b")
-        nc.vector.tensor_copy(out=ident_b[:], in_=ident_raw[:])
+        make_identity(nc, ident_b[:])
+        ident = keep.tile([P, P], F32, name="ident")
+        nc.scalar.activation(out=ident[:], in_=zeros[:], func=COPY)
+        make_identity(nc, ident[:], nomemset=True)
 
-        gsc = {}
         gs_view = g_scale.rearrange("(g p t) o -> p g (t o)", p=P, t=4)
         gb_view = g_bytes.rearrange("(g p t) s -> g p t s", p=P, t=4)
         j_view = j_in.rearrange("(g p t) n -> g p t n", p=P, t=4)
-        gb, jr = {}, {}
+        e_view = e_in.rearrange("(p u) n -> p u n", u=4)
+        g_raw, j_raw, g_sc, noise = {}, {}, {}, {}
+
+        def load_scales(g0, g1):
+            tile = keep.tile([P, g1 - g0, 4], F32, name="g_sc%d" % g0)
+            nc.sync.dma_start(out=tile[:], in_=gs_view[:, g0:g1, :])
+            for g in range(g0, g1):
+                g_sc[g] = tile[:, g - g0, :]
 
         def load_g(g):
-            gb[g] = keep.tile([P, 4, SEN], U8, name="gb%d" % g, align_bytes=64)
-            gsc[g] = keep.tile([P, 1, 4], F32, name="gsc%d" % g)
-            nc.sync.dma_start(out=gsc[g][:], in_=gs_view[:, g:g + 1, :])
-            for t in range(0, 4, 2) if g == 0 else ():
-                nc.sync.dma_start(out=gb[g][:, t:t + 2, :], in_=gb_view[g][:, t:t + 2, :])
-            if g > 0:
-                nc.sync.dma_start(out=gb[g][:], in_=gb_view[g])
+            g_raw[g] = keep.tile([P, 4, SEN], U8, name="g_raw%d" % g, align_bytes=64)
+            for t0, t1 in ((0, 2), (2, 4)) if g == 0 else ((0, 4),):
+                nc.sync.dma_start(out=g_raw[g][:, t0:t1, :], in_=gb_view[g][:, t0:t1, :])
 
-        def load_j(c, g):
-            jr[c, g] = work.tile([P, 4, W], BF16, name="jr", bufs=12, align_bytes=64)
-            nc.sync.dma_start(out=jr[c, g][:], in_=j_view[g][:, :, c * W:(c + 1) * W])
+        def load_j(g, n0, n1):
+            tile = keep.tile([P, 4, n1 - n0], BF16, name="j_raw%d_%d" % (g, n0), align_bytes=64)
+            nc.sync.dma_start(out=tile[:], in_=j_view[g][:, :, n0:n1])
+            for first, width in (WIDE, MID, LAST):
+                if n0 <= first < n1:
+                    j_raw[g, first] = tile[:, :, first - n0:first - n0 + width]
+
+        def load_noise(n0, n1):
+            tile = keep.tile([P, 4, n1 - n0], BF16, name="noise%d" % n0, align_bytes=64)
+            nc.sync.dma_start(out=tile[:], in_=e_view[:, :, n0:n1])
+            for first, width in (WIDE, MID, LAST, LAST_A, LAST_B):
+                if n0 <= first < n1:
+                    noise[first, width] = tile[:, :, first - n0:first - n0 + width]
 
         v_raw = keep.tile([P, 4, SEN], BF16, name="v_raw", align_bytes=64)
-        for g in range(CFG["gfirst"]):
-            load_g(g)
-        for g in range(PASSES):
-            if g + CFG["gfirst"] < PASSES:
-                load_g(g + CFG["gfirst"])
-            load_j(0, g)
-            if g == 3:
-                nc.sync.dma_start(out=v_raw[:], in_=v_in.rearrange("(b p) s -> p b s", p=P))
         gain = keep.tile([P, 4], BF16, name="gain")
-        nc.sync.dma_start(out=gain[:], in_=gain_in.rearrange("(p t) -> p t", t=4))
-        for g in range(PASSES):
-            load_j(1, g)
-            if g == 3:
-                e_sb = keep.tile([P, 4, TIM], BF16, name="e_sb", align_bytes=64)
-                nc.sync.dma_start(out=e_sb[:], in_=e_in.rearrange("(p t) n -> p t n", t=4))
 
-        gw, gi, ji = {}, {}, {}
-        gc, gs, jc, js = {}, {}, {}, {}
-        acc = {}
-        bank_of = {0: 0, 1: 0 if CFG["late"] else 4}
-        turn = [0]
+        def load_v():
+            nc.sync.dma_start(out=v_raw[:], in_=v_in.rearrange("(b p) s -> p b s", p=P))
 
-        def widen(g, t, on_vector=False):
-            if t == 0:
-                gw[g] = work.tile([P, 4, SEN], BF16, name="gw", align_bytes=64)
-            sc = gsc[g][:, 0, t:t + 1]
-            src = gb[g][:, t, :].bitcast(FP8)
-            if on_vector:
-                nc.vector.tensor_scalar(out=gw[g][:, t, :], in0=src, scalar1=sc, scalar2=None, op0=MULT)
-            else:
-                nc.scalar.activation(out=gw[g][:, t, :], in_=src, func=COPY, scale=sc)
+        def load_gain():
+            nc.sync.dma_start(out=gain[:], in_=gain_in.rearrange("(p u) -> p u", u=4))
 
-        def g_interleave(g):
-            gi[g] = work.tile([P, SEN, 4], BF16, name="gi", align_bytes=64)
-            nc.vector.tensor_copy(
-                out=gi[g][:].rearrange("p (t m) j -> p m j t", t=4),
-                in_=gw[g][:].rearrange("p j (m t) -> p m j t", t=4),
-            )
+        load_scales(0, 2)
+        load_g(0)
+        load_g(1)
+        load_j(0, 0, 512)
+        load_g(2)
+        load_scales(2, PASSES)
+        for g in range(1, PASSES):
+            if 2 < g + 1 < PASSES:
+                load_g(g + 1)
+            load_j(g, 0, 512 if g < HALVED else TIM)
+        load_v()
+        load_gain()
+        load_noise(0, 512)
+        for g in range(HALVED):
+            load_j(g, 512, TIM)
+        load_noise(512, TIM)
 
-        def g_quant(g):
-            gc[g] = keep.tile([P, SEN], U32, name="gc%d" % g, align_bytes=64)
-            gs[g] = keep.tile([P, SEN], U8, name="gs%d" % g, align_bytes=64)
+        def quantize(name, pool, grouped, width):
+            codes = pool.tile([P, width], U32, name="codes_" + name, align_bytes=64)
+            scales = pool.tile([P, width], U8, name="scales_" + name, align_bytes=64)
             nc.vector.quantize_mx(
-                out=gc[g][:].bitcast(FP8X4), scales=gs[g][:], in_=gi[g][:].rearrange("p n t -> p (n t)")
+                out=codes[:].bitcast(FP8X4), scales=scales[:], in_=grouped[:].rearrange("p n t -> p (n t)")
             )
+            return codes, scales
 
-        def j_interleave(c, g, on_scalar):
-            ji[c, g] = work.tile([P, W, 4], BF16, name="ji", bufs=6, align_bytes=64)
-            dst = ji[c, g][:].rearrange("p (c i) t -> p c t i", i=4)
-            src = jr[c, g][:].rearrange("p t (c i) -> p c t i", i=4)
+        def interleave(on_scalar, grouped, planes):
+            dst = grouped.rearrange("p (c i) t -> p c t i", i=4)
+            src = planes.rearrange("p t (c i) -> p c t i", i=4)
             if on_scalar:
                 nc.scalar.copy(out=dst, in_=src)
             else:
                 nc.vector.tensor_copy(out=dst, in_=src)
 
-        packed = {}
+        g_wide, g_grp, g_mx, g_psum = {}, {}, {}, {}
 
-        def next_bank():
-            turn[0] += 1
-            return "bank%d" % (4 + (turn[0] - 1) % 4)
+        def widen(g, t, on_vector=False):
+            if g not in g_wide:
+                g_wide[g] = work.tile([P, 4, SEN], BF16, name="g_wide", align_bytes=64)
+            scale = g_sc[g][:, t:t + 1]
+            src = g_raw[g][:, t, :].bitcast(FP8)
+            if on_vector:
+                nc.vector.tensor_scalar(out=g_wide[g][:, t, :], in0=src, scalar1=scale, scalar2=None, op0=MULT)
+            else:
+                nc.scalar.activation(out=g_wide[g][:, t, :], in_=src, func=COPY, scale=scale)
 
-        def pe_pack(g):
+        def g_interleave(g):
+            g_grp[g] = work.tile([P, SEN, 4], BF16, name="g_grp", align_bytes=64)
+            nc.vector.tensor_copy(
+                out=g_grp[g][:].rearrange("p (u m) t -> p m t u", u=4),
+                in_=g_wide[g][:].rearrange("p t (m u) -> p m t u", u=4),
+            )
+
+        def g_route(g):
+            bank = 4 + 2 * (ROUTED.index(g) % 2)
             for q in range(2):
-                packed[g, q] = psum.tile([P, 1024], BF16, name=next_bank())
-                for h in range(2):
-                    n0 = 256 * q + 128 * h
+                g_psum[g, q] = psum.tile([P, 4, 64, 4], BF16, name="bank%d" % (bank + q))
+            for t0 in (0, 2):
+                for q in range(2):
                     nc.tensor.matmul(
-                        out=packed[g, q][:, 512 * h:512 * (h + 1)].rearrange("p (n t) -> p t n", t=4),
+                        out=g_psum[g, q][:, :, :, t0:t0 + 2].rearrange("p u m t -> p t m u"),
                         lhsT=ident_b[:],
-                        rhs=jr[0, g][:, :, n0:n0 + 128],
+                        rhs=g_wide[g][:, t0:t0 + 2, 256 * q:256 * (q + 1)].rearrange("p t (m u) -> p t m u", u=4),
                         start=True,
                         stop=True,
                     )
 
-        def pe_fetch(g):
-            ji[0, g] = work.tile([P, W, 4], BF16, name="ji", bufs=6, align_bytes=64)
-            flat = ji[0, g][:].rearrange("p n t -> p (n t)")
+        def g_fetch(g):
+            g_grp[g] = work.tile([P, SEN, 4], BF16, name="g_grp", align_bytes=64)
+            dst = g_grp[g][:].rearrange("p (u m) t -> p u (m t)", u=4).bitcast(F32)
             for q in range(2):
-                nc.scalar.copy(out=flat[:, 1024 * q:1024 * (q + 1)], in_=packed[g, q][:])
+                nc.scalar.copy(
+                    out=dst[:, :, 128 * q:128 * (q + 1)],
+                    in_=g_psum[g, q][:].rearrange("p u m t -> p u (m t)").bitcast(F32),
+                )
 
-        def j_quant(c, g):
-            jc[c, g] = keep.tile([P, W], U32, name="jc%d_%d" % (c, g), align_bytes=64)
-            js[c, g] = keep.tile([P, W], U8, name="js%d_%d" % (c, g), align_bytes=64)
-            nc.vector.quantize_mx(
-                out=jc[c, g][:].bitcast(FP8X4), scales=js[c, g][:], in_=ji[c, g][:].rearrange("p n t -> p (n t)")
+        def g_quant(g):
+            g_mx[g] = quantize("g%d" % g, keep, g_grp[g], SEN)
+
+        j_grp, j_mx, field = {}, {}, {}
+
+        def j_interleave(g, cols, on_scalar=False):
+            first, width = cols
+            j_grp[g, first] = work.tile(
+                [P, width, 4], BF16, name="j_grp%d" % width, bufs=3 if cols == WIDE else 11, align_bytes=64
             )
+            interleave(on_scalar, j_grp[g, first][:], j_raw[g, first])
 
-        def stage1(c, g):
-            for m in range(4):
-                if g == 0:
-                    acc[c, m] = psum.tile([P, W], F32, name="bank%d" % (bank_of[c] + m))
+        def j_quant(g, cols):
+            first, width = cols
+            if cols == WIDE:
+                j_mx[g, first] = quantize("j_wide", work, j_grp[g, first], width)
+            else:
+                j_mx[g, first] = quantize("j%d_%d" % (first, g), keep, j_grp[g, first], width)
+
+        def bank_tiles(first_bank, banks, width):
+            per_bank = 4 // banks
+            tiles = []
+            for b in range(banks):
+                tile = psum.tile([P, per_bank, width], F32, name="bank%d" % (first_bank + b))
+                tiles.append(tile)
+            return tiles, per_bank
+
+        done = {WIDE: [], MID: [], LAST: []}
+
+        def forward(g, cols):
+            if not done[cols]:
+                field[cols] = bank_tiles({WIDE: 0, MID: 6, LAST: 4}[cols], cols[1] // P, cols[1])
+            done[cols].append(g)
+            tiles, per_bank = field[cols]
+            codes, scales = j_mx[g, cols[0]]
+            for u in range(4):
                 nc.tensor.matmul_mx(
-                    out=acc[c, m][:],
-                    lhsT=gc[g][:, m * P:(m + 1) * P].bitcast(FP8X4),
-                    lhsT_scale=gs[g][:, m * P:(m + 1) * P],
-                    rhs=jc[c, g][:].bitcast(FP8X4),
-                    rhs_scale=js[c, g][:],
-                    start=(g == 0),
-                    stop=(g == PASSES - 1),
+                    out=tiles[u // per_bank][:, u % per_bank, :],
+                    lhsT=g_mx[g][0][:, u * P:(u + 1) * P].bitcast(FP8X4),
+                    lhsT_scale=g_mx[g][1][:, u * P:(u + 1) * P],
+                    rhs=codes[:].bitcast(FP8X4),
+                    rhs_scale=scales[:],
+                    start=(len(done[cols]) == 1 and u % per_bank == 0),
+                    stop=(len(done[cols]) == PASSES and u % per_bank == per_bank - 1),
                 )
 
         v_grp = keep.tile([P, SEN, 4], BF16, name="v_grp", align_bytes=64)
-        v_codes = keep.tile([P, SEN], U32, name="v_codes", align_bytes=64)
-        v_scales = keep.tile([P, SEN], U8, name="v_scales", align_bytes=64)
-        vt = {}
+        v_mx, v_psum = [], []
 
-        def v_transpose():
+        def v_turn():
             words = v_raw[:].rearrange("p b s -> p (b s)").bitcast(F32)
             for h in range(2):
-                vt[h] = psum.tile([P, 2, 2, P], F32, name=next_bank())
+                turned = psum.tile([P, 2, 2, P], F32, name="bank%d" % (4 + h))
+                v_psum.append(turned)
                 for b in range(2):
                     for u in range(2):
                         w0 = (2 * h + b) * 256
-                        nc.tensor.transpose(vt[h][:, b, u, :], words[:, w0 + u:w0 + 256:2], ident[:])
+                        nc.tensor.transpose(turned[:, b, u, :], words[:, w0 + u:w0 + 256:2], ident[:])
 
-        def v_copy(h):
-            dst = v_grp[:].rearrange("p w t -> p (w t)").bitcast(F32)[:, 512 * h:512 * (h + 1)]
-            nc.scalar.copy(
-                out=dst.rearrange("p (b r u) -> p b r u", b=2, u=2), in_=vt[h][:].rearrange("p b u r -> p b r u")
-            )
+        def v_fetch():
+            for h in range(2):
+                dst = v_grp[:].rearrange("p w t -> p (w t)").bitcast(F32)[:, 512 * h:512 * (h + 1)]
+                nc.scalar.copy(
+                    out=dst.rearrange("p (b r u) -> p b r u", b=2, u=2),
+                    in_=v_psum[h][:].rearrange("p b u r -> p b r u"),
+                )
 
         def v_quant():
-            nc.vector.quantize_mx(
-                out=v_codes[:].bitcast(FP8X4), scales=v_scales[:], in_=v_grp[:].rearrange("p w t -> p (w t)")
-            )
+            v_mx.extend(quantize("v", keep, v_grp, SEN))
 
-        bp, bi, bc, bs, y, acc2 = {}, {}, {}, {}, {}, {}
+        b_planes, b_grp, b_mx, white = {}, {}, {}, {}
 
-        def gain_noise(c, m, h, parts):
-            n = W // parts
-            if m == 0:
-                bp[c, h] = work.tile([P, 4, n], BF16, name="bp%d" % n, bufs=parts, align_bytes=64)
-            nc.vector.scalar_tensor_tensor(
-                out=bp[c, h][:, m, :],
-                in0=acc[c, m][:, h * n:(h + 1) * n],
-                scalar=gain[:, m:m + 1],
-                in1=e_sb[:, m, c * W + h * n:c * W + (h + 1) * n],
-                op0=MULT,
-                op1=ADD,
-            )
+        def record(cols, within, planes=range(4)):
+            first, width = cols
+            if cols not in b_planes:
+                b_planes[cols] = work.tile([P, 4, width], BF16, name="g_wide", align_bytes=64)
+            tiles, per_bank = field[within]
+            for u in planes:
+                nc.vector.scalar_tensor_tensor(
+                    out=b_planes[cols][:, u, :],
+                    in0=tiles[u // per_bank][:, u % per_bank, first - within[0]:first - within[0] + width],
+                    scalar=gain[:, u:u + 1],
+                    in1=noise[cols][:, u, :],
+                    op0=MULT,
+                    op1=ADD,
+                )
 
-        def b_interleave(c, h, parts, on_scalar):
-            n = W // parts
-            bi[c, h] = work.tile([P, n, 4], BF16, name="bi%d" % n, bufs=parts, align_bytes=64)
-            dst = bi[c, h][:].rearrange("p (c i) t -> p c t i", i=4)
-            src = bp[c, h][:].rearrange("p t (c i) -> p c t i", i=4)
-            if on_scalar:
-                nc.scalar.copy(out=dst, in_=src)
-            else:
-                nc.vector.tensor_copy(out=dst, in_=src)
+        def b_interleave(cols, on_scalar=False):
+            b_grp[cols] = keep.tile([P, cols[1], 4], BF16, name="b_grp%d" % cols[0], align_bytes=64)
+            interleave(on_scalar, b_grp[cols][:], b_planes[cols][:])
 
-        def b_quant(c, h, parts):
-            n = W // parts
-            bc[c, h] = work.tile([P, n], U32, name="bc%d" % n, bufs=parts, align_bytes=64)
-            bs[c, h] = work.tile([P, n], U8, name="bs%d" % n, bufs=parts, align_bytes=64)
-            nc.vector.quantize_mx(
-                out=bc[c, h][:].bitcast(FP8X4), scales=bs[c, h][:], in_=bi[c, h][:].rearrange("p n t -> p (n t)")
-            )
+        def b_quant(cols):
+            b_mx[cols] = quantize("b%d" % cols[0], keep, b_grp[cols], cols[1])
 
-        def stage2(c, h, parts):
-            n = W // parts
+        def whiten(cols, first_bank, banks):
+            white[cols] = bank_tiles(first_bank, banks, cols[1])
+            tiles, per_bank = white[cols]
             for b in range(4):
-                bank = ((4 if CFG["late"] else 0) if c == 0 else 4 * h) + b
-                if c == 1 and CFG["late"]:
-                    bank = 4 * (1 - h) + b
-                acc2[c, h, b] = psum.tile([P, n], F32, name="bank%d" % bank)
                 nc.tensor.matmul_mx(
-                    out=acc2[c, h, b][:],
-                    lhsT=v_codes[:, b * P:(b + 1) * P].bitcast(FP8X4),
-                    lhsT_scale=v_scales[:, b * P:(b + 1) * P],
-                    rhs=bc[c, h][:].bitcast(FP8X4),
-                    rhs_scale=bs[c, h][:],
+                    out=tiles[b // per_bank][:, b % per_bank, :],
+                    lhsT=v_mx[0][:, b * P:(b + 1) * P].bitcast(FP8X4),
+                    lhsT_scale=v_mx[1][:, b * P:(b + 1) * P],
+                    rhs=b_mx[cols][0][:].bitcast(FP8X4),
+                    rhs_scale=b_mx[cols][1][:],
                     start=True,
                     stop=True,
                 )
 
-        def finish(c, h, b, parts, on_scalar):
-            n = W // parts
-            y = work.tile([P, n], F32, name="y%d" % n, bufs=4 * parts)
+        out_view = out.rearrange("(b p) n -> p b n", p=P)
+
+        def finish(cols, i, on_scalar=True):
+            first, width = cols
+            tiles, per_bank = white[cols]
+            y = keep.tile([P, per_bank, width], F32, name="y%d_%d" % (first, i))
             if on_scalar:
-                nc.scalar.copy(out=y[:], in_=acc2[c, h, b][:])
+                nc.scalar.copy(out=y[:], in_=tiles[i][:])
             else:
-                nc.vector.tensor_copy(out=y[:], in_=acc2[c, h, b][:])
-            nc.sync.dma_start(out=out[b * P:(b + 1) * P, c * W + h * n:c * W + (h + 1) * n], in_=y[:])
+                nc.vector.tensor_copy(out=y[:], in_=tiles[i][:])
+            nc.sync.dma_start(out=out_view[:, i * per_bank:(i + 1) * per_bank, first:first + width], in_=y[:])
 
-        with tc.manual_schedule():
-            pending = []
+        def qf(g, cols):
+            j_quant(g, cols)
+            forward(g, cols)
 
-            held = []
-
-            def flush(keep_back):
-                while len(pending) > keep_back:
-                    c, g = pending.pop(0)
-                    j_quant(c, g)
-                    if CFG["late"] and c == 1 and not bp.get("done"):
-                        held.append(g)
-                    else:
-                        stage1(c, g)
-
-            def widen_all(g):
-                for t in range(4):
-                    widen(g, t, on_vector=t >= 4 - CFG["vw"][g])
-
-            widen_all(0)
-            for g in range(PASSES):
-                on_scalar = g in CFG["sj"][0]
-                on_scalar = on_scalar or g in CFG["pj"][0]
-                do_s = lambda c, g: pe_fetch(g) if g in CFG["pj"][0] else j_interleave(c, g, True)
-                if g == 0 and 0 in CFG["pj"][0]:
-                    pe_pack(0)
-                if on_scalar and CFG["jfirst"]:
-                    do_s(0, g)
-                if g + 1 < PASSES:
-                    widen_all(g + 1)
-                if on_scalar and not CFG["jfirst"]:
-                    do_s(0, g)
-                if g + 1 in CFG["pj"][0]:
-                    pe_pack(g + 1)
-                if g == CFG["vc"]:
-                    v_transpose()
-                    v_copy(0)
-                    v_copy(1)
+        for t in range(4):
+            widen(0, t, on_vector=t < 3)
+        for g in range(PASSES - 1):
+            for t in range(4):
+                widen(g + 1, t, on_vector=(g == 1 and t < 2))
+            if g in ROUTED:
+                g_fetch(g)
+            else:
                 g_interleave(g)
-                if not on_scalar:
-                    j_interleave(0, g, False)
-                flush(CFG["lag"])
+            if g + 1 in ROUTED:
+                g_route(g + 1)
+            j_interleave(g, WIDE)
+            if g >= HALVED:
+                j_interleave(g, MID)
+                j_quant(g, WIDE)
+                j_quant(g, MID)
                 g_quant(g)
-                pending.append((0, g))
-                if not on_scalar:
-                    flush(CFG["lag"])
-            for g in range(PASSES):
-                on_scalar = g in CFG["sj"][1]
-                on_scalar = on_scalar or g in CFG["pj"][1]
-                j_interleave(1, g, on_scalar)
-                flush(0 if g == 0 else CFG["lag"])
-                if g == CFG["vq"]:
-                    v_quant()
-                for m in range(4):
-                    if CFG["st"][m] == g:
-                        gain_noise(0, m, 0, 1)
-                        if m == 3:
-                            bp["done"] = True
-                            for k in held:
-                                stage1(1, k)
-                            held.clear()
-                pending.append((1, g))
-                if not on_scalar:
-                    flush(CFG["lag"])
-                if g == CFG["bi"][0]:
-                    b_interleave(0, 0, 1, CFG["bi"][1])
-                if g == CFG["bq"]:
-                    b_quant(0, 0, 1)
-                    stage2(0, 0, 1)
-                if g == CFG["ev"]:
-                    for b in range(4):
-                        finish(0, 0, b, 1, True)
-            flush(0)
-            for h in range(2):
-                for m in range(4):
-                    gain_noise(1, m, h, 2)
-                if h == 0 and CFG["bq"] == 8:
-                    b_quant(0, 0, 1)
-                    stage2(0, 0, 1)
-                if h == 0 and CFG["ev"] == 8:
-                    for b in range(4):
-                        finish(0, 0, b, 1, True)
-                if h == 1:
-                    b_quant(1, 0, 2)
-                    stage2(1, 0, 2)
-                b_interleave(1, h, 2, CFG["tail"][h])
-            b_quant(1, 1, 2)
-            stage2(1, 1, 2)
-            for h in range(2):
-                for b in range(4):
-                    finish(1, h, b, 2, (4 * h + b) not in CFG["evv"])
+            else:
+                g_quant(g)
+                j_quant(g, WIDE)
+            if g == PASSES - 2:
+                v_turn()
+            forward(g, WIDE)
+        last = PASSES - 1
+        j_interleave(last, WIDE, True)
+        v_fetch()
+        for g in range(HALVED, last - 2):
+            forward(g, MID)
+        g_interleave(last)
+        j_interleave(last, MID)
+        g_quant(last)
+        qf(last, WIDE)
+        for g in range(last - 2, last):
+            forward(g, MID)
+        qf(last, MID)
+        j_interleave(0, MID)
+        j_interleave(2, LAST, True)
+        j_interleave(1, MID, True)
+        for g in (3, 4, 5, 6, 7, 0, 1):
+            j_interleave(g, LAST, True)
+        v_quant()
+        record(WIDE, WIDE, [0])
+        qf(0, MID)
+        record(WIDE, WIDE, [1])
+        qf(2, LAST)
+        record(WIDE, WIDE, [2])
+        qf(1, MID)
+        record(WIDE, WIDE, [3])
+        qf(3, LAST)
+        b_interleave(WIDE)
+        qf(4, LAST)
+        b_quant(WIDE)
+        whiten(WIDE, 0, 4)
+        for i in range(4):
+            finish(WIDE, i)
+        for u, g in enumerate((5, 6, 7, 0)):
+            qf(g, LAST)
+            record(MID, MID, [u])
+        qf(1, LAST)
+        b_interleave(MID)
+        record(LAST_A, LAST, [0])
+        b_quant(MID)
+        whiten(MID, 6, 2)
+        finish(MID, 0)
+        finish(MID, 1)
+        record(LAST_A, LAST, [1, 2, 3])
+        record(LAST_B, LAST)
+        b_interleave(LAST_A)
+        b_interleave(LAST_B)
+        b_quant(LAST_A)
+        whiten(LAST_A, 0, 2)
+        b_quant(LAST_B)
+        whiten(LAST_B, 2, 2)
+        finish(LAST_A, 0)
+        finish(LAST_A, 1, on_scalar=False)
+        finish(LAST_B, 0)
+        finish(LAST_B, 1, on_scalar=False)

@@ -21,7 +21,7 @@ PASSES = SRC // 512
 WIDE, MID, LAST = (0, 512), (512, 256), (768, 256)
 LAST_A, LAST_B = (768, 128), (896, 128)
 ROUTED = (1, 2, 3, 4, 5, 6)
-HALVED = 2
+HALVED = 1
 
 
 def tile_meg_forward_whitened_d3_kernel(tc, g_bytes, g_scale, j_in, gain_in, e_in, v_in, out):
@@ -76,7 +76,7 @@ def tile_meg_forward_whitened_d3_kernel(tc, g_bytes, g_scale, j_in, gain_in, e_i
         gain = keep.tile([P, 4], BF16, name="gain")
 
         def load_v():
-            nc.sync.dma_start(out=v_raw[:], in_=v_in.rearrange("(b p) s -> p b s", p=P))
+            nc.sync.dma_start(out=v_raw[:], in_=v_in.rearrange("(p b) s -> p b s", b=4))
 
         def load_gain():
             nc.sync.dma_start(out=gain[:], in_=gain_in.rearrange("(p u) -> p u", u=4))
@@ -85,18 +85,16 @@ def tile_meg_forward_whitened_d3_kernel(tc, g_bytes, g_scale, j_in, gain_in, e_i
         load_g(0)
         load_g(1)
         load_j(0, 0, 512)
-        load_g(2)
-        load_scales(2, PASSES)
         for g in range(1, PASSES):
-            if 2 < g + 1 < PASSES:
+            if g + 1 < PASSES:
+                load_scales(g + 1, g + 2)
                 load_g(g + 1)
             load_j(g, 0, 512 if g < HALVED else TIM)
         load_v()
         load_gain()
-        load_noise(0, 512)
         for g in range(HALVED):
             load_j(g, 512, TIM)
-        load_noise(512, TIM)
+        load_noise(0, TIM)
 
         def quantize(name, pool, grouped, width):
             codes = pool.tile([P, width], U32, name="codes_" + name, align_bytes=64)
@@ -264,7 +262,7 @@ def tile_meg_forward_whitened_d3_kernel(tc, g_bytes, g_scale, j_in, gain_in, e_i
                     stop=True,
                 )
 
-        out_view = out.rearrange("(b p) n -> p b n", p=P)
+        out_view = out.rearrange("(p b) n -> p b n", b=4)
 
         def finish(cols, i, on_scalar=True):
             first, width = cols
@@ -284,7 +282,7 @@ def tile_meg_forward_whitened_d3_kernel(tc, g_bytes, g_scale, j_in, gain_in, e_i
             widen(0, t, on_vector=t < 3)
         for g in range(PASSES - 1):
             for t in range(4):
-                widen(g + 1, t, on_vector=(g == 1 and t < 2))
+                widen(g + 1, t)
             if g in ROUTED:
                 g_fetch(g)
             else:
@@ -306,54 +304,54 @@ def tile_meg_forward_whitened_d3_kernel(tc, g_bytes, g_scale, j_in, gain_in, e_i
         last = PASSES - 1
         j_interleave(last, WIDE, True)
         v_fetch()
-        for g in range(HALVED, last - 2):
+        for g in range(HALVED, last - 3):
             forward(g, MID)
         g_interleave(last)
         j_interleave(last, MID)
         g_quant(last)
         qf(last, WIDE)
-        for g in range(last - 2, last):
+        for g in range(last - 3, last):
             forward(g, MID)
         qf(last, MID)
         j_interleave(0, MID)
-        j_interleave(2, LAST, True)
-        j_interleave(1, MID, True)
-        for g in (3, 4, 5, 6, 7, 0, 1):
+        for g in (1, 2, 3, 4, 5, 6, 7, 0):
             j_interleave(g, LAST, True)
         v_quant()
         record(WIDE, WIDE, [0])
         qf(0, MID)
         record(WIDE, WIDE, [1])
-        qf(2, LAST)
+        qf(1, LAST)
         record(WIDE, WIDE, [2])
-        qf(1, MID)
+        qf(2, LAST)
         record(WIDE, WIDE, [3])
         qf(3, LAST)
-        b_interleave(WIDE)
         qf(4, LAST)
+        b_interleave(WIDE)
+        qf(5, LAST)
         b_quant(WIDE)
         whiten(WIDE, 0, 4)
         for i in range(4):
             finish(WIDE, i)
-        for u, g in enumerate((5, 6, 7, 0)):
-            qf(g, LAST)
-            record(MID, MID, [u])
-        qf(1, LAST)
+        record(MID, MID, [0, 1])
+        qf(6, LAST)
+        record(MID, MID, [2, 3])
+        qf(7, LAST)
+        qf(0, LAST)
         b_interleave(MID)
-        record(LAST_A, LAST, [0])
         b_quant(MID)
         whiten(MID, 6, 2)
         finish(MID, 0)
         finish(MID, 1)
-        record(LAST_A, LAST, [1, 2, 3])
-        record(LAST_B, LAST)
+        record(LAST_A, LAST)
+        record(LAST_B, LAST, [0])
         b_interleave(LAST_A)
-        b_interleave(LAST_B)
+        record(LAST_B, LAST, [1, 2, 3])
         b_quant(LAST_A)
         whiten(LAST_A, 0, 2)
+        b_interleave(LAST_B)
+        finish(LAST_A, 0)
+        finish(LAST_A, 1)
         b_quant(LAST_B)
         whiten(LAST_B, 2, 2)
-        finish(LAST_A, 0)
-        finish(LAST_A, 1, on_scalar=False)
         finish(LAST_B, 0)
         finish(LAST_B, 1, on_scalar=False)

@@ -280,6 +280,9 @@ def tile_meg_forward_whitened_d3_kernel(tc, g_bytes, g_scale, j_in, gain_in, e_i
 
         for t in range(4):
             widen(0, t, on_vector=t < 3)
+        idle = psum.tile([P, SEN], F32, name="bank0")
+        for t in range(3):
+            nc.tensor.matmul(out=idle[:], lhsT=ident_b[:], rhs=g_wide[0][:, t, :], start=True, stop=True)
         for g in range(PASSES - 1):
             for t in range(4):
                 widen(g + 1, t)

@@ -105,8 +105,9 @@ def tile_meg_forward_whitened_d3_kernel(tc, g_bytes, g_scale, j_in, gain_in, e_i
             return codes, scales
 
         def interleave(on_scalar, grouped, planes):
-            dst = grouped.rearrange("p (c i) t -> p c t i", i=4)
-            src = planes.rearrange("p t (c i) -> p c t i", i=4)
+            run = 4 if on_scalar else 2
+            dst = grouped.rearrange("p (c i) t -> p c t i", i=run)
+            src = planes.rearrange("p t (c i) -> p c t i", i=run)
             if on_scalar:
                 nc.scalar.copy(out=dst, in_=src)
             else:
@@ -127,8 +128,8 @@ def tile_meg_forward_whitened_d3_kernel(tc, g_bytes, g_scale, j_in, gain_in, e_i
         def g_interleave(g):
             g_grp[g] = work.tile([P, SEN, 4], BF16, name="g_grp", align_bytes=64)
             nc.vector.tensor_copy(
-                out=g_grp[g][:].rearrange("p (u m) t -> p m t u", u=4),
-                in_=g_wide[g][:].rearrange("p t (m u) -> p m t u", u=4),
+                out=g_grp[g][:].rearrange("p (u c i) t -> p u c t i", u=4, i=2),
+                in_=g_wide[g][:].rearrange("p t (c i u) -> p u c t i", u=4, i=2),
             )
 
         def g_route(g):
@@ -316,7 +317,7 @@ def tile_meg_forward_whitened_d3_kernel(tc, g_bytes, g_scale, j_in, gain_in, e_i
         for g in range(last - 3, last):
             forward(g, MID)
         qf(last, MID)
-        j_interleave(0, MID)
+        j_interleave(0, MID, True)
         for g in (1, 2, 3, 4, 5, 6, 7, 0):
             j_interleave(g, LAST, True)
         v_quant()

@@ -286,13 +286,15 @@ def tile_meg_forward_whitened_d3_kernel(tc, g_bytes, g_scale, j_in, gain_in, e_i
             nc.tensor.matmul(out=idle[:], lhsT=ident_b[:], rhs=g_wide[0][:, t, :], start=True, stop=True)
         for g in range(PASSES - 1):
             for t in range(4):
-                widen(g + 1, t)
+                widen(g + 1, t, on_vector=(g == 1 and t < 2))
             if g in ROUTED:
                 g_fetch(g)
             else:
                 g_interleave(g)
             if g + 1 in ROUTED:
                 g_route(g + 1)
+            if g == 1:
+                j_interleave(1, LAST, True)
             j_interleave(g, WIDE)
             if g >= HALVED:
                 j_interleave(g, MID)
@@ -318,7 +320,7 @@ def tile_meg_forward_whitened_d3_kernel(tc, g_bytes, g_scale, j_in, gain_in, e_i
             forward(g, MID)
         qf(last, MID)
         j_interleave(0, MID, True)
-        for g in (1, 2, 3, 4, 5, 6, 7, 0):
+        for g in (2, 3, 4, 5, 6, 7, 0):
             j_interleave(g, LAST, True)
         v_quant()
         record(WIDE, WIDE, [0])

@@ -89,8 +89,9 @@ def tile_meg_forward_whitened_d3_kernel(tc, g_bytes, g_scale, j_in, gain_in, e_i
             if g + 1 < PASSES:
                 load_scales(g + 1, g + 2)
                 load_g(g + 1)
+            if g == PASSES - 1:
+                load_v()
             load_j(g, 0, 512 if g < HALVED else TIM)
-        load_v()
         load_gain()
         for g in range(HALVED):
             load_j(g, 512, TIM)
@@ -105,9 +106,8 @@ def tile_meg_forward_whitened_d3_kernel(tc, g_bytes, g_scale, j_in, gain_in, e_i
             return codes, scales
 
         def interleave(on_scalar, grouped, planes):
-            run = 4 if on_scalar else 2
-            dst = grouped.rearrange("p (c i) t -> p c t i", i=run)
-            src = planes.rearrange("p t (c i) -> p c t i", i=run)
+            dst = grouped.rearrange("p (c i) t -> p c t i", i=4)
+            src = planes.rearrange("p t (c i) -> p c t i", i=4)
             if on_scalar:
                 nc.scalar.copy(out=dst, in_=src)
             else:
@@ -162,10 +162,26 @@ def tile_meg_forward_whitened_d3_kernel(tc, g_bytes, g_scale, j_in, gain_in, e_i
 
         def j_interleave(g, cols, on_scalar=False):
             first, width = cols
+            if (g, cols) == (PASSES - 1, MID):
+                j_grp[g, first] = keep.tile([P, width, 4], BF16, name="j_handover", align_bytes=64)
+                interleave(on_scalar, j_grp[g, first][:], j_raw[g, first])
+                return
             j_grp[g, first] = work.tile(
-                [P, width, 4], BF16, name="j_grp%d" % width, bufs=3 if cols == WIDE else 11, align_bytes=64
+                [P, width, 4], BF16, name="j_grp%d" % width, bufs=3 if cols == WIDE else 10, align_bytes=64
             )
             interleave(on_scalar, j_grp[g, first][:], j_raw[g, first])
+
+        def j_interleave_gpsimd(g, cols, name):
+            first, width = cols
+            j_grp[g, first] = keep.tile([P, width, 4], BF16, name=name, align_bytes=64)
+            nc.gpsimd.tensor_scalar(
+                out=j_grp[g, first][:],
+                in0=j_raw[g, first].rearrange("p t n -> p n t"),
+                scalar1=1.0,
+                scalar2=0.0,
+                op0=MULT,
+                op1=ADD,
+            )
 
         def j_quant(g, cols):
             first, width = cols
@@ -306,43 +322,44 @@ def tile_meg_forward_whitened_d3_kernel(tc, g_bytes, g_scale, j_in, gain_in, e_i
                 j_quant(g, WIDE)
             if g == PASSES - 2:
                 v_turn()
+                forward(1, MID)
+                forward(2, MID)
             forward(g, WIDE)
         last = PASSES - 1
         j_interleave(last, WIDE, True)
         v_fetch()
-        for g in range(HALVED, last - 3):
+        for g in (3, 4):
             forward(g, MID)
         g_interleave(last)
-        j_interleave(last, MID)
+        j_quant(last, WIDE)
         g_quant(last)
-        qf(last, WIDE)
-        for g in range(last - 3, last):
+        forward(last, WIDE)
+        for g in (5, 6):
             forward(g, MID)
-        qf(last, MID)
-        j_interleave(0, MID, True)
-        for g in (2, 3, 4, 5, 6, 7, 0):
+        for g in (last, 0):
+            j_interleave(g, MID, True)
+        for g in range(2, PASSES):
             j_interleave(g, LAST, True)
-        v_quant()
-        record(WIDE, WIDE, [0])
-        qf(0, MID)
-        record(WIDE, WIDE, [1])
         qf(1, LAST)
-        record(WIDE, WIDE, [2])
+        v_quant()
+        qf(last, MID)
+        j_interleave_gpsimd(0, LAST, "j_handover")
+        record(WIDE, WIDE)
+        qf(0, MID)
+        qf(0, LAST)
         qf(2, LAST)
-        record(WIDE, WIDE, [3])
         qf(3, LAST)
-        qf(4, LAST)
         b_interleave(WIDE)
-        qf(5, LAST)
+        qf(4, LAST)
         b_quant(WIDE)
         whiten(WIDE, 0, 4)
         for i in range(4):
             finish(WIDE, i)
+        qf(5, LAST)
         record(MID, MID, [0, 1])
         qf(6, LAST)
         record(MID, MID, [2, 3])
         qf(7, LAST)
-        qf(0, LAST)
         b_interleave(MID)
         b_quant(MID)
         whiten(MID, 6, 2)

@@ -315,8 +315,8 @@ def tile_meg_forward_whitened_d3_kernel(tc, g_bytes, g_scale, j_in, gain_in, e_i
             if g >= HALVED:
                 j_interleave(g, MID)
                 j_quant(g, WIDE)
-                j_quant(g, MID)
                 g_quant(g)
+                j_quant(g, MID)
             else:
                 g_quant(g)
                 j_quant(g, WIDE)

@@ -91,9 +91,9 @@ def tile_meg_forward_whitened_d3_kernel(tc, g_bytes, g_scale, j_in, gain_in, e_i
                 load_g(g + 1)
             if g == PASSES - 1:
                 load_v()
-            load_j(g, 0, 512 if g < HALVED else TIM)
+            load_j(g, 0, 512 if g in (0, PASSES - 1) else TIM)
         load_gain()
-        for g in range(HALVED):
+        for g in (PASSES - 1, 0):
             load_j(g, 512, TIM)
         load_noise(0, TIM)
 
@@ -366,9 +366,9 @@ def tile_meg_forward_whitened_d3_kernel(tc, g_bytes, g_scale, j_in, gain_in, e_i
         finish(MID, 0)
         finish(MID, 1)
         record(LAST_A, LAST)
-        record(LAST_B, LAST, [0])
+        record(LAST_B, LAST, [0, 1])
         b_interleave(LAST_A)
-        record(LAST_B, LAST, [1, 2, 3])
+        record(LAST_B, LAST, [2, 3])
         b_quant(LAST_A)
         whiten(LAST_A, 0, 2)
         b_interleave(LAST_B)

@@ -18,10 +18,15 @@ COPY = mybir.ActivationFunctionType.Copy
 
 P = 128
 PASSES = SRC // 512
+FINAL = PASSES - 1
+
 WIDE, MID, LAST = (0, 512), (512, 256), (768, 256)
 LAST_A, LAST_B = (768, 128), (896, 128)
-ROUTED = (1, 2, 3, 4, 5, 6)
-HALVED = 1
+FIELD_BANK = {WIDE: 0, MID: 6, LAST: 4}
+
+ROUTED = range(1, FINAL)
+
+PIECE_BUFS = 10
 
 
 def tile_meg_forward_whitened_d3_kernel(tc, g_bytes, g_scale, j_in, gain_in, e_in, v_in, out):
@@ -44,8 +49,7 @@ def tile_meg_forward_whitened_d3_kernel(tc, g_bytes, g_scale, j_in, gain_in, e_i
         gs_view = g_scale.rearrange("(g p t) o -> p g (t o)", p=P, t=4)
         gb_view = g_bytes.rearrange("(g p t) s -> g p t s", p=P, t=4)
         j_view = j_in.rearrange("(g p t) n -> g p t n", p=P, t=4)
-        e_view = e_in.rearrange("(p u) n -> p u n", u=4)
-        g_raw, j_raw, g_sc, noise = {}, {}, {}, {}
+        g_raw, g_sc, j_raw = {}, {}, {}
 
         def load_scales(g0, g1):
             tile = keep.tile([P, g1 - g0, 4], F32, name="g_sc%d" % g0)
@@ -65,37 +69,24 @@ def tile_meg_forward_whitened_d3_kernel(tc, g_bytes, g_scale, j_in, gain_in, e_i
                 if n0 <= first < n1:
                     j_raw[g, first] = tile[:, :, first - n0:first - n0 + width]
 
-        def load_noise(n0, n1):
-            tile = keep.tile([P, 4, n1 - n0], BF16, name="noise%d" % n0, align_bytes=64)
-            nc.sync.dma_start(out=tile[:], in_=e_view[:, :, n0:n1])
-            for first, width in (WIDE, MID, LAST, LAST_A, LAST_B):
-                if n0 <= first < n1:
-                    noise[first, width] = tile[:, :, first - n0:first - n0 + width]
-
         v_raw = keep.tile([P, 4, SEN], BF16, name="v_raw", align_bytes=64)
         gain = keep.tile([P, 4], BF16, name="gain")
-
-        def load_v():
-            nc.sync.dma_start(out=v_raw[:], in_=v_in.rearrange("(p b) s -> p b s", b=4))
-
-        def load_gain():
-            nc.sync.dma_start(out=gain[:], in_=gain_in.rearrange("(p u) -> p u", u=4))
 
         load_scales(0, 2)
         load_g(0)
         load_g(1)
-        load_j(0, 0, 512)
-        for g in range(1, PASSES):
-            if g + 1 < PASSES:
-                load_scales(g + 1, g + 2)
-                load_g(g + 1)
-            if g == PASSES - 1:
-                load_v()
-            load_j(g, 0, 512 if g in (0, PASSES - 1) else TIM)
-        load_gain()
-        for g in (PASSES - 1, 0):
-            load_j(g, 512, TIM)
-        load_noise(0, TIM)
+        load_j(0, 0, WIDE[1])
+        for g in range(1, FINAL):
+            load_scales(g + 1, g + 2)
+            load_g(g + 1)
+            load_j(g, 0, TIM)
+        nc.sync.dma_start(out=v_raw[:], in_=v_in.rearrange("(p b) s -> p b s", b=4))
+        load_j(FINAL, 0, WIDE[1])
+        nc.sync.dma_start(out=gain[:], in_=gain_in.rearrange("(p u) -> p u", u=4))
+        for g in (FINAL, 0):
+            load_j(g, WIDE[1], TIM)
+        noise = keep.tile([P, 4, TIM], BF16, name="noise0", align_bytes=64)
+        nc.sync.dma_start(out=noise[:], in_=e_in.rearrange("(p u) n -> p u n", u=4))
 
         def quantize(name, pool, grouped, width):
             codes = pool.tile([P, width], U32, name="codes_" + name, align_bytes=64)
@@ -115,8 +106,8 @@ def tile_meg_forward_whitened_d3_kernel(tc, g_bytes, g_scale, j_in, gain_in, e_i
 
         g_wide, g_grp, g_mx, g_psum = {}, {}, {}, {}
 
-        def widen(g, t, on_vector=False):
-            if g not in g_wide:
+        def widen(g, t, on_vector):
+            if t == 0:
                 g_wide[g] = work.tile([P, 4, SEN], BF16, name="g_wide", align_bytes=64)
             scale = g_sc[g][:, t:t + 1]
             src = g_raw[g][:, t, :].bitcast(FP8)
@@ -133,7 +124,7 @@ def tile_meg_forward_whitened_d3_kernel(tc, g_bytes, g_scale, j_in, gain_in, e_i
             )
 
         def g_route(g):
-            bank = 4 + 2 * (ROUTED.index(g) % 2)
+            bank = 4 + 2 * ((g - 1) % 2)
             for q in range(2):
                 g_psum[g, q] = psum.tile([P, 4, 64, 4], BF16, name="bank%d" % (bank + q))
             for t0 in (0, 2):
@@ -160,20 +151,18 @@ def tile_meg_forward_whitened_d3_kernel(tc, g_bytes, g_scale, j_in, gain_in, e_i
 
         j_grp, j_mx, field = {}, {}, {}
 
-        def j_interleave(g, cols, on_scalar=False):
+        def j_interleave(g, cols, on_scalar):
             first, width = cols
-            if (g, cols) == (PASSES - 1, MID):
+            if (g, cols) == (FINAL, MID):
                 j_grp[g, first] = keep.tile([P, width, 4], BF16, name="j_handover", align_bytes=64)
-                interleave(on_scalar, j_grp[g, first][:], j_raw[g, first])
-                return
-            j_grp[g, first] = work.tile(
-                [P, width, 4], BF16, name="j_grp%d" % width, bufs=3 if cols == WIDE else 10, align_bytes=64
-            )
+            else:
+                bufs = 3 if cols == WIDE else PIECE_BUFS
+                j_grp[g, first] = work.tile([P, width, 4], BF16, name="j_grp%d" % width, bufs=bufs, align_bytes=64)
             interleave(on_scalar, j_grp[g, first][:], j_raw[g, first])
 
-        def j_interleave_gpsimd(g, cols, name):
+        def j_interleave_gpsimd(g, cols):
             first, width = cols
-            j_grp[g, first] = keep.tile([P, width, 4], BF16, name=name, align_bytes=64)
+            j_grp[g, first] = keep.tile([P, width, 4], BF16, name="j_handover", align_bytes=64)
             nc.gpsimd.tensor_scalar(
                 out=j_grp[g, first][:],
                 in0=j_raw[g, first].rearrange("p t n -> p n t"),
@@ -198,12 +187,12 @@ def tile_meg_forward_whitened_d3_kernel(tc, g_bytes, g_scale, j_in, gain_in, e_i
                 tiles.append(tile)
             return tiles, per_bank
 
-        done = {WIDE: [], MID: [], LAST: []}
+        passes_done = {WIDE: [], MID: [], LAST: []}
 
         def forward(g, cols):
-            if not done[cols]:
-                field[cols] = bank_tiles({WIDE: 0, MID: 6, LAST: 4}[cols], cols[1] // P, cols[1])
-            done[cols].append(g)
+            if not passes_done[cols]:
+                field[cols] = bank_tiles(FIELD_BANK[cols], cols[1] // P, cols[1])
+            passes_done[cols].append(g)
             tiles, per_bank = field[cols]
             codes, scales = j_mx[g, cols[0]]
             for u in range(4):
@@ -213,9 +202,13 @@ def tile_meg_forward_whitened_d3_kernel(tc, g_bytes, g_scale, j_in, gain_in, e_i
                     lhsT_scale=g_mx[g][1][:, u * P:(u + 1) * P],
                     rhs=codes[:].bitcast(FP8X4),
                     rhs_scale=scales[:],
-                    start=(len(done[cols]) == 1 and u % per_bank == 0),
-                    stop=(len(done[cols]) == PASSES and u % per_bank == per_bank - 1),
+                    start=(len(passes_done[cols]) == 1 and u % per_bank == 0),
+                    stop=(len(passes_done[cols]) == PASSES and u % per_bank == per_bank - 1),
                 )
+
+        def quant_forward(g, cols):
+            j_quant(g, cols)
+            forward(g, cols)
 
         v_grp = keep.tile([P, SEN, 4], BF16, name="v_grp", align_bytes=64)
         v_mx, v_psum = [], []
@@ -223,49 +216,48 @@ def tile_meg_forward_whitened_d3_kernel(tc, g_bytes, g_scale, j_in, gain_in, e_i
         def v_turn():
             words = v_raw[:].rearrange("p b s -> p (b s)").bitcast(F32)
             for h in range(2):
-                turned = psum.tile([P, 2, 2, P], F32, name="bank%d" % (4 + h))
+                turned = psum.tile([P, 2, 2, P], F32, name="bank%d" % (FIELD_BANK[LAST] + h))
                 v_psum.append(turned)
                 for b in range(2):
-                    for u in range(2):
+                    for w in range(2):
                         w0 = (2 * h + b) * 256
-                        nc.tensor.transpose(turned[:, b, u, :], words[:, w0 + u:w0 + 256:2], ident[:])
+                        nc.tensor.transpose(turned[:, b, w, :], words[:, w0 + w:w0 + 256:2], ident[:])
 
         def v_fetch():
             for h in range(2):
-                dst = v_grp[:].rearrange("p w t -> p (w t)").bitcast(F32)[:, 512 * h:512 * (h + 1)]
+                dst = v_grp[:].rearrange("p n t -> p (n t)").bitcast(F32)[:, 512 * h:512 * (h + 1)]
                 nc.scalar.copy(
-                    out=dst.rearrange("p (b r u) -> p b r u", b=2, u=2),
-                    in_=v_psum[h][:].rearrange("p b u r -> p b r u"),
+                    out=dst.rearrange("p (b r w) -> p b r w", b=2, w=2),
+                    in_=v_psum[h][:].rearrange("p b w r -> p b r w"),
                 )
 
         def v_quant():
             v_mx.extend(quantize("v", keep, v_grp, SEN))
 
-        b_planes, b_grp, b_mx, white = {}, {}, {}, {}
+        b_planes, b_grp, white = {}, {}, {}
 
-        def record(cols, within, planes=range(4)):
+        def record(cols, stretch, planes):
             first, width = cols
             if cols not in b_planes:
                 b_planes[cols] = work.tile([P, 4, width], BF16, name="g_wide", align_bytes=64)
-            tiles, per_bank = field[within]
+            tiles, per_bank = field[stretch]
+            n0 = first - stretch[0]
             for u in planes:
                 nc.vector.scalar_tensor_tensor(
                     out=b_planes[cols][:, u, :],
-                    in0=tiles[u // per_bank][:, u % per_bank, first - within[0]:first - within[0] + width],
+                    in0=tiles[u // per_bank][:, u % per_bank, n0:n0 + width],
                     scalar=gain[:, u:u + 1],
-                    in1=noise[cols][:, u, :],
+                    in1=noise[:, u, first:first + width],
                     op0=MULT,
                     op1=ADD,
                 )
 
-        def b_interleave(cols, on_scalar=False):
+        def b_interleave(cols):
             b_grp[cols] = keep.tile([P, cols[1], 4], BF16, name="b_grp%d" % cols[0], align_bytes=64)
-            interleave(on_scalar, b_grp[cols][:], b_planes[cols][:])
-
-        def b_quant(cols):
-            b_mx[cols] = quantize("b%d" % cols[0], keep, b_grp[cols], cols[1])
+            interleave(False, b_grp[cols][:], b_planes[cols][:])
 
         def whiten(cols, first_bank, banks):
+            codes, scales = quantize("b%d" % cols[0], keep, b_grp[cols], cols[1])
             white[cols] = bank_tiles(first_bank, banks, cols[1])
             tiles, per_bank = white[cols]
             for b in range(4):
@@ -273,15 +265,15 @@ def tile_meg_forward_whitened_d3_kernel(tc, g_bytes, g_scale, j_in, gain_in, e_i
                     out=tiles[b // per_bank][:, b % per_bank, :],
                     lhsT=v_mx[0][:, b * P:(b + 1) * P].bitcast(FP8X4),
                     lhsT_scale=v_mx[1][:, b * P:(b + 1) * P],
-                    rhs=b_mx[cols][0][:].bitcast(FP8X4),
-                    rhs_scale=b_mx[cols][1][:],
+                    rhs=codes[:].bitcast(FP8X4),
+                    rhs_scale=scales[:],
                     start=True,
                     stop=True,
                 )
 
         out_view = out.rearrange("(p b) n -> p b n", b=4)
 
-        def finish(cols, i, on_scalar=True):
+        def store(cols, i, on_scalar):
             first, width = cols
             tiles, per_bank = white[cols]
             y = keep.tile([P, per_bank, width], F32, name="y%d_%d" % (first, i))
@@ -291,16 +283,10 @@ def tile_meg_forward_whitened_d3_kernel(tc, g_bytes, g_scale, j_in, gain_in, e_i
                 nc.vector.tensor_copy(out=y[:], in_=tiles[i][:])
             nc.sync.dma_start(out=out_view[:, i * per_bank:(i + 1) * per_bank, first:first + width], in_=y[:])
 
-        def qf(g, cols):
-            j_quant(g, cols)
-            forward(g, cols)
-
         for t in range(4):
             widen(0, t, on_vector=t < 3)
-        idle = psum.tile([P, SEN], F32, name="bank0")
-        for t in range(3):
-            nc.tensor.matmul(out=idle[:], lhsT=ident_b[:], rhs=g_wide[0][:, t, :], start=True, stop=True)
-        for g in range(PASSES - 1):
+
+        for g in range(FINAL):
             for t in range(4):
                 widen(g + 1, t, on_vector=(g == 1 and t < 2))
             if g in ROUTED:
@@ -310,71 +296,67 @@ def tile_meg_forward_whitened_d3_kernel(tc, g_bytes, g_scale, j_in, gain_in, e_i
             if g + 1 in ROUTED:
                 g_route(g + 1)
             if g == 1:
-                j_interleave(1, LAST, True)
-            j_interleave(g, WIDE)
-            if g >= HALVED:
-                j_interleave(g, MID)
+                j_interleave(g, LAST, on_scalar=True)
+            j_interleave(g, WIDE, on_scalar=False)
+            if g == 0:
+                g_quant(g)
+                j_quant(g, WIDE)
+            else:
+                j_interleave(g, MID, on_scalar=False)
                 j_quant(g, WIDE)
                 g_quant(g)
                 j_quant(g, MID)
-            else:
-                g_quant(g)
-                j_quant(g, WIDE)
-            if g == PASSES - 2:
+            if g == FINAL - 1:
                 v_turn()
-                forward(1, MID)
-                forward(2, MID)
+                for k in (1, 2):
+                    forward(k, MID)
             forward(g, WIDE)
-        last = PASSES - 1
-        j_interleave(last, WIDE, True)
+
+        j_interleave(FINAL, WIDE, on_scalar=True)
         v_fetch()
-        for g in (3, 4):
-            forward(g, MID)
-        g_interleave(last)
-        j_quant(last, WIDE)
-        g_quant(last)
-        forward(last, WIDE)
-        for g in (5, 6):
-            forward(g, MID)
-        for g in (last, 0):
-            j_interleave(g, MID, True)
+        for k in (3, 4):
+            forward(k, MID)
+        g_interleave(FINAL)
+        j_quant(FINAL, WIDE)
+        g_quant(FINAL)
+        forward(FINAL, WIDE)
+        for k in (5, 6):
+            forward(k, MID)
+        for g in (FINAL, 0):
+            j_interleave(g, MID, on_scalar=True)
         for g in range(2, PASSES):
-            j_interleave(g, LAST, True)
-        qf(1, LAST)
+            j_interleave(g, LAST, on_scalar=True)
+        quant_forward(1, LAST)
         v_quant()
-        qf(last, MID)
-        j_interleave_gpsimd(0, LAST, "j_handover")
-        record(WIDE, WIDE)
-        qf(0, MID)
-        qf(0, LAST)
-        qf(2, LAST)
-        qf(3, LAST)
+        quant_forward(FINAL, MID)
+        j_interleave_gpsimd(0, LAST)
+
+        record(WIDE, WIDE, range(4))
+        quant_forward(0, MID)
+        for g in (0, 2, 3):
+            quant_forward(g, LAST)
         b_interleave(WIDE)
-        qf(4, LAST)
-        b_quant(WIDE)
-        whiten(WIDE, 0, 4)
+        quant_forward(4, LAST)
+        whiten(WIDE, FIELD_BANK[WIDE], 4)
         for i in range(4):
-            finish(WIDE, i)
-        qf(5, LAST)
-        record(MID, MID, [0, 1])
-        qf(6, LAST)
-        record(MID, MID, [2, 3])
-        qf(7, LAST)
+            store(WIDE, i, on_scalar=True)
+        for half in range(2):
+            quant_forward(5 + half, LAST)
+            record(MID, MID, (2 * half, 2 * half + 1))
+        quant_forward(FINAL, LAST)
         b_interleave(MID)
-        b_quant(MID)
-        whiten(MID, 6, 2)
-        finish(MID, 0)
-        finish(MID, 1)
-        record(LAST_A, LAST)
-        record(LAST_B, LAST, [0, 1])
+        whiten(MID, FIELD_BANK[MID], 2)
+        for i in range(2):
+            store(MID, i, on_scalar=True)
+
+        record(LAST_A, LAST, range(4))
+        record(LAST_B, LAST, (0, 1))
         b_interleave(LAST_A)
-        record(LAST_B, LAST, [2, 3])
-        b_quant(LAST_A)
+        record(LAST_B, LAST, (2, 3))
         whiten(LAST_A, 0, 2)
         b_interleave(LAST_B)
-        finish(LAST_A, 0)
-        finish(LAST_A, 1)
-        b_quant(LAST_B)
+        for i in range(2):
+            store(LAST_A, i, on_scalar=True)
         whiten(LAST_B, 2, 2)
-        finish(LAST_B, 0)
-        finish(LAST_B, 1, on_scalar=False)
+        for i in range(2):
+            store(LAST_B, i, on_scalar=i == 0)

@@ -130,9 +130,9 @@ def tile_meg_forward_whitened_d3_kernel(tc, g_bytes, g_scale, j_in, gain_in, e_i
             for t0 in (0, 2):
                 for q in range(2):
                     nc.tensor.matmul(
-                        out=g_psum[g, q][:, :, :, t0:t0 + 2].rearrange("p u m t -> p t m u"),
+                        out=g_psum[g, q][:, :, :, t0:t0 + 2].rearrange("p u m t -> p m u t"),
                         lhsT=ident_b[:],
-                        rhs=g_wide[g][:, t0:t0 + 2, 256 * q:256 * (q + 1)].rearrange("p t (m u) -> p t m u", u=4),
+                        rhs=g_wide[g][:, t0:t0 + 2, 256 * q:256 * (q + 1)].rearrange("p t (m u) -> p m u t", u=4),
                         start=True,
                         stop=True,
                     )

@@ -22,11 +22,13 @@ FINAL = PASSES - 1
 
 WIDE, MID, LAST = (0, 512), (512, 256), (768, 256)
 LAST_A, LAST_B = (768, 128), (896, 128)
-FIELD_BANK = {WIDE: 0, MID: 6, LAST: 4}
+FIELD_BANK = {WIDE: 0, MID: 4, LAST: 6}
 
-ROUTED = range(1, FINAL)
+ROUTED = (0, 2, 3, 4, 5, 6)
 
-PIECE_BUFS = 10
+PIECE_BUFS = 6
+WIDENED_BUFS = 4
+HANDOVER = (6, MID)
 
 
 def tile_meg_forward_whitened_d3_kernel(tc, g_bytes, g_scale, j_in, gain_in, e_in, v_in, out):
@@ -49,7 +51,8 @@ def tile_meg_forward_whitened_d3_kernel(tc, g_bytes, g_scale, j_in, gain_in, e_i
         gs_view = g_scale.rearrange("(g p t) o -> p g (t o)", p=P, t=4)
         gb_view = g_bytes.rearrange("(g p t) s -> g p t s", p=P, t=4)
         j_view = j_in.rearrange("(g p t) n -> g p t n", p=P, t=4)
-        g_raw, g_sc, j_raw = {}, {}, {}
+        e_view = e_in.rearrange("(p u) n -> p u n", u=4)
+        g_raw, g_sc, j_raw, noise = {}, {}, {}, {}
 
         def load_scales(g0, g1):
             tile = keep.tile([P, g1 - g0, 4], F32, name="g_sc%d" % g0)
@@ -69,24 +72,38 @@ def tile_meg_forward_whitened_d3_kernel(tc, g_bytes, g_scale, j_in, gain_in, e_i
                 if n0 <= first < n1:
                     j_raw[g, first] = tile[:, :, first - n0:first - n0 + width]
 
+        def load_e(n0, n1):
+            tile = keep.tile([P, 4, n1 - n0], BF16, name="noise%d" % n0, align_bytes=64)
+            nc.sync.dma_start(out=tile[:], in_=e_view[:, :, n0:n1])
+            for first, width in (WIDE, MID, LAST_A, LAST_B):
+                if n0 <= first < n1:
+                    noise[first] = tile[:, :, first - n0:first - n0 + width]
+
         v_raw = keep.tile([P, 4, SEN], BF16, name="v_raw", align_bytes=64)
         gain = keep.tile([P, 4], BF16, name="gain")
 
+        half = WIDE[1]
         load_scales(0, 2)
         load_g(0)
         load_g(1)
-        load_j(0, 0, WIDE[1])
-        for g in range(1, FINAL):
-            load_scales(g + 1, g + 2)
-            load_g(g + 1)
+        load_scales(2, 4)
+        load_g(2)
+        load_j(0, 0, half)
+        load_g(3)
+        for g in range(1, 5):
+            load_scales(g + 3, g + 4)
+            load_g(g + 3)
             load_j(g, 0, TIM)
         nc.sync.dma_start(out=v_raw[:], in_=v_in.rearrange("(p b) s -> p b s", b=4))
-        load_j(FINAL, 0, WIDE[1])
+        load_j(5, 0, TIM)
+        for g in (6, FINAL):
+            load_j(g, 0, half)
+        for g in (0, 6):
+            load_j(g, half, TIM)
         nc.sync.dma_start(out=gain[:], in_=gain_in.rearrange("(p u) -> p u", u=4))
-        for g in (FINAL, 0):
-            load_j(g, WIDE[1], TIM)
-        noise = keep.tile([P, 4, TIM], BF16, name="noise0", align_bytes=64)
-        nc.sync.dma_start(out=noise[:], in_=e_in.rearrange("(p u) n -> p u n", u=4))
+        load_e(0, half)
+        load_j(FINAL, half, TIM)
+        load_e(half, TIM)
 
         def quantize(name, pool, grouped, width):
             codes = pool.tile([P, width], U32, name="codes_" + name, align_bytes=64)
@@ -107,8 +124,8 @@ def tile_meg_forward_whitened_d3_kernel(tc, g_bytes, g_scale, j_in, gain_in, e_i
         g_wide, g_grp, g_mx, g_psum = {}, {}, {}, {}
 
         def widen(g, t, on_vector):
-            if t == 0:
-                g_wide[g] = work.tile([P, 4, SEN], BF16, name="g_wide", align_bytes=64)
+            if g not in g_wide:
+                g_wide[g] = work.tile([P, 4, SEN], BF16, name="g_wide", bufs=WIDENED_BUFS, align_bytes=64)
             scale = g_sc[g][:, t:t + 1]
             src = g_raw[g][:, t, :].bitcast(FP8)
             if on_vector:
@@ -123,24 +140,25 @@ def tile_meg_forward_whitened_d3_kernel(tc, g_bytes, g_scale, j_in, gain_in, e_i
                 in_=g_wide[g][:].rearrange("p t (c i u) -> p u c t i", u=4, i=2),
             )
 
-        def g_route(g):
-            bank = 4 + 2 * ((g - 1) % 2)
+        def g_route(g, planes_first=False):
+            bank = 4 + 2 * (ROUTED.index(g) % 2)
             for q in range(2):
                 g_psum[g, q] = psum.tile([P, 4, 64, 4], BF16, name="bank%d" % (bank + q))
-            for t0 in (0, 2):
-                for q in range(2):
-                    nc.tensor.matmul(
-                        out=g_psum[g, q][:, :, :, t0:t0 + 2].rearrange("p u m t -> p m u t"),
-                        lhsT=ident_b[:],
-                        rhs=g_wide[g][:, t0:t0 + 2, 256 * q:256 * (q + 1)].rearrange("p t (m u) -> p m u t", u=4),
-                        start=True,
-                        stop=True,
-                    )
+            for step in range(4):
+                q, t0 = (step % 2, 2 * (step // 2)) if planes_first else (step // 2, 2 * (step % 2))
+                nc.tensor.matmul(
+                    out=g_psum[g, q][:, :, :, t0:t0 + 2].rearrange("p u m t -> p t m u"),
+                    lhsT=ident_b[:],
+                    rhs=g_wide[g][:, t0:t0 + 2, 256 * q:256 * (q + 1)].rearrange("p t (m u) -> p t m u", u=4),
+                    start=True,
+                    stop=True,
+                )
 
-        def g_fetch(g):
-            g_grp[g] = work.tile([P, SEN, 4], BF16, name="g_grp", align_bytes=64)
+        def g_fetch(g, banks=(0, 1)):
+            if g not in g_grp:
+                g_grp[g] = work.tile([P, SEN, 4], BF16, name="g_grp", align_bytes=64)
             dst = g_grp[g][:].rearrange("p (u m) t -> p u (m t)", u=4).bitcast(F32)
-            for q in range(2):
+            for q in banks:
                 nc.scalar.copy(
                     out=dst[:, :, 128 * q:128 * (q + 1)],
                     in_=g_psum[g, q][:].rearrange("p u m t -> p u (m t)").bitcast(F32),
@@ -153,7 +171,7 @@ def tile_meg_forward_whitened_d3_kernel(tc, g_bytes, g_scale, j_in, gain_in, e_i
 
         def j_interleave(g, cols, on_scalar):
             first, width = cols
-            if (g, cols) == (FINAL, MID):
+            if (g, cols) == HANDOVER:
                 j_grp[g, first] = keep.tile([P, width, 4], BF16, name="j_handover", align_bytes=64)
             else:
                 bufs = 3 if cols == WIDE else PIECE_BUFS
@@ -239,7 +257,7 @@ def tile_meg_forward_whitened_d3_kernel(tc, g_bytes, g_scale, j_in, gain_in, e_i
         def record(cols, stretch, planes):
             first, width = cols
             if cols not in b_planes:
-                b_planes[cols] = work.tile([P, 4, width], BF16, name="g_wide", align_bytes=64)
+                b_planes[cols] = work.tile([P, 4, width], BF16, name="g_wide", bufs=WIDENED_BUFS, align_bytes=64)
             tiles, per_bank = field[stretch]
             n0 = first - stretch[0]
             for u in planes:
@@ -247,7 +265,7 @@ def tile_meg_forward_whitened_d3_kernel(tc, g_bytes, g_scale, j_in, gain_in, e_i
                     out=b_planes[cols][:, u, :],
                     in0=tiles[u // per_bank][:, u % per_bank, n0:n0 + width],
                     scalar=gain[:, u:u + 1],
-                    in1=noise[:, u, first:first + width],
+                    in1=noise[first][:, u, :],
                     op0=MULT,
                     op1=ADD,
                 )
@@ -283,66 +301,96 @@ def tile_meg_forward_whitened_d3_kernel(tc, g_bytes, g_scale, j_in, gain_in, e_i
                 nc.vector.tensor_copy(out=y[:], in_=tiles[i][:])
             nc.sync.dma_start(out=out_view[:, i * per_bank:(i + 1) * per_bank, first:first + width], in_=y[:])
 
-        for t in range(4):
-            widen(0, t, on_vector=t < 3)
-
-        for g in range(FINAL):
+        def widen_pass(g, on_scalar=()):
             for t in range(4):
-                widen(g + 1, t, on_vector=(g == 1 and t < 2))
-            if g in ROUTED:
-                g_fetch(g)
+                widen(g, t, on_vector=t not in on_scalar)
+
+        widen_pass(0, on_scalar=(2,))
+        g_route(0)
+        widen_pass(1, on_scalar=(3,))
+        widen(2, 0, on_vector=True)
+        g_interleave(1)
+        widen(2, 1, on_vector=False)
+        g_fetch(0, (0,))
+        widen(2, 2, on_vector=False)
+        widen(2, 3, on_vector=False)
+        g_fetch(0, (1,))
+        g_route(2, planes_first=True)
+        j_interleave(0, WIDE, on_scalar=False)
+        widen_pass(3, on_scalar=(2, 3))
+        g_route(3, planes_first=True)
+        g_quant(0)
+        quant_forward(0, WIDE)
+        g_quant(1)
+        for q in range(2):
+            widen(4, q, on_vector=True)
+            g_fetch(2, (q,))
+            widen(4, 2 + q, on_vector=False)
+        g_route(4)
+        j_interleave(1, WIDE, on_scalar=False)
+        g_quant(2)
+        g_fetch(3)
+        j_interleave(1, MID, on_scalar=True)
+        widen(5, 0, on_vector=True)
+        quant_forward(1, WIDE)
+        for t in range(1, 4):
+            widen(5, t, on_vector=True)
+        g_quant(3)
+
+        for g in range(2, 5):
+            j_interleave(g, WIDE, on_scalar=True)
+            g_fetch(g + 2)
+            if g + 3 in ROUTED:
+                g_route(g + 3)
+            if g + 4 < PASSES:
+                widen_pass(g + 4)
             else:
-                g_interleave(g)
-            if g + 1 in ROUTED:
-                g_route(g + 1)
-            if g == 1:
-                j_interleave(g, LAST, on_scalar=True)
-            j_interleave(g, WIDE, on_scalar=False)
-            if g == 0:
-                g_quant(g)
-                j_quant(g, WIDE)
-            else:
-                j_interleave(g, MID, on_scalar=False)
-                j_quant(g, WIDE)
-                g_quant(g)
-                j_quant(g, MID)
-            if g == FINAL - 1:
-                v_turn()
+                g_interleave(FINAL)
+            j_quant(g - 1, MID)
+            if g + 3 not in ROUTED:
                 for k in (1, 2):
                     forward(k, MID)
-            forward(g, WIDE)
+                v_turn()
+            quant_forward(g, WIDE)
+            j_interleave(g, MID, on_scalar=False)
+            g_quant(g + 2)
 
-        j_interleave(FINAL, WIDE, on_scalar=True)
+        j_interleave(5, WIDE, on_scalar=True)
         v_fetch()
-        for k in (3, 4):
-            forward(k, MID)
-        g_interleave(FINAL)
-        j_quant(FINAL, WIDE)
+        j_interleave(6, WIDE, on_scalar=False)
+        j_quant(4, MID)
+        forward(3, MID)
+        quant_forward(5, WIDE)
+        j_interleave(FINAL, WIDE, on_scalar=True)
+        quant_forward(6, WIDE)
+        forward(4, MID)
+        j_interleave(1, LAST, on_scalar=False)
         g_quant(FINAL)
-        forward(FINAL, WIDE)
-        for k in (5, 6):
-            forward(k, MID)
-        for g in (FINAL, 0):
-            j_interleave(g, MID, on_scalar=True)
-        for g in range(2, PASSES):
-            j_interleave(g, LAST, on_scalar=True)
-        quant_forward(1, LAST)
-        v_quant()
-        quant_forward(FINAL, MID)
+        j_interleave(5, MID, on_scalar=False)
+        quant_forward(FINAL, WIDE)
+        for g, cols in ((2, LAST), HANDOVER, (0, MID), (3, LAST), (FINAL, MID)):
+            j_interleave(g, cols, on_scalar=True)
+            if cols == LAST and g == 2:
+                quant_forward(1, LAST)
+                v_quant()
+                quant_forward(5, MID)
+                quant_forward(2, LAST)
+        quant_forward(*HANDOVER)
         j_interleave_gpsimd(0, LAST)
 
         record(WIDE, WIDE, range(4))
-        quant_forward(0, MID)
-        for g in (0, 2, 3):
-            quant_forward(g, LAST)
+        for g, cols in ((0, MID), (0, LAST), (3, LAST), (FINAL, MID)):
+            quant_forward(g, cols)
+        for g in range(4, PASSES):
+            j_interleave(g, LAST, on_scalar=True)
         b_interleave(WIDE)
         quant_forward(4, LAST)
         whiten(WIDE, FIELD_BANK[WIDE], 4)
         for i in range(4):
             store(WIDE, i, on_scalar=True)
-        for half in range(2):
-            quant_forward(5 + half, LAST)
-            record(MID, MID, (2 * half, 2 * half + 1))
+        for part in range(2):
+            quant_forward(5 + part, LAST)
+            record(MID, MID, (2 * part, 2 * part + 1))
         quant_forward(FINAL, LAST)
         b_interleave(MID)
         whiten(MID, FIELD_BANK[MID], 2)

@@ -28,6 +28,7 @@ ROUTED = (0, 2, 3, 4, 5, 6)
 
 PIECE_BUFS = 6
 WIDENED_BUFS = 4
+PLANE_GAP, PAIR_GAP = 18, 20
 HANDOVER = (6, MID)
 
 
@@ -66,11 +67,18 @@ def tile_meg_forward_whitened_d3_kernel(tc, g_bytes, g_scale, j_in, gain_in, e_i
                 nc.sync.dma_start(out=g_raw[g][:, t0:t1, :], in_=gb_view[g][:, t0:t1, :])
 
         def load_j(g, n0, n1):
-            tile = keep.tile([P, 4, n1 - n0], BF16, name="j_raw%d_%d" % (g, n0), align_bytes=64)
-            nc.sync.dma_start(out=tile[:], in_=j_view[g][:, :, n0:n1])
+            name = "j_raw%d_%d" % (g, n0)
+            if n1 - n0 == TIM:
+                tile = keep.tile([P, 2, 2 * TIM + PAIR_GAP], BF16, name=name, align_bytes=64)
+                nc.sync.dma_start(out=tile[:, :, :2 * TIM], in_=j_view[g].rearrange("p (h e) n -> p h (e n)", h=2))
+                planes = tile[:, :, :2 * TIM].rearrange("p h (e n) -> p h e n", e=2)
+            else:
+                tile = keep.tile([P, 4, n1 - n0 + PLANE_GAP], BF16, name=name, align_bytes=64)
+                nc.sync.dma_start(out=tile[:, :, :n1 - n0], in_=j_view[g][:, :, n0:n1])
+                planes = tile[:, :, :n1 - n0].rearrange("p (h e) n -> p h e n", e=2)
             for first, width in (WIDE, MID, LAST):
                 if n0 <= first < n1:
-                    j_raw[g, first] = tile[:, :, first - n0:first - n0 + width]
+                    j_raw[g, first] = planes[:, :, :, first - n0:first - n0 + width]
 
         def load_e(n0, n1):
             tile = keep.tile([P, 4, n1 - n0], BF16, name="noise%d" % n0, align_bytes=64)
@@ -114,8 +122,8 @@ def tile_meg_forward_whitened_d3_kernel(tc, g_bytes, g_scale, j_in, gain_in, e_i
             return codes, scales
 
         def interleave(on_scalar, grouped, planes):
-            dst = grouped.rearrange("p (c i) t -> p c t i", i=4)
-            src = planes.rearrange("p t (c i) -> p c t i", i=4)
+            dst = grouped.rearrange("p (c i) (h e) -> p c h e i", i=2, e=2)
+            src = planes.rearrange("p h e (c i) -> p c h e i", i=2)
             if on_scalar:
                 nc.scalar.copy(out=dst, in_=src)
             else:
@@ -136,8 +144,8 @@ def tile_meg_forward_whitened_d3_kernel(tc, g_bytes, g_scale, j_in, gain_in, e_i
         def g_interleave(g):
             g_grp[g] = work.tile([P, SEN, 4], BF16, name="g_grp", align_bytes=64)
             nc.vector.tensor_copy(
-                out=g_grp[g][:].rearrange("p (u c i) t -> p u c t i", u=4, i=2),
-                in_=g_wide[g][:].rearrange("p t (c i u) -> p u c t i", u=4, i=2),
+                out=g_grp[g][:].rearrange("p (u c i) t -> p c u t i", u=4, i=2),
+                in_=g_wide[g][:].rearrange("p t (c i u) -> p c u t i", u=4, i=2),
             )
 
         def g_route(g, planes_first=False):
@@ -183,7 +191,7 @@ def tile_meg_forward_whitened_d3_kernel(tc, g_bytes, g_scale, j_in, gain_in, e_i
             j_grp[g, first] = keep.tile([P, width, 4], BF16, name="j_handover", align_bytes=64)
             nc.gpsimd.tensor_scalar(
                 out=j_grp[g, first][:],
-                in0=j_raw[g, first].rearrange("p t n -> p n t"),
+                in0=j_raw[g, first].rearrange("p h e n -> p n (h e)"),
                 scalar1=1.0,
                 scalar2=0.0,
                 op0=MULT,
@@ -257,12 +265,14 @@ def tile_meg_forward_whitened_d3_kernel(tc, g_bytes, g_scale, j_in, gain_in, e_i
         def record(cols, stretch, planes):
             first, width = cols
             if cols not in b_planes:
-                b_planes[cols] = work.tile([P, 4, width], BF16, name="g_wide", bufs=WIDENED_BUFS, align_bytes=64)
+                b_planes[cols] = work.tile(
+                    [P, 4, width + PLANE_GAP], BF16, name="g_wide", bufs=WIDENED_BUFS, align_bytes=64
+                )
             tiles, per_bank = field[stretch]
             n0 = first - stretch[0]
             for u in planes:
                 nc.vector.scalar_tensor_tensor(
-                    out=b_planes[cols][:, u, :],
+                    out=b_planes[cols][:, u, :width],
                     in0=tiles[u // per_bank][:, u % per_bank, n0:n0 + width],
                     scalar=gain[:, u:u + 1],
                     in1=noise[first][:, u, :],
@@ -272,7 +282,8 @@ def tile_meg_forward_whitened_d3_kernel(tc, g_bytes, g_scale, j_in, gain_in, e_i
 
         def b_interleave(cols):
             b_grp[cols] = keep.tile([P, cols[1], 4], BF16, name="b_grp%d" % cols[0], align_bytes=64)
-            interleave(False, b_grp[cols][:], b_planes[cols][:])
+            planes = b_planes[cols][:, :, :cols[1]].rearrange("p (h e) n -> p h e n", e=2)
+            interleave(False, b_grp[cols][:], planes)
 
         def whiten(cols, first_bank, banks):
             codes, scales = quantize("b%d" % cols[0], keep, b_grp[cols], cols[1])

@@ -102,8 +102,8 @@ def tile_meg_forward_whitened_d3_kernel(tc, g_bytes, g_scale, j_in, gain_in, e_i
             load_scales(g + 3, g + 4)
             load_g(g + 3)
             load_j(g, 0, TIM)
-        nc.sync.dma_start(out=v_raw[:], in_=v_in.rearrange("(p b) s -> p b s", b=4))
         load_j(5, 0, TIM)
+        nc.sync.dma_start(out=v_raw[:], in_=v_in.rearrange("(p b) s -> p b s", b=4))
         for g in (6, FINAL):
             load_j(g, 0, half)
         for g in (0, 6):
@@ -337,33 +337,26 @@ def tile_meg_forward_whitened_d3_kernel(tc, g_bytes, g_scale, j_in, gain_in, e_i
             widen(4, q, on_vector=True)
             g_fetch(2, (q,))
             widen(4, 2 + q, on_vector=False)
-        g_route(4)
-        j_interleave(1, WIDE, on_scalar=False)
-        g_quant(2)
-        g_fetch(3)
-        j_interleave(1, MID, on_scalar=True)
-        widen(5, 0, on_vector=True)
-        quant_forward(1, WIDE)
-        for t in range(1, 4):
-            widen(5, t, on_vector=True)
-        g_quant(3)
 
-        for g in range(2, 5):
-            j_interleave(g, WIDE, on_scalar=True)
-            g_fetch(g + 2)
+        for g in range(1, 5):
             if g + 3 in ROUTED:
                 g_route(g + 3)
+            g_fetch(g + 2)
             if g + 4 < PASSES:
-                widen_pass(g + 4)
+                widen_pass(g + 4, on_scalar=range(4))
+            j_interleave(g, WIDE, on_scalar=False)
+            if g == 1:
+                g_quant(2)
             else:
-                g_interleave(FINAL)
-            j_quant(g - 1, MID)
+                j_quant(g - 1, MID)
+            j_interleave(g, MID, on_scalar=False)
             if g + 3 not in ROUTED:
                 for k in (1, 2):
                     forward(k, MID)
                 v_turn()
             quant_forward(g, WIDE)
-            j_interleave(g, MID, on_scalar=False)
+            if g + 3 == FINAL:
+                g_interleave(FINAL)
             g_quant(g + 2)
 
         j_interleave(5, WIDE, on_scalar=True)

@@ -22,14 +22,16 @@ FINAL = PASSES - 1
 
 WIDE, MID, LAST = (0, 512), (512, 256), (768, 256)
 LAST_A, LAST_B = (768, 128), (896, 128)
+FRONT, REST = (0, 768), (512, 512)
 FIELD_BANK = {WIDE: 0, MID: 4, LAST: 6}
 
 ROUTED = (0, 2, 3, 4, 5, 6)
 
-PIECE_BUFS = 6
+PIECE_BUFS = 5
 WIDENED_BUFS = 4
+JOINT_BUFS = 4
 PLANE_GAP, PAIR_GAP = 18, 20
-HANDOVER = (6, MID)
+HANDOVER = (6, REST)
 
 
 def tile_meg_forward_whitened_d3_kernel(tc, g_bytes, g_scale, j_in, gain_in, e_in, v_in, out):
@@ -76,9 +78,9 @@ def tile_meg_forward_whitened_d3_kernel(tc, g_bytes, g_scale, j_in, gain_in, e_i
                 tile = keep.tile([P, 4, n1 - n0 + PLANE_GAP], BF16, name=name, align_bytes=64)
                 nc.sync.dma_start(out=tile[:, :, :n1 - n0], in_=j_view[g][:, :, n0:n1])
                 planes = tile[:, :, :n1 - n0].rearrange("p (h e) n -> p h e n", e=2)
-            for first, width in (WIDE, MID, LAST):
-                if n0 <= first < n1:
-                    j_raw[g, first] = planes[:, :, :, first - n0:first - n0 + width]
+            for first, width in (WIDE, MID, LAST, FRONT, REST):
+                if n0 <= first and first + width <= n1:
+                    j_raw[g, (first, width)] = planes[:, :, :, first - n0:first - n0 + width]
 
         def load_e(n0, n1):
             tile = keep.tile([P, 4, n1 - n0], BF16, name="noise%d" % n0, align_bytes=64)
@@ -103,10 +105,10 @@ def tile_meg_forward_whitened_d3_kernel(tc, g_bytes, g_scale, j_in, gain_in, e_i
             load_g(g + 3)
             load_j(g, 0, TIM)
         load_j(5, 0, TIM)
-        nc.sync.dma_start(out=v_raw[:], in_=v_in.rearrange("(p b) s -> p b s", b=4))
         for g in (6, FINAL):
             load_j(g, 0, half)
-        for g in (0, 6):
+        nc.sync.dma_start(out=v_raw[:], in_=v_in.rearrange("(p b) s -> p b s", b=4))
+        for g in (6, 0):
             load_j(g, half, TIM)
         nc.sync.dma_start(out=gain[:], in_=gain_in.rearrange("(p u) -> p u", u=4))
         load_e(0, half)
@@ -117,7 +119,7 @@ def tile_meg_forward_whitened_d3_kernel(tc, g_bytes, g_scale, j_in, gain_in, e_i
             codes = pool.tile([P, width], U32, name="codes_" + name, align_bytes=64)
             scales = pool.tile([P, width], U8, name="scales_" + name, align_bytes=64)
             nc.vector.quantize_mx(
-                out=codes[:].bitcast(FP8X4), scales=scales[:], in_=grouped[:].rearrange("p n t -> p (n t)")
+                out=codes[:].bitcast(FP8X4), scales=scales[:], in_=grouped.rearrange("p n t -> p (n t)")
             )
             return codes, scales
 
@@ -129,7 +131,17 @@ def tile_meg_forward_whitened_d3_kernel(tc, g_bytes, g_scale, j_in, gain_in, e_i
             else:
                 nc.vector.tensor_copy(out=dst, in_=src)
 
-        g_wide, g_grp, g_mx, g_psum = {}, {}, {}, {}
+        joint = {}
+
+        def joint_part(g, n0, n1):
+            if g not in joint:
+                joint[g] = work.tile([P, 4 * (SEN + FRONT[1])], BF16, name="joint", bufs=JOINT_BUFS, align_bytes=64)
+            return joint[g][:, 4 * n0:4 * n1].rearrange("p (n t) -> p n t", t=4)
+
+        def g_grouped(g):
+            return joint_part({0: 0, 1: "alone"}.get(g, g - 1), 0, SEN)
+
+        g_wide, g_mx, g_psum = {}, {}, {}
 
         def widen(g, t, on_vector):
             if g not in g_wide:
@@ -142,9 +154,8 @@ def tile_meg_forward_whitened_d3_kernel(tc, g_bytes, g_scale, j_in, gain_in, e_i
                 nc.scalar.activation(out=g_wide[g][:, t, :], in_=src, func=COPY, scale=scale)
 
         def g_interleave(g):
-            g_grp[g] = work.tile([P, SEN, 4], BF16, name="g_grp", align_bytes=64)
             nc.vector.tensor_copy(
-                out=g_grp[g][:].rearrange("p (u c i) t -> p c u t i", u=4, i=2),
+                out=g_grouped(g).rearrange("p (u c i) t -> p c u t i", u=4, i=2),
                 in_=g_wide[g][:].rearrange("p t (c i u) -> p c u t i", u=4, i=2),
             )
 
@@ -163,35 +174,35 @@ def tile_meg_forward_whitened_d3_kernel(tc, g_bytes, g_scale, j_in, gain_in, e_i
                 )
 
         def g_fetch(g, banks=(0, 1)):
-            if g not in g_grp:
-                g_grp[g] = work.tile([P, SEN, 4], BF16, name="g_grp", align_bytes=64)
-            dst = g_grp[g][:].rearrange("p (u m) t -> p u (m t)", u=4).bitcast(F32)
+            dst = g_grouped(g).rearrange("p (u m) t -> p u (m t)", u=4).bitcast(F32)
             for q in banks:
                 nc.scalar.copy(
                     out=dst[:, :, 128 * q:128 * (q + 1)],
                     in_=g_psum[g, q][:].rearrange("p u m t -> p u (m t)").bitcast(F32),
                 )
 
-        def g_quant(g):
-            g_mx[g] = quantize("g%d" % g, keep, g_grp[g], SEN)
-
         j_grp, j_mx, field = {}, {}, {}
 
         def j_interleave(g, cols, on_scalar):
             first, width = cols
-            if (g, cols) == HANDOVER:
-                j_grp[g, first] = keep.tile([P, width, 4], BF16, name="j_handover", align_bytes=64)
+            if first == 0:
+                grouped = joint_part(g, SEN, SEN + width)
+                if cols == FRONT:
+                    j_grp[g, MID] = joint_part(g, SEN + MID[0], SEN + width)
             else:
-                bufs = 3 if cols == WIDE else PIECE_BUFS
-                j_grp[g, first] = work.tile([P, width, 4], BF16, name="j_grp%d" % width, bufs=bufs, align_bytes=64)
-            interleave(on_scalar, j_grp[g, first][:], j_raw[g, first])
+                if (g, cols) == HANDOVER:
+                    tile = keep.tile([P, width, 4], BF16, name="j_handover", align_bytes=64)
+                else:
+                    tile = work.tile([P, width, 4], BF16, name="j_grp", bufs=PIECE_BUFS, align_bytes=64)
+                grouped = j_grp[g, cols] = tile[:]
+            interleave(on_scalar, grouped, j_raw[g, cols])
 
         def j_interleave_gpsimd(g, cols):
-            first, width = cols
-            j_grp[g, first] = keep.tile([P, width, 4], BF16, name="j_handover", align_bytes=64)
+            tile = keep.tile([P, cols[1], 4], BF16, name="j_handover", align_bytes=64)
+            j_grp[g, cols] = tile[:]
             nc.gpsimd.tensor_scalar(
-                out=j_grp[g, first][:],
-                in0=j_raw[g, first].rearrange("p h e n -> p n (h e)"),
+                out=tile[:],
+                in0=j_raw[g, cols].rearrange("p h e n -> p n (h e)"),
                 scalar1=1.0,
                 scalar2=0.0,
                 op0=MULT,
@@ -200,10 +211,15 @@ def tile_meg_forward_whitened_d3_kernel(tc, g_bytes, g_scale, j_in, gain_in, e_i
 
         def j_quant(g, cols):
             first, width = cols
-            if cols == WIDE:
-                j_mx[g, first] = quantize("j_wide", work, j_grp[g, first], width)
-            else:
-                j_mx[g, first] = quantize("j%d_%d" % (first, g), keep, j_grp[g, first], width)
+            codes, scales = quantize("j%d_%d" % (first, g), keep, j_grp[g, cols], width)
+            for n0, w in (MID, LAST):
+                if first <= n0 < first + width:
+                    j_mx[g, (n0, w)] = codes[:, n0 - first:n0 - first + w], scales[:, n0 - first:n0 - first + w]
+
+        def joint_quant(g):
+            codes, scales = quantize("joint%d" % g, keep, joint_part(g, 0, SEN + WIDE[1]), SEN + WIDE[1])
+            j_mx[g, WIDE] = codes[:, SEN:], scales[:, SEN:]
+            g_mx[g + 1 if g else 0] = codes[:, :SEN], scales[:, :SEN]
 
         def bank_tiles(first_bank, banks, width):
             per_bank = 4 // banks
@@ -220,14 +236,14 @@ def tile_meg_forward_whitened_d3_kernel(tc, g_bytes, g_scale, j_in, gain_in, e_i
                 field[cols] = bank_tiles(FIELD_BANK[cols], cols[1] // P, cols[1])
             passes_done[cols].append(g)
             tiles, per_bank = field[cols]
-            codes, scales = j_mx[g, cols[0]]
+            codes, scales = j_mx[g, cols]
             for u in range(4):
                 nc.tensor.matmul_mx(
                     out=tiles[u // per_bank][:, u % per_bank, :],
                     lhsT=g_mx[g][0][:, u * P:(u + 1) * P].bitcast(FP8X4),
                     lhsT_scale=g_mx[g][1][:, u * P:(u + 1) * P],
-                    rhs=codes[:].bitcast(FP8X4),
-                    rhs_scale=scales[:],
+                    rhs=codes.bitcast(FP8X4),
+                    rhs_scale=scales,
                     start=(len(passes_done[cols]) == 1 and u % per_bank == 0),
                     stop=(len(passes_done[cols]) == PASSES and u % per_bank == per_bank - 1),
                 )
@@ -236,8 +252,7 @@ def tile_meg_forward_whitened_d3_kernel(tc, g_bytes, g_scale, j_in, gain_in, e_i
             j_quant(g, cols)
             forward(g, cols)
 
-        v_grp = keep.tile([P, SEN, 4], BF16, name="v_grp", align_bytes=64)
-        v_mx, v_psum = [], []
+        v_psum = []
 
         def v_turn():
             words = v_raw[:].rearrange("p b s -> p (b s)").bitcast(F32)
@@ -251,14 +266,11 @@ def tile_meg_forward_whitened_d3_kernel(tc, g_bytes, g_scale, j_in, gain_in, e_i
 
         def v_fetch():
             for h in range(2):
-                dst = v_grp[:].rearrange("p n t -> p (n t)").bitcast(F32)[:, 512 * h:512 * (h + 1)]
+                dst = g_grouped(PASSES).rearrange("p n t -> p (n t)").bitcast(F32)[:, 512 * h:512 * (h + 1)]
                 nc.scalar.copy(
                     out=dst.rearrange("p (b r w) -> p b r w", b=2, w=2),
                     in_=v_psum[h][:].rearrange("p b w r -> p b r w"),
                 )
-
-        def v_quant():
-            v_mx.extend(quantize("v", keep, v_grp, SEN))
 
         b_planes, b_grp, white = {}, {}, {}
 
@@ -281,12 +293,13 @@ def tile_meg_forward_whitened_d3_kernel(tc, g_bytes, g_scale, j_in, gain_in, e_i
                 )
 
         def b_interleave(cols):
-            b_grp[cols] = keep.tile([P, cols[1], 4], BF16, name="b_grp%d" % cols[0], align_bytes=64)
+            b_grp[cols] = work.tile([P, cols[1], 4], BF16, name="joint", bufs=JOINT_BUFS, align_bytes=64)
             planes = b_planes[cols][:, :, :cols[1]].rearrange("p (h e) n -> p h e n", e=2)
             interleave(False, b_grp[cols][:], planes)
 
         def whiten(cols, first_bank, banks):
-            codes, scales = quantize("b%d" % cols[0], keep, b_grp[cols], cols[1])
+            codes, scales = quantize("b%d" % cols[0], keep, b_grp[cols][:], cols[1])
+            v_mx = g_mx[PASSES]
             white[cols] = bank_tiles(first_bank, banks, cols[1])
             tiles, per_bank = white[cols]
             for b in range(4):
@@ -302,10 +315,12 @@ def tile_meg_forward_whitened_d3_kernel(tc, g_bytes, g_scale, j_in, gain_in, e_i
 
         out_view = out.rearrange("(p b) n -> p b n", b=4)
 
+        spent = ["j_raw%d_0" % g for g in (0, 6, 7, 1, 2, 3, 4, 5)] + ["j_raw%d_%d" % (g, half) for g in (0, 6)]
+
         def store(cols, i, on_scalar):
             first, width = cols
             tiles, per_bank = white[cols]
-            y = keep.tile([P, per_bank, width], F32, name="y%d_%d" % (first, i))
+            y = keep.tile([P, per_bank, width], F32, name=spent.pop(0), align_bytes=64)
             if on_scalar:
                 nc.scalar.copy(out=y[:], in_=tiles[i][:])
             else:
@@ -321,22 +336,19 @@ def tile_meg_forward_whitened_d3_kernel(tc, g_bytes, g_scale, j_in, gain_in, e_i
         widen_pass(1, on_scalar=(3,))
         widen(2, 0, on_vector=True)
         g_interleave(1)
-        widen(2, 1, on_vector=False)
-        g_fetch(0, (0,))
-        widen(2, 2, on_vector=False)
-        widen(2, 3, on_vector=False)
-        g_fetch(0, (1,))
+        for t in range(1, 4):
+            widen(2, t, on_vector=False)
+        g_fetch(0)
         g_route(2, planes_first=True)
         j_interleave(0, WIDE, on_scalar=False)
         widen_pass(3, on_scalar=(2, 3))
         g_route(3, planes_first=True)
-        g_quant(0)
-        quant_forward(0, WIDE)
-        g_quant(1)
         for q in range(2):
             widen(4, q, on_vector=True)
             g_fetch(2, (q,))
             widen(4, 2 + q, on_vector=False)
+        joint_quant(0)
+        forward(0, WIDE)
 
         for g in range(1, 5):
             if g + 3 in ROUTED:
@@ -344,56 +356,57 @@ def tile_meg_forward_whitened_d3_kernel(tc, g_bytes, g_scale, j_in, gain_in, e_i
             g_fetch(g + 2)
             if g + 4 < PASSES:
                 widen_pass(g + 4, on_scalar=range(4))
-            j_interleave(g, WIDE, on_scalar=False)
-            if g == 1:
-                g_quant(2)
-            else:
+            j_interleave(g, FRONT, on_scalar=False)
+            if g > 1:
                 j_quant(g - 1, MID)
-            j_interleave(g, MID, on_scalar=False)
+            else:
+                g_mx[1] = quantize("g1", keep, g_grouped(1), SEN)
             if g + 3 not in ROUTED:
                 for k in (1, 2):
                     forward(k, MID)
-                v_turn()
-            quant_forward(g, WIDE)
-            if g + 3 == FINAL:
-                g_interleave(FINAL)
-            g_quant(g + 2)
+            joint_quant(g)
+            forward(g, WIDE)
 
-        j_interleave(5, WIDE, on_scalar=True)
-        v_fetch()
-        j_interleave(6, WIDE, on_scalar=False)
+        g_interleave(FINAL)
         j_quant(4, MID)
+        j_interleave(5, WIDE, on_scalar=True)
+        j_interleave(6, WIDE, on_scalar=False)
         forward(3, MID)
-        quant_forward(5, WIDE)
+        joint_quant(5)
+        v_turn()
+        forward(5, WIDE)
         j_interleave(FINAL, WIDE, on_scalar=True)
-        quant_forward(6, WIDE)
+        v_fetch()
+        joint_quant(6)
         forward(4, MID)
+        forward(6, WIDE)
         j_interleave(1, LAST, on_scalar=False)
-        g_quant(FINAL)
         j_interleave(5, MID, on_scalar=False)
-        quant_forward(FINAL, WIDE)
-        for g, cols in ((2, LAST), HANDOVER, (0, MID), (3, LAST), (FINAL, MID)):
-            j_interleave(g, cols, on_scalar=True)
-            if cols == LAST and g == 2:
-                quant_forward(1, LAST)
-                v_quant()
-                quant_forward(5, MID)
-                quant_forward(2, LAST)
-        quant_forward(*HANDOVER)
+        j_quant(1, LAST)
+        joint_quant(FINAL)
+        forward(1, LAST)
+        forward(FINAL, WIDE)
+        j_interleave(*HANDOVER, on_scalar=True)
+        quant_forward(5, MID)
+        j_quant(*HANDOVER)
+        for cols in (MID, LAST):
+            forward(6, cols)
         j_interleave_gpsimd(0, LAST)
+        for g, cols in ((2, LAST), (0, MID), (FINAL, MID), (3, LAST)):
+            j_interleave(g, cols, on_scalar=True)
 
         record(WIDE, WIDE, range(4))
-        for g, cols in ((0, MID), (0, LAST), (3, LAST), (FINAL, MID)):
+        for g, cols in ((2, LAST), (0, LAST), (0, MID), (FINAL, MID)):
             quant_forward(g, cols)
-        for g in range(4, PASSES):
+        for g in (4, 5, FINAL):
             j_interleave(g, LAST, on_scalar=True)
         b_interleave(WIDE)
-        quant_forward(4, LAST)
+        quant_forward(3, LAST)
         whiten(WIDE, FIELD_BANK[WIDE], 4)
         for i in range(4):
             store(WIDE, i, on_scalar=True)
         for part in range(2):
-            quant_forward(5 + part, LAST)
+            quant_forward(4 + part, LAST)
             record(MID, MID, (2 * part, 2 * part + 1))
         quant_forward(FINAL, LAST)
         b_interleave(MID)

@@ -19,10 +19,14 @@ COPY = mybir.ActivationFunctionType.Copy
 P = 128
 PASSES = SRC // 512
 FINAL = PASSES - 1
+STEPS = 4
+SHARED = (5, 6, FINAL)
+WITH_REST = (2, 3)
+HALVED = (0, FINAL - 1, 1, FINAL)
 
 WIDE, MID, LAST = (0, 512), (512, 256), (768, 256)
 LAST_A, LAST_B = (768, 128), (896, 128)
-FRONT, REST = (0, 768), (512, 512)
+REST = (512, 512)
 FIELD_BANK = {WIDE: 0, MID: 4, LAST: 6}
 
 ROUTED = (0, 2, 3, 4, 5, 6)
@@ -31,7 +35,7 @@ PIECE_BUFS = 5
 WIDENED_BUFS = 4
 JOINT_BUFS = 4
 PLANE_GAP, PAIR_GAP = 18, 20
-HANDOVER = (6, REST)
+HANDOVER = (STEPS, REST)
 
 
 def tile_meg_forward_whitened_d3_kernel(tc, g_bytes, g_scale, j_in, gain_in, e_in, v_in, out):
@@ -78,7 +82,7 @@ def tile_meg_forward_whitened_d3_kernel(tc, g_bytes, g_scale, j_in, gain_in, e_i
                 tile = keep.tile([P, 4, n1 - n0 + PLANE_GAP], BF16, name=name, align_bytes=64)
                 nc.sync.dma_start(out=tile[:, :, :n1 - n0], in_=j_view[g][:, :, n0:n1])
                 planes = tile[:, :, :n1 - n0].rearrange("p (h e) n -> p h e n", e=2)
-            for first, width in (WIDE, MID, LAST, FRONT, REST):
+            for first, width in (WIDE, MID, LAST, REST):
                 if n0 <= first and first + width <= n1:
                     j_raw[g, (first, width)] = planes[:, :, :, first - n0:first - n0 + width]
 
@@ -100,19 +104,19 @@ def tile_meg_forward_whitened_d3_kernel(tc, g_bytes, g_scale, j_in, gain_in, e_i
         load_g(2)
         load_j(0, 0, half)
         load_g(3)
-        for g in range(1, 5):
+        for g in range(1, STEPS + 1):
             load_scales(g + 3, g + 4)
             load_g(g + 3)
-            load_j(g, 0, TIM)
-        load_j(5, 0, TIM)
-        for g in (6, FINAL):
-            load_j(g, 0, half)
+            load_j(g, 0, half if g in HALVED else TIM)
+        for g in SHARED:
+            load_j(g, 0, half if g in HALVED else TIM)
         nc.sync.dma_start(out=v_raw[:], in_=v_in.rearrange("(p b) s -> p b s", b=4))
-        for g in (6, 0):
+        for g in HALVED[:2]:
             load_j(g, half, TIM)
         nc.sync.dma_start(out=gain[:], in_=gain_in.rearrange("(p u) -> p u", u=4))
         load_e(0, half)
-        load_j(FINAL, half, TIM)
+        for g in HALVED[2:]:
+            load_j(g, half, TIM)
         load_e(half, TIM)
 
         def quantize(name, pool, grouped, width):
@@ -135,7 +139,7 @@ def tile_meg_forward_whitened_d3_kernel(tc, g_bytes, g_scale, j_in, gain_in, e_i
 
         def joint_part(g, n0, n1):
             if g not in joint:
-                joint[g] = work.tile([P, 4 * (SEN + FRONT[1])], BF16, name="joint", bufs=JOINT_BUFS, align_bytes=64)
+                joint[g] = work.tile([P, 4 * (SEN + WIDE[1])], BF16, name="joint", bufs=JOINT_BUFS, align_bytes=64)
             return joint[g][:, 4 * n0:4 * n1].rearrange("p (n t) -> p n t", t=4)
 
         def g_grouped(g):
@@ -173,9 +177,9 @@ def tile_meg_forward_whitened_d3_kernel(tc, g_bytes, g_scale, j_in, gain_in, e_i
                     stop=True,
                 )
 
-        def g_fetch(g, banks=(0, 1)):
+        def g_fetch(g, halves=(0, 1)):
             dst = g_grouped(g).rearrange("p (u m) t -> p u (m t)", u=4).bitcast(F32)
-            for q in banks:
+            for q in halves:
                 nc.scalar.copy(
                     out=dst[:, :, 128 * q:128 * (q + 1)],
                     in_=g_psum[g, q][:].rearrange("p u m t -> p u (m t)").bitcast(F32),
@@ -187,11 +191,11 @@ def tile_meg_forward_whitened_d3_kernel(tc, g_bytes, g_scale, j_in, gain_in, e_i
             first, width = cols
             if first == 0:
                 grouped = joint_part(g, SEN, SEN + width)
-                if cols == FRONT:
-                    j_grp[g, MID] = joint_part(g, SEN + MID[0], SEN + width)
             else:
                 if (g, cols) == HANDOVER:
                     tile = keep.tile([P, width, 4], BF16, name="j_handover", align_bytes=64)
+                elif cols == REST:
+                    tile = work.tile([P, width, 4], BF16, name="j_rest", bufs=1, align_bytes=64)
                 else:
                     tile = work.tile([P, width, 4], BF16, name="j_grp", bufs=PIECE_BUFS, align_bytes=64)
                 grouped = j_grp[g, cols] = tile[:]
@@ -315,7 +319,7 @@ def tile_meg_forward_whitened_d3_kernel(tc, g_bytes, g_scale, j_in, gain_in, e_i
 
         out_view = out.rearrange("(p b) n -> p b n", b=4)
 
-        spent = ["j_raw%d_0" % g for g in (0, 6, 7, 1, 2, 3, 4, 5)] + ["j_raw%d_%d" % (g, half) for g in (0, 6)]
+        spent = ["j_raw%d_0" % g for g in range(PASSES)] + ["j_raw%d_%d" % (g, half) for g in HALVED[:2]]
 
         def store(cols, i, on_scalar):
             first, width = cols
@@ -350,63 +354,64 @@ def tile_meg_forward_whitened_d3_kernel(tc, g_bytes, g_scale, j_in, gain_in, e_i
         joint_quant(0)
         forward(0, WIDE)
 
-        for g in range(1, 5):
+        for g in range(1, STEPS + 1):
             if g + 3 in ROUTED:
                 g_route(g + 3)
             g_fetch(g + 2)
             if g + 4 < PASSES:
                 widen_pass(g + 4, on_scalar=range(4))
-            j_interleave(g, FRONT, on_scalar=False)
-            if g > 1:
-                j_quant(g - 1, MID)
-            else:
+            j_interleave(g, WIDE, on_scalar=False)
+            if g == 1:
                 g_mx[1] = quantize("g1", keep, g_grouped(1), SEN)
+            if g - 1 in WITH_REST:
+                j_quant(g - 1, REST)
+            if g in WITH_REST:
+                j_interleave(g, REST, on_scalar=False)
             if g + 3 not in ROUTED:
-                for k in (1, 2):
-                    forward(k, MID)
+                forward(WITH_REST[0], MID)
             joint_quant(g)
             forward(g, WIDE)
 
         g_interleave(FINAL)
-        j_quant(4, MID)
         j_interleave(5, WIDE, on_scalar=True)
         j_interleave(6, WIDE, on_scalar=False)
-        forward(3, MID)
+        forward(WITH_REST[1], MID)
         joint_quant(5)
         v_turn()
         forward(5, WIDE)
         j_interleave(FINAL, WIDE, on_scalar=True)
         v_fetch()
         joint_quant(6)
-        forward(4, MID)
         forward(6, WIDE)
-        j_interleave(1, LAST, on_scalar=False)
-        j_interleave(5, MID, on_scalar=False)
-        j_quant(1, LAST)
+        for g in WITH_REST:
+            forward(g, LAST)
+        j_interleave(5, REST, on_scalar=False)
         joint_quant(FINAL)
-        forward(1, LAST)
         forward(FINAL, WIDE)
         j_interleave(*HANDOVER, on_scalar=True)
-        quant_forward(5, MID)
+        j_quant(5, REST)
         j_quant(*HANDOVER)
-        for cols in (MID, LAST):
-            forward(6, cols)
-        j_interleave_gpsimd(0, LAST)
-        for g, cols in ((2, LAST), (0, MID), (FINAL, MID), (3, LAST)):
-            j_interleave(g, cols, on_scalar=True)
+        for g in (5, HANDOVER[0]):
+            for cols in (MID, LAST):
+                forward(g, cols)
+        j_interleave_gpsimd(HALVED[0], LAST)
+        for g in HALVED:
+            j_interleave(g, MID, on_scalar=True)
 
         record(WIDE, WIDE, range(4))
-        for g, cols in ((2, LAST), (0, LAST), (0, MID), (FINAL, MID)):
-            quant_forward(g, cols)
-        for g in (4, 5, FINAL):
+        for cols in (MID, LAST):
+            quant_forward(HALVED[0], cols)
+        for g in HALVED[1:3]:
+            quant_forward(g, MID)
+        for g in HALVED[1:]:
             j_interleave(g, LAST, on_scalar=True)
         b_interleave(WIDE)
-        quant_forward(3, LAST)
+        quant_forward(FINAL, MID)
         whiten(WIDE, FIELD_BANK[WIDE], 4)
         for i in range(4):
             store(WIDE, i, on_scalar=True)
         for part in range(2):
-            quant_forward(4 + part, LAST)
+            quant_forward(HALVED[1 + part], LAST)
             record(MID, MID, (2 * part, 2 * part + 1))
         quant_forward(FINAL, LAST)
         b_interleave(MID)

@@ -22,7 +22,8 @@ FINAL = PASSES - 1
 STEPS = 4
 SHARED = (5, 6, FINAL)
 WITH_REST = (2, 3)
-HALVED = (0, FINAL - 1, 1, FINAL)
+HALVED = (0, FINAL - 1, 1)
+LATE = (HALVED[0], FINAL) + HALVED[1:]
 
 WIDE, MID, LAST = (0, 512), (512, 256), (768, 256)
 LAST_A, LAST_B = (768, 128), (896, 128)
@@ -35,7 +36,7 @@ PIECE_BUFS = 5
 WIDENED_BUFS = 4
 JOINT_BUFS = 4
 PLANE_GAP, PAIR_GAP = 18, 20
-HANDOVER = (STEPS, REST)
+HANDOVER = (STEPS, LAST)
 
 
 def tile_meg_forward_whitened_d3_kernel(tc, g_bytes, g_scale, j_in, gain_in, e_in, v_in, out):
@@ -108,15 +109,15 @@ def tile_meg_forward_whitened_d3_kernel(tc, g_bytes, g_scale, j_in, gain_in, e_i
             load_scales(g + 3, g + 4)
             load_g(g + 3)
             load_j(g, 0, half if g in HALVED else TIM)
-        for g in SHARED:
-            load_j(g, 0, half if g in HALVED else TIM)
+        load_j(SHARED[0], 0, TIM)
         nc.sync.dma_start(out=v_raw[:], in_=v_in.rearrange("(p b) s -> p b s", b=4))
+        for g in SHARED[1:]:
+            load_j(g, 0, half if g in HALVED else TIM)
         for g in HALVED[:2]:
             load_j(g, half, TIM)
         nc.sync.dma_start(out=gain[:], in_=gain_in.rearrange("(p u) -> p u", u=4))
         load_e(0, half)
-        for g in HALVED[2:]:
-            load_j(g, half, TIM)
+        load_j(HALVED[2], half, TIM)
         load_e(half, TIM)
 
         def quantize(name, pool, grouped, width):
@@ -195,7 +196,7 @@ def tile_meg_forward_whitened_d3_kernel(tc, g_bytes, g_scale, j_in, gain_in, e_i
                 if (g, cols) == HANDOVER:
                     tile = keep.tile([P, width, 4], BF16, name="j_handover", align_bytes=64)
                 elif cols == REST:
-                    tile = work.tile([P, width, 4], BF16, name="j_rest", bufs=1, align_bytes=64)
+                    tile = work.tile([P, width, 4], BF16, name="j_rest", bufs=2, align_bytes=64)
                 else:
                     tile = work.tile([P, width, 4], BF16, name="j_grp", bufs=PIECE_BUFS, align_bytes=64)
                 grouped = j_grp[g, cols] = tile[:]
@@ -348,15 +349,15 @@ def tile_meg_forward_whitened_d3_kernel(tc, g_bytes, g_scale, j_in, gain_in, e_i
         widen_pass(3, on_scalar=(2, 3))
         g_route(3, planes_first=True)
         for q in range(2):
-            widen(4, q, on_vector=True)
+            widen(4, q, on_vector=q == 0)
             g_fetch(2, (q,))
             widen(4, 2 + q, on_vector=False)
         joint_quant(0)
-        forward(0, WIDE)
 
         for g in range(1, STEPS + 1):
             if g + 3 in ROUTED:
                 g_route(g + 3)
+            forward(g - 1, WIDE)
             g_fetch(g + 2)
             if g + 4 < PASSES:
                 widen_pass(g + 4, on_scalar=range(4))
@@ -369,51 +370,53 @@ def tile_meg_forward_whitened_d3_kernel(tc, g_bytes, g_scale, j_in, gain_in, e_i
                 j_interleave(g, REST, on_scalar=False)
             if g + 3 not in ROUTED:
                 forward(WITH_REST[0], MID)
+                v_turn()
             joint_quant(g)
-            forward(g, WIDE)
+        forward(STEPS, WIDE)
 
         g_interleave(FINAL)
         j_interleave(5, WIDE, on_scalar=True)
+        v_fetch()
         j_interleave(6, WIDE, on_scalar=False)
         forward(WITH_REST[1], MID)
         joint_quant(5)
-        v_turn()
+        forward(WITH_REST[0], LAST)
         forward(5, WIDE)
+        j_interleave(STEPS, MID, on_scalar=True)
         j_interleave(FINAL, WIDE, on_scalar=True)
-        v_fetch()
         joint_quant(6)
+        forward(WITH_REST[1], LAST)
         forward(6, WIDE)
-        for g in WITH_REST:
-            forward(g, LAST)
         j_interleave(5, REST, on_scalar=False)
+        quant_forward(STEPS, MID)
         joint_quant(FINAL)
         forward(FINAL, WIDE)
         j_interleave(*HANDOVER, on_scalar=True)
         j_quant(5, REST)
         j_quant(*HANDOVER)
-        for g in (5, HANDOVER[0]):
-            for cols in (MID, LAST):
-                forward(g, cols)
-        j_interleave_gpsimd(HALVED[0], LAST)
-        for g in HALVED:
+        for cols in (MID, LAST):
+            forward(5, cols)
+        forward(*HANDOVER)
+        j_interleave_gpsimd(LATE[0], LAST)
+        for g in LATE:
             j_interleave(g, MID, on_scalar=True)
 
         record(WIDE, WIDE, range(4))
         for cols in (MID, LAST):
-            quant_forward(HALVED[0], cols)
-        for g in HALVED[1:3]:
+            quant_forward(LATE[0], cols)
+        for g in LATE[1:3]:
             quant_forward(g, MID)
-        for g in HALVED[1:]:
+        for g in LATE[1:]:
             j_interleave(g, LAST, on_scalar=True)
         b_interleave(WIDE)
-        quant_forward(FINAL, MID)
+        quant_forward(LATE[3], MID)
         whiten(WIDE, FIELD_BANK[WIDE], 4)
         for i in range(4):
             store(WIDE, i, on_scalar=True)
         for part in range(2):
-            quant_forward(HALVED[1 + part], LAST)
+            quant_forward(LATE[1 + part], LAST)
             record(MID, MID, (2 * part, 2 * part + 1))
-        quant_forward(FINAL, LAST)
+        quant_forward(LATE[3], LAST)
         b_interleave(MID)
         whiten(MID, FIELD_BANK[MID], 2)
         for i in range(2):

@@ -32,6 +32,8 @@ FIELD_BANK = {WIDE: 0, MID: 4, LAST: 6}
 
 ROUTED = (0, 2, 3, 4, 5, 6)
 
+SPLIT_PLANE = 256
+
 PIECE_BUFS = 5
 WIDENED_BUFS = 4
 JOINT_BUFS = 4
@@ -113,11 +115,11 @@ def tile_meg_forward_whitened_d3_kernel(tc, g_bytes, g_scale, j_in, gain_in, e_i
         nc.sync.dma_start(out=v_raw[:], in_=v_in.rearrange("(p b) s -> p b s", b=4))
         for g in SHARED[1:]:
             load_j(g, 0, half if g in HALVED else TIM)
-        for g in HALVED[:2]:
-            load_j(g, half, TIM)
+        load_j(HALVED[0], half, TIM)
         nc.sync.dma_start(out=gain[:], in_=gain_in.rearrange("(p u) -> p u", u=4))
         load_e(0, half)
-        load_j(HALVED[2], half, TIM)
+        for g in HALVED[1:]:
+            load_j(g, half, TIM)
         load_e(half, TIM)
 
         def quantize(name, pool, grouped, width):
@@ -148,15 +150,15 @@ def tile_meg_forward_whitened_d3_kernel(tc, g_bytes, g_scale, j_in, gain_in, e_i
 
         g_wide, g_mx, g_psum = {}, {}, {}
 
-        def widen(g, t, on_vector):
+        def widen(g, t, on_vector, n0=0, n1=SEN):
             if g not in g_wide:
                 g_wide[g] = work.tile([P, 4, SEN], BF16, name="g_wide", bufs=WIDENED_BUFS, align_bytes=64)
             scale = g_sc[g][:, t:t + 1]
-            src = g_raw[g][:, t, :].bitcast(FP8)
+            src = g_raw[g][:, t, n0:n1].bitcast(FP8)
             if on_vector:
-                nc.vector.tensor_scalar(out=g_wide[g][:, t, :], in0=src, scalar1=scale, scalar2=None, op0=MULT)
+                nc.vector.tensor_scalar(out=g_wide[g][:, t, n0:n1], in0=src, scalar1=scale, scalar2=None, op0=MULT)
             else:
-                nc.scalar.activation(out=g_wide[g][:, t, :], in_=src, func=COPY, scale=scale)
+                nc.scalar.activation(out=g_wide[g][:, t, n0:n1], in_=src, func=COPY, scale=scale)
 
         def g_interleave(g):
             nc.vector.tensor_copy(
@@ -325,12 +327,15 @@ def tile_meg_forward_whitened_d3_kernel(tc, g_bytes, g_scale, j_in, gain_in, e_i
         def store(cols, i, on_scalar):
             first, width = cols
             tiles, per_bank = white[cols]
-            y = keep.tile([P, per_bank, width], F32, name=spent.pop(0), align_bytes=64)
-            if on_scalar:
-                nc.scalar.copy(out=y[:], in_=tiles[i][:])
-            else:
-                nc.vector.tensor_copy(out=y[:], in_=tiles[i][:])
-            nc.sync.dma_start(out=out_view[:, i * per_bank:(i + 1) * per_bank, first:first + width], in_=y[:])
+            rows = per_bank * len(on_scalar)
+            y = keep.tile([P, rows, width], F32, name=spent.pop(0), align_bytes=64)
+            for k, scalar in enumerate(on_scalar):
+                part = y[:, k * per_bank:(k + 1) * per_bank, :]
+                if scalar:
+                    nc.scalar.copy(out=part, in_=tiles[i + k][:])
+                else:
+                    nc.vector.tensor_copy(out=part, in_=tiles[i + k][:])
+            nc.sync.dma_start(out=out_view[:, i * per_bank:i * per_bank + rows, first:first + width], in_=y[:])
 
         def widen_pass(g, on_scalar=()):
             for t in range(4):
@@ -349,7 +354,9 @@ def tile_meg_forward_whitened_d3_kernel(tc, g_bytes, g_scale, j_in, gain_in, e_i
         widen_pass(3, on_scalar=(2, 3))
         g_route(3, planes_first=True)
         for q in range(2):
-            widen(4, q, on_vector=q == 0)
+            widen(4, q, True, 0, SEN if q == 0 else SPLIT_PLANE)
+            if q:
+                widen(4, q, False, SPLIT_PLANE, SEN)
             g_fetch(2, (q,))
             widen(4, 2 + q, on_vector=False)
         joint_quant(0)
@@ -412,7 +419,7 @@ def tile_meg_forward_whitened_d3_kernel(tc, g_bytes, g_scale, j_in, gain_in, e_i
         quant_forward(LATE[3], MID)
         whiten(WIDE, FIELD_BANK[WIDE], 4)
         for i in range(4):
-            store(WIDE, i, on_scalar=True)
+            store(WIDE, i, on_scalar=(True,))
         for part in range(2):
             quant_forward(LATE[1 + part], LAST)
             record(MID, MID, (2 * part, 2 * part + 1))
@@ -420,7 +427,7 @@ def tile_meg_forward_whitened_d3_kernel(tc, g_bytes, g_scale, j_in, gain_in, e_i
         b_interleave(MID)
         whiten(MID, FIELD_BANK[MID], 2)
         for i in range(2):
-            store(MID, i, on_scalar=True)
+            store(MID, i, on_scalar=(True,))
 
         record(LAST_A, LAST, range(4))
         record(LAST_B, LAST, (0, 1))
@@ -428,8 +435,8 @@ def tile_meg_forward_whitened_d3_kernel(tc, g_bytes, g_scale, j_in, gain_in, e_i
         record(LAST_B, LAST, (2, 3))
         whiten(LAST_A, 0, 2)
         b_interleave(LAST_B)
+        whiten(LAST_B, 2, 4)
         for i in range(2):
-            store(LAST_A, i, on_scalar=True)
-        whiten(LAST_B, 2, 2)
-        for i in range(2):
-            store(LAST_B, i, on_scalar=i == 0)
+            store(LAST_A, i, on_scalar=(i == 0,))
+        for i in (0, 2):
+            store(LAST_B, i, on_scalar=(True, False))

@@ -65,10 +65,10 @@ def tile_meg_forward_whitened_d3_kernel(tc, g_bytes, g_scale, j_in, gain_in, e_i
         g_raw, g_sc, j_raw, noise = {}, {}, {}, {}
 
         def load_scales(g0, g1):
-            tile = keep.tile([P, g1 - g0, 4], F32, name="g_sc%d" % g0)
-            nc.sync.dma_start(out=tile[:], in_=gs_view[:, g0:g1, :])
+            tile = keep.tile([P, g1 - g0, 8], F32, name="g_sc%d" % g0)
+            nc.sync.dma_start(out=tile[:, :, :4], in_=gs_view[:, g0:g1, :])
             for g in range(g0, g1):
-                g_sc[g] = tile[:, g - g0, :]
+                g_sc[g] = tile[:, g - g0, :4]
 
         def load_g(g):
             g_raw[g] = keep.tile([P, 4, SEN], U8, name="g_raw%d" % g, align_bytes=64)

@@ -19,26 +19,16 @@ COPY = mybir.ActivationFunctionType.Copy
 P = 128
 PASSES = SRC // 512
 FINAL = PASSES - 1
-STEPS = 4
-SHARED = (5, 6, FINAL)
-WITH_REST = (2, 3)
-HALVED = (0, FINAL - 1, 1)
-LATE = (HALVED[0], FINAL) + HALVED[1:]
-
-WIDE, MID, LAST = (0, 512), (512, 256), (768, 256)
-LAST_A, LAST_B = (768, 128), (896, 128)
+WIDE, MID, LAST_A, LAST_B = (0, 512), (512, 256), (768, 128), (896, 128)
+LAST = (768, 256)
 REST = (512, 512)
-FIELD_BANK = {WIDE: 0, MID: 4, LAST: 6}
-
 ROUTED = (0, 2, 3, 4, 5, 6)
-
-SPLIT_PLANE = 256
-
-PIECE_BUFS = 5
-WIDENED_BUFS = 4
-JOINT_BUFS = 4
 PLANE_GAP, PAIR_GAP = 18, 20
-HANDOVER = (STEPS, LAST)
+JOINT_COLS = SEN + 512
+JOINT_BUFS, WIDENED_BUFS, PIECE_BUFS, REST_BUFS = 4, 4, 5, 2
+FIELD_BANKS = {WIDE: (0, 1, 2, 3), MID: (4, 5), LAST: (6, 7)}
+SPLIT_PLANE = 256
+SPLIT_LOADS = (0,)
 
 
 def tile_meg_forward_whitened_d3_kernel(tc, g_bytes, g_scale, j_in, gain_in, e_in, v_in, out):
@@ -62,7 +52,7 @@ def tile_meg_forward_whitened_d3_kernel(tc, g_bytes, g_scale, j_in, gain_in, e_i
         gb_view = g_bytes.rearrange("(g p t) s -> g p t s", p=P, t=4)
         j_view = j_in.rearrange("(g p t) n -> g p t n", p=P, t=4)
         e_view = e_in.rearrange("(p u) n -> p u n", u=4)
-        g_raw, g_sc, j_raw, noise = {}, {}, {}, {}
+        g_raw, g_sc, j_raw, noise = {}, {}, {}, []
 
         def load_scales(g0, g1):
             tile = keep.tile([P, g1 - g0, 8], F32, name="g_sc%d" % g0)
@@ -72,7 +62,7 @@ def tile_meg_forward_whitened_d3_kernel(tc, g_bytes, g_scale, j_in, gain_in, e_i
 
         def load_g(g):
             g_raw[g] = keep.tile([P, 4, SEN], U8, name="g_raw%d" % g, align_bytes=64)
-            for t0, t1 in ((0, 2), (2, 4)) if g == 0 else ((0, 4),):
+            for t0, t1 in ((0, 2), (2, 4)) if g in SPLIT_LOADS else ((0, 4),):
                 nc.sync.dma_start(out=g_raw[g][:, t0:t1, :], in_=gb_view[g][:, t0:t1, :])
 
         def load_j(g, n0, n1):
@@ -85,19 +75,28 @@ def tile_meg_forward_whitened_d3_kernel(tc, g_bytes, g_scale, j_in, gain_in, e_i
                 tile = keep.tile([P, 4, n1 - n0 + PLANE_GAP], BF16, name=name, align_bytes=64)
                 nc.sync.dma_start(out=tile[:, :, :n1 - n0], in_=j_view[g][:, :, n0:n1])
                 planes = tile[:, :, :n1 - n0].rearrange("p (h e) n -> p h e n", e=2)
-            for first, width in (WIDE, MID, LAST, REST):
+            j_raw.setdefault(g, []).append((n0, n1, planes))
+
+        def j_planes(g, cols):
+            first, width = cols
+            for n0, n1, planes in j_raw[g]:
                 if n0 <= first and first + width <= n1:
-                    j_raw[g, (first, width)] = planes[:, :, :, first - n0:first - n0 + width]
+                    return planes[:, :, :, first - n0:first - n0 + width]
+            raise ValueError("columns not loaded")
 
         def load_e(n0, n1):
             tile = keep.tile([P, 4, n1 - n0], BF16, name="noise%d" % n0, align_bytes=64)
             nc.sync.dma_start(out=tile[:], in_=e_view[:, :, n0:n1])
-            for first, width in (WIDE, MID, LAST_A, LAST_B):
-                if n0 <= first < n1:
-                    noise[first] = tile[:, :, first - n0:first - n0 + width]
+            noise.append((n0, n1, tile))
 
         v_raw = keep.tile([P, 4, SEN], BF16, name="v_raw", align_bytes=64)
         gain = keep.tile([P, 4], BF16, name="gain")
+
+        def load_v():
+            nc.sync.dma_start(out=v_raw[:], in_=v_in.rearrange("(p b) s -> p b s", b=4))
+
+        def load_gain():
+            nc.sync.dma_start(out=gain[:], in_=gain_in.rearrange("(p u) -> p u", u=4))
 
         half = WIDE[1]
         load_scales(0, 2)
@@ -107,33 +106,43 @@ def tile_meg_forward_whitened_d3_kernel(tc, g_bytes, g_scale, j_in, gain_in, e_i
         load_g(2)
         load_j(0, 0, half)
         load_g(3)
-        for g in range(1, STEPS + 1):
+        for g in range(1, 5):
             load_scales(g + 3, g + 4)
             load_g(g + 3)
-            load_j(g, 0, half if g in HALVED else TIM)
-        load_j(SHARED[0], 0, TIM)
-        nc.sync.dma_start(out=v_raw[:], in_=v_in.rearrange("(p b) s -> p b s", b=4))
-        for g in SHARED[1:]:
-            load_j(g, 0, half if g in HALVED else TIM)
-        load_j(HALVED[0], half, TIM)
-        nc.sync.dma_start(out=gain[:], in_=gain_in.rearrange("(p u) -> p u", u=4))
+            load_j(g, 0, half if g == 1 else TIM)
+        load_j(5, 0, TIM)
+        load_v()
+        load_j(6, 0, half)
+        load_j(7, 0, TIM)
+        load_j(0, half, TIM)
+        load_gain()
         load_e(0, half)
-        for g in HALVED[1:]:
-            load_j(g, half, TIM)
+        load_j(6, half, TIM)
+        load_j(1, half, TIM)
         load_e(half, TIM)
 
-        def quantize(name, pool, grouped, width):
-            codes = pool.tile([P, width], U32, name="codes_" + name, align_bytes=64)
-            scales = pool.tile([P, width], U8, name="scales_" + name, align_bytes=64)
+        def quantize(name, grouped, width):
+            codes = keep.tile([P, width], U32, name="codes_" + name, align_bytes=64)
+            scales = keep.tile([P, width], U8, name="scales_" + name, align_bytes=64)
             nc.vector.quantize_mx(
                 out=codes[:].bitcast(FP8X4), scales=scales[:], in_=grouped.rearrange("p n t -> p (n t)")
             )
             return codes, scales
 
-        def interleave(on_scalar, grouped, planes):
+        def interleave(engine, grouped, planes):
+            if engine == "gpsimd":
+                nc.gpsimd.tensor_scalar(
+                    out=grouped.rearrange("p n (h e) -> p n h e", e=2),
+                    in0=planes.rearrange("p h e n -> p n h e"),
+                    scalar1=1.0,
+                    scalar2=0.0,
+                    op0=MULT,
+                    op1=ADD,
+                )
+                return
             dst = grouped.rearrange("p (c i) (h e) -> p c h e i", i=2, e=2)
             src = planes.rearrange("p h e (c i) -> p c h e i", i=2)
-            if on_scalar:
+            if engine == "scalar":
                 nc.scalar.copy(out=dst, in_=src)
             else:
                 nc.vector.tensor_copy(out=dst, in_=src)
@@ -142,7 +151,7 @@ def tile_meg_forward_whitened_d3_kernel(tc, g_bytes, g_scale, j_in, gain_in, e_i
 
         def joint_part(g, n0, n1):
             if g not in joint:
-                joint[g] = work.tile([P, 4 * (SEN + WIDE[1])], BF16, name="joint", bufs=JOINT_BUFS, align_bytes=64)
+                joint[g] = work.tile([P, 4 * JOINT_COLS], BF16, name="joint", bufs=JOINT_BUFS, align_bytes=64)
             return joint[g][:, 4 * n0:4 * n1].rearrange("p (n t) -> p n t", t=4)
 
         def g_grouped(g):
@@ -159,6 +168,10 @@ def tile_meg_forward_whitened_d3_kernel(tc, g_bytes, g_scale, j_in, gain_in, e_i
                 nc.vector.tensor_scalar(out=g_wide[g][:, t, n0:n1], in0=src, scalar1=scale, scalar2=None, op0=MULT)
             else:
                 nc.scalar.activation(out=g_wide[g][:, t, n0:n1], in_=src, func=COPY, scale=scale)
+
+        def widen_pass(g, on_scalar=()):
+            for t in range(4):
+                widen(g, t, on_vector=t not in on_scalar)
 
         def g_interleave(g):
             nc.vector.tensor_copy(
@@ -190,57 +203,54 @@ def tile_meg_forward_whitened_d3_kernel(tc, g_bytes, g_scale, j_in, gain_in, e_i
 
         j_grp, j_mx, field = {}, {}, {}
 
-        def j_interleave(g, cols, on_scalar):
-            first, width = cols
-            if first == 0:
-                grouped = joint_part(g, SEN, SEN + width)
-            else:
-                if (g, cols) == HANDOVER:
-                    tile = keep.tile([P, width, 4], BF16, name="j_handover", align_bytes=64)
-                elif cols == REST:
-                    tile = work.tile([P, width, 4], BF16, name="j_rest", bufs=2, align_bytes=64)
-                else:
-                    tile = work.tile([P, width, 4], BF16, name="j_grp", bufs=PIECE_BUFS, align_bytes=64)
-                grouped = j_grp[g, cols] = tile[:]
-            interleave(on_scalar, grouped, j_raw[g, cols])
+        def j_joint(g, engine, n0=0, n1=WIDE[1]):
+            interleave(engine, joint_part(g, SEN + n0, SEN + n1), j_planes(g, (n0, n1 - n0)))
 
-        def j_interleave_gpsimd(g, cols):
-            tile = keep.tile([P, cols[1], 4], BF16, name="j_handover", align_bytes=64)
-            j_grp[g, cols] = tile[:]
-            nc.gpsimd.tensor_scalar(
-                out=tile[:],
-                in0=j_raw[g, cols].rearrange("p h e n -> p n (h e)"),
-                scalar1=1.0,
-                scalar2=0.0,
-                op0=MULT,
-                op1=ADD,
-            )
+        def j_piece(g, cols, engine, tag=None, part=None):
+            if (g, cols) not in j_grp:
+                if tag is not None:
+                    tile = keep.tile([P, cols[1], 4], BF16, name=tag, align_bytes=64)
+                elif cols[1] == REST[1]:
+                    tile = work.tile([P, cols[1], 4], BF16, name="j_rest", bufs=REST_BUFS, align_bytes=64)
+                else:
+                    tile = work.tile([P, cols[1], 4], BF16, name="j_grp", bufs=PIECE_BUFS, align_bytes=64)
+                j_grp[g, cols] = tile[:]
+            part = part or cols
+            n0 = part[0] - cols[0]
+            interleave(engine, j_grp[g, cols][:, n0:n0 + part[1], :], j_planes(g, part))
+
+        def hand_out(g, cols, codes, scales):
+            for n0, w in FIELD_BANKS:
+                if cols[0] <= n0 and n0 + w <= cols[0] + cols[1]:
+                    j_mx[g, (n0, w)] = codes[:, n0 - cols[0]:n0 - cols[0] + w], scales[:, n0 - cols[0]:n0 - cols[0] + w]
 
         def j_quant(g, cols):
-            first, width = cols
-            codes, scales = quantize("j%d_%d" % (first, g), keep, j_grp[g, cols], width)
-            for n0, w in (MID, LAST):
-                if first <= n0 < first + width:
-                    j_mx[g, (n0, w)] = codes[:, n0 - first:n0 - first + w], scales[:, n0 - first:n0 - first + w]
+            codes, scales = quantize("j%d_%d" % (cols[0], g), j_grp[g, cols], cols[1])
+            hand_out(g, cols, codes, scales)
 
         def joint_quant(g):
-            codes, scales = quantize("joint%d" % g, keep, joint_part(g, 0, SEN + WIDE[1]), SEN + WIDE[1])
-            j_mx[g, WIDE] = codes[:, SEN:], scales[:, SEN:]
+            codes, scales = quantize("joint%d" % g, joint_part(g, 0, SEN + WIDE[1]), SEN + WIDE[1])
+            hand_out(g, WIDE, codes[:, SEN:], scales[:, SEN:])
             g_mx[g + 1 if g else 0] = codes[:, :SEN], scales[:, :SEN]
 
-        def bank_tiles(first_bank, banks, width):
-            per_bank = 4 // banks
+        def joint_mid_quant(g):
+            codes, scales = quantize("mid%d" % g, joint_part(g, SEN + MID[0], SEN + MID[0] + MID[1]), MID[1])
+            hand_out(g, MID, codes, scales)
+
+        def bank_tiles(banks, width):
+            per_bank = 4 // len(banks)
             tiles = []
-            for b in range(banks):
-                tile = psum.tile([P, per_bank, width], F32, name="bank%d" % (first_bank + b))
+            for b in banks:
+                tile = psum.tile([P, per_bank, width], F32, name="bank%d" % b)
                 tiles.append(tile)
             return tiles, per_bank
 
-        passes_done = {WIDE: [], MID: [], LAST: []}
+        passes_done = {}
 
         def forward(g, cols):
-            if not passes_done[cols]:
-                field[cols] = bank_tiles(FIELD_BANK[cols], cols[1] // P, cols[1])
+            if cols not in passes_done:
+                passes_done[cols] = []
+                field[cols] = bank_tiles(FIELD_BANKS[cols], cols[1])
             passes_done[cols].append(g)
             tiles, per_bank = field[cols]
             codes, scales = j_mx[g, cols]
@@ -255,16 +265,21 @@ def tile_meg_forward_whitened_d3_kernel(tc, g_bytes, g_scale, j_in, gain_in, e_i
                     stop=(len(passes_done[cols]) == PASSES and u % per_bank == per_bank - 1),
                 )
 
+        def forward_all(g, cols):
+            for stretch in FIELD_BANKS:
+                if cols[0] <= stretch[0] and stretch[0] + stretch[1] <= cols[0] + cols[1]:
+                    forward(g, stretch)
+
         def quant_forward(g, cols):
             j_quant(g, cols)
-            forward(g, cols)
+            forward_all(g, cols)
 
         v_psum = []
 
         def v_turn():
             words = v_raw[:].rearrange("p b s -> p (b s)").bitcast(F32)
             for h in range(2):
-                turned = psum.tile([P, 2, 2, P], F32, name="bank%d" % (FIELD_BANK[LAST] + h))
+                turned = psum.tile([P, 2, 2, P], F32, name="bank%d" % (6 + h))
                 v_psum.append(turned)
                 for b in range(2):
                     for w in range(2):
@@ -279,7 +294,7 @@ def tile_meg_forward_whitened_d3_kernel(tc, g_bytes, g_scale, j_in, gain_in, e_i
                     in_=v_psum[h][:].rearrange("p b w r -> p b r w"),
                 )
 
-        b_planes, b_grp, white = {}, {}, {}
+        b_planes, b_grp, b_mx, white = {}, {}, {}, {}
 
         def record(cols, stretch, planes):
             first, width = cols
@@ -289,25 +304,43 @@ def tile_meg_forward_whitened_d3_kernel(tc, g_bytes, g_scale, j_in, gain_in, e_i
                 )
             tiles, per_bank = field[stretch]
             n0 = first - stretch[0]
+            e0, e_tile = [(a, tile) for a, b, tile in noise if a <= first < b][0]
             for u in planes:
                 nc.vector.scalar_tensor_tensor(
                     out=b_planes[cols][:, u, :width],
                     in0=tiles[u // per_bank][:, u % per_bank, n0:n0 + width],
                     scalar=gain[:, u:u + 1],
-                    in1=noise[first][:, u, :],
+                    in1=e_tile[:, u, first - e0:first - e0 + width],
                     op0=MULT,
                     op1=ADD,
                 )
 
-        def b_interleave(cols):
-            b_grp[cols] = work.tile([P, cols[1], 4], BF16, name="joint", bufs=JOINT_BUFS, align_bytes=64)
-            planes = b_planes[cols][:, :, :cols[1]].rearrange("p (h e) n -> p h e n", e=2)
-            interleave(False, b_grp[cols][:], planes)
+        def b_interleave(cols, engine, n0=0, n1=None):
+            n1 = n1 or cols[1]
+            if cols not in b_grp:
+                b_grp[cols] = work.tile([P, cols[1], 4], BF16, name="joint", bufs=JOINT_BUFS, align_bytes=64)
+            planes = b_planes[cols][:, :, n0:n1].rearrange("p (h e) n -> p h e n", e=2)
+            interleave(engine, b_grp[cols][:, n0:n1, :], planes)
 
-        def whiten(cols, first_bank, banks):
-            codes, scales = quantize("b%d" % cols[0], keep, b_grp[cols][:], cols[1])
+        def b_quant(cols, n0=0, n1=None):
+            n1 = n1 or cols[1]
+            if cols not in b_mx:
+                codes = keep.tile([P, cols[1]], U32, name="codes_b%d" % cols[0], align_bytes=64)
+                scales = keep.tile([P, cols[1]], U8, name="scales_b%d" % cols[0], align_bytes=64)
+                b_mx[cols] = codes, scales
+            codes, scales = b_mx[cols]
+            nc.vector.quantize_mx(
+                out=codes[:, n0:n1].bitcast(FP8X4),
+                scales=scales[:, n0:n1],
+                in_=b_grp[cols][:, n0:n1, :].rearrange("p n t -> p (n t)"),
+            )
+
+        def whiten(cols, banks):
+            if cols not in b_mx:
+                b_quant(cols)
+            codes, scales = b_mx[cols]
             v_mx = g_mx[PASSES]
-            white[cols] = bank_tiles(first_bank, banks, cols[1])
+            white[cols] = bank_tiles(banks, cols[1])
             tiles, per_bank = white[cols]
             for b in range(4):
                 nc.tensor.matmul_mx(
@@ -321,8 +354,7 @@ def tile_meg_forward_whitened_d3_kernel(tc, g_bytes, g_scale, j_in, gain_in, e_i
                 )
 
         out_view = out.rearrange("(p b) n -> p b n", b=4)
-
-        spent = ["j_raw%d_0" % g for g in range(PASSES)] + ["j_raw%d_%d" % (g, half) for g in HALVED[:2]]
+        spent = ["j_raw%d_0" % g for g in range(PASSES)] + ["v_raw", "noise0", "g_raw0", "g_raw1"]
 
         def store(cols, i, on_scalar):
             first, width = cols
@@ -337,11 +369,7 @@ def tile_meg_forward_whitened_d3_kernel(tc, g_bytes, g_scale, j_in, gain_in, e_i
                     nc.vector.tensor_copy(out=part, in_=tiles[i + k][:])
             nc.sync.dma_start(out=out_view[:, i * per_bank:i * per_bank + rows, first:first + width], in_=y[:])
 
-        def widen_pass(g, on_scalar=()):
-            for t in range(4):
-                widen(g, t, on_vector=t not in on_scalar)
-
-        widen_pass(0, on_scalar=(2,))
+        widen_pass(0, on_scalar=(1, 3))
         g_route(0)
         widen_pass(1, on_scalar=(3,))
         widen(2, 0, on_vector=True)
@@ -350,93 +378,95 @@ def tile_meg_forward_whitened_d3_kernel(tc, g_bytes, g_scale, j_in, gain_in, e_i
             widen(2, t, on_vector=False)
         g_fetch(0)
         g_route(2, planes_first=True)
-        j_interleave(0, WIDE, on_scalar=False)
+        j_joint(0, "vector")
         widen_pass(3, on_scalar=(2, 3))
         g_route(3, planes_first=True)
         for q in range(2):
-            widen(4, q, True, 0, SEN if q == 0 else SPLIT_PLANE)
-            if q:
-                widen(4, q, False, SPLIT_PLANE, SEN)
+            widen(4, q, True)
             g_fetch(2, (q,))
             widen(4, 2 + q, on_vector=False)
         joint_quant(0)
 
-        for g in range(1, STEPS + 1):
+        for g in range(1, 5):
             if g + 3 in ROUTED:
                 g_route(g + 3)
             forward(g - 1, WIDE)
             g_fetch(g + 2)
             if g + 4 < PASSES:
                 widen_pass(g + 4, on_scalar=range(4))
-            j_interleave(g, WIDE, on_scalar=False)
+            j_joint(g, "vector")
             if g == 1:
-                g_mx[1] = quantize("g1", keep, g_grouped(1), SEN)
-            if g - 1 in WITH_REST:
+                g_mx[1] = quantize("g1", g_grouped(1), SEN)
+            if g - 1 in (2, 3):
                 j_quant(g - 1, REST)
-            if g in WITH_REST:
-                j_interleave(g, REST, on_scalar=False)
-            if g + 3 not in ROUTED:
-                forward(WITH_REST[0], MID)
+            if g in (2, 3):
+                j_piece(g, REST, "vector")
+            if g == 4:
+                forward(2, MID)
                 v_turn()
             joint_quant(g)
-        forward(STEPS, WIDE)
-
+        forward(4, WIDE)
         g_interleave(FINAL)
-        j_interleave(5, WIDE, on_scalar=True)
+        j_joint(5, "scalar")
         v_fetch()
-        j_interleave(6, WIDE, on_scalar=False)
-        forward(WITH_REST[1], MID)
+        j_joint(6, "vector")
+        forward(3, MID)
         joint_quant(5)
-        forward(WITH_REST[0], LAST)
+        forward(2, LAST)
         forward(5, WIDE)
-        j_interleave(STEPS, MID, on_scalar=True)
-        j_interleave(FINAL, WIDE, on_scalar=True)
+        j_piece(4, MID, "scalar")
+        j_joint(7, "scalar")
         joint_quant(6)
-        forward(WITH_REST[1], LAST)
+        forward(3, LAST)
         forward(6, WIDE)
-        j_interleave(5, REST, on_scalar=False)
-        quant_forward(STEPS, MID)
-        joint_quant(FINAL)
-        forward(FINAL, WIDE)
-        j_interleave(*HANDOVER, on_scalar=True)
+        j_piece(5, REST, "vector")
+        quant_forward(4, MID)
+        joint_quant(7)
+        forward(7, WIDE)
+        j_piece(4, LAST, "scalar", tag="hand")
         j_quant(5, REST)
-        j_quant(*HANDOVER)
-        for cols in (MID, LAST):
-            forward(5, cols)
-        forward(*HANDOVER)
-        j_interleave_gpsimd(LATE[0], LAST)
-        for g in LATE:
-            j_interleave(g, MID, on_scalar=True)
-
+        j_quant(4, LAST)
+        forward(5, MID)
+        forward(5, LAST)
+        forward(4, LAST)
+        j_piece(0, LAST, "gpsimd", tag="hand")
+        for g in (0, 7, 6, 1):
+            j_piece(g, MID, "scalar")
         record(WIDE, WIDE, range(4))
-        for cols in (MID, LAST):
-            quant_forward(LATE[0], cols)
-        for g in LATE[1:3]:
-            quant_forward(g, MID)
-        for g in LATE[1:]:
-            j_interleave(g, LAST, on_scalar=True)
-        b_interleave(WIDE)
-        quant_forward(LATE[3], MID)
-        whiten(WIDE, FIELD_BANK[WIDE], 4)
+        quant_forward(0, MID)
+        quant_forward(0, LAST)
+        quant_forward(7, MID)
+        quant_forward(6, MID)
+        for g in (7, 6, 1):
+            j_piece(g, LAST, "scalar")
+        b_interleave(WIDE, "vector")
+        quant_forward(1, MID)
+        whiten(WIDE, (0, 1, 2, 3))
         for i in range(4):
-            store(WIDE, i, on_scalar=(True,))
-        for part in range(2):
-            quant_forward(LATE[1 + part], LAST)
-            record(MID, MID, (2 * part, 2 * part + 1))
-        quant_forward(LATE[3], LAST)
-        b_interleave(MID)
-        whiten(MID, FIELD_BANK[MID], 2)
+            store(WIDE, i, (True,))
+        quant_forward(7, LAST)
+        record(MID, MID, (0, 1))
+        quant_forward(6, LAST)
+        record(MID, MID, (2, 3))
+        quant_forward(1, LAST)
+        b_interleave(MID, "vector", 0, 128)
+        b_interleave(MID, "vector", 128, 256)
+        b_quant(MID, 0, 128)
+        b_quant(MID, 128, 256)
+        whiten(MID, (4, 5))
         for i in range(2):
-            store(MID, i, on_scalar=(True,))
-
+            store(MID, i, (True,))
         record(LAST_A, LAST, range(4))
         record(LAST_B, LAST, (0, 1))
-        b_interleave(LAST_A)
+        b_interleave(LAST_A, "vector")
         record(LAST_B, LAST, (2, 3))
-        whiten(LAST_A, 0, 2)
-        b_interleave(LAST_B)
-        whiten(LAST_B, 2, 4)
+        whiten(LAST_A, (0, 1))
+        b_interleave(LAST_B, "vector", 0, 64)
+        b_interleave(LAST_B, "vector", 64, 128)
+        b_quant(LAST_B, 0, 64)
+        b_quant(LAST_B, 64, 128)
+        whiten(LAST_B, (2, 3, 4, 5))
         for i in range(2):
-            store(LAST_A, i, on_scalar=(i == 0,))
+            store(LAST_A, i, (i == 0,))
         for i in (0, 2):
-            store(LAST_B, i, on_scalar=(True, False))
+            store(LAST_B, i, (True, False))

@@ -28,7 +28,7 @@ JOINT_COLS = SEN + 512
 JOINT_BUFS, WIDENED_BUFS, PIECE_BUFS, REST_BUFS = 4, 4, 5, 2
 FIELD_BANKS = {WIDE: (0, 1, 2, 3), MID: (4, 5), LAST: (6, 7)}
 SPLIT_PLANE = 256
-SPLIT_LOADS = (0,)
+SPLIT_LOADS = (0, 1)
 
 
 def tile_meg_forward_whitened_d3_kernel(tc, g_bytes, g_scale, j_in, gain_in, e_in, v_in, out):
@@ -40,13 +40,6 @@ def tile_meg_forward_whitened_d3_kernel(tc, g_bytes, g_scale, j_in, gain_in, e_i
         psum = ctx.enter_context(tc.psum_pool(name="psum", bufs=1))
         ctx.enter_context(tc.manual_schedule())
 
-        zeros = keep.tile([P, P], F32, name="zeros")
-        nc.vector.memset(zeros[:], 0.0)
-        ident_b = keep.tile([P, P], BF16, name="ident_b")
-        make_identity(nc, ident_b[:])
-        ident = keep.tile([P, P], F32, name="ident")
-        nc.scalar.activation(out=ident[:], in_=zeros[:], func=COPY)
-        make_identity(nc, ident[:], nomemset=True)
 
         gs_view = g_scale.rearrange("(g p t) o -> p g (t o)", p=P, t=4)
         gb_view = g_bytes.rearrange("(g p t) s -> g p t s", p=P, t=4)
@@ -56,7 +49,8 @@ def tile_meg_forward_whitened_d3_kernel(tc, g_bytes, g_scale, j_in, gain_in, e_i
 
         def load_scales(g0, g1):
             tile = keep.tile([P, g1 - g0, 8], F32, name="g_sc%d" % g0)
-            nc.sync.dma_start(out=tile[:, :, :4], in_=gs_view[:, g0:g1, :])
+            queue = nc.scalar if g0 < 1 else nc.sync
+            queue.dma_start(out=tile[:, :, :4], in_=gs_view[:, g0:g1, :])
             for g in range(g0, g1):
                 g_sc[g] = tile[:, g - g0, :4]
 
@@ -99,15 +93,23 @@ def tile_meg_forward_whitened_d3_kernel(tc, g_bytes, g_scale, j_in, gain_in, e_i
             nc.sync.dma_start(out=gain[:], in_=gain_in.rearrange("(p u) -> p u", u=4))
 
         half = WIDE[1]
-        load_scales(0, 2)
+        load_scales(0, 3)
+        zeros = keep.tile([P, P], F32, name="zeros")
+        nc.vector.memset(zeros[:], 0.0)
+        ident_b = keep.tile([P, P], BF16, name="ident_b")
+        make_identity(nc, ident_b[:])
+        ident = keep.tile([P, P], F32, name="ident")
+        nc.scalar.activation(out=ident[:], in_=zeros[:], func=COPY)
+        make_identity(nc, ident[:], nomemset=True)
         load_g(0)
         load_g(1)
-        load_scales(2, 4)
         load_g(2)
         load_j(0, 0, half)
+        load_scales(3, 5)
         load_g(3)
         for g in range(1, 5):
-            load_scales(g + 3, g + 4)
+            if g > 1:
+                load_scales(g + 3, g + 4)
             load_g(g + 3)
             load_j(g, 0, half if g == 1 else TIM)
         load_j(5, 0, TIM)
@@ -382,7 +384,9 @@ def tile_meg_forward_whitened_d3_kernel(tc, g_bytes, g_scale, j_in, gain_in, e_i
         widen_pass(3, on_scalar=(2, 3))
         g_route(3, planes_first=True)
         for q in range(2):
-            widen(4, q, True)
+            widen(4, q, True, 0, SEN if q == 0 else SPLIT_PLANE)
+            if q:
+                widen(4, q, False, SPLIT_PLANE, SEN)
             g_fetch(2, (q,))
             widen(4, 2 + q, on_vector=False)
         joint_quant(0)

@@ -23,7 +23,7 @@ WIDE, MID, LAST_A, LAST_B = (0, 512), (512, 256), (768, 128), (896, 128)
 LAST = (768, 256)
 REST = (512, 512)
 ROUTED = (0, 2, 3, 4, 5, 6)
-PLANE_GAP, PAIR_GAP = 18, 20
+PLANE_GAP, PAIR_GAP = 20, 20
 JOINT_COLS = SEN + 512
 JOINT_BUFS, WIDENED_BUFS, PIECE_BUFS, REST_BUFS = 4, 4, 5, 2
 FIELD_BANKS = {WIDE: (0, 1, 2, 3), MID: (4, 5), LAST: (6, 7)}

@@ -428,8 +428,8 @@ def tile_meg_forward_whitened_d3_kernel(tc, g_bytes, g_scale, j_in, gain_in, e_i
         joint_quant(7)
         forward(7, WIDE)
         j_piece(4, LAST, "scalar", tag="hand")
-        j_quant(5, REST)
         j_quant(4, LAST)
+        j_quant(5, REST)
         forward(5, MID)
         forward(5, LAST)
         forward(4, LAST)

@@ -25,10 +25,12 @@ REST = (512, 512)
 ROUTED = (0, 2, 3, 4, 5, 6)
 PLANE_GAP, PAIR_GAP = 20, 20
 JOINT_COLS = SEN + 512
-JOINT_BUFS, WIDENED_BUFS, PIECE_BUFS, REST_BUFS = 4, 4, 5, 2
+JOINT_BUFS, WIDENED_BUFS, PIECE_BUFS, REST_BUFS = 4, 4, 4, 2
 FIELD_BANKS = {WIDE: (0, 1, 2, 3), MID: (4, 5), LAST: (6, 7)}
 SPLIT_PLANE = 256
 SPLIT_LOADS = (0, 1)
+POOL_COLS = 352
+SCALAR_B = 96
 
 
 def tile_meg_forward_whitened_d3_kernel(tc, g_bytes, g_scale, j_in, gain_in, e_in, v_in, out):
@@ -69,13 +71,13 @@ def tile_meg_forward_whitened_d3_kernel(tc, g_bytes, g_scale, j_in, gain_in, e_i
                 tile = keep.tile([P, 4, n1 - n0 + PLANE_GAP], BF16, name=name, align_bytes=64)
                 nc.sync.dma_start(out=tile[:, :, :n1 - n0], in_=j_view[g][:, :, n0:n1])
                 planes = tile[:, :, :n1 - n0].rearrange("p (h e) n -> p h e n", e=2)
-            j_raw.setdefault(g, []).append((n0, n1, planes))
+            j_raw.setdefault(g, []).append((n0, n1, planes, "c e h i" if n1 - n0 == TIM else "c h e i"))
 
         def j_planes(g, cols):
             first, width = cols
-            for n0, n1, planes in j_raw[g]:
+            for n0, n1, planes, walk in j_raw[g]:
                 if n0 <= first and first + width <= n1:
-                    return planes[:, :, :, first - n0:first - n0 + width]
+                    return planes[:, :, :, first - n0:first - n0 + width], walk
             raise ValueError("columns not loaded")
 
         def load_e(n0, n1):
@@ -131,7 +133,7 @@ def tile_meg_forward_whitened_d3_kernel(tc, g_bytes, g_scale, j_in, gain_in, e_i
             )
             return codes, scales
 
-        def interleave(engine, grouped, planes):
+        def interleave(engine, grouped, planes, walk="c h e i"):
             if engine == "gpsimd":
                 nc.gpsimd.tensor_scalar(
                     out=grouped.rearrange("p n (h e) -> p n h e", e=2),
@@ -142,8 +144,8 @@ def tile_meg_forward_whitened_d3_kernel(tc, g_bytes, g_scale, j_in, gain_in, e_i
                     op1=ADD,
                 )
                 return
-            dst = grouped.rearrange("p (c i) (h e) -> p c h e i", i=2, e=2)
-            src = planes.rearrange("p h e (c i) -> p c h e i", i=2)
+            dst = grouped.rearrange("p (c i) (h e) -> p " + walk, i=2, e=2)
+            src = planes.rearrange("p h e (c i) -> p " + walk, i=2)
             if engine == "scalar":
                 nc.scalar.copy(out=dst, in_=src)
             else:
@@ -206,20 +208,18 @@ def tile_meg_forward_whitened_d3_kernel(tc, g_bytes, g_scale, j_in, gain_in, e_i
         j_grp, j_mx, field = {}, {}, {}
 
         def j_joint(g, engine, n0=0, n1=WIDE[1]):
-            interleave(engine, joint_part(g, SEN + n0, SEN + n1), j_planes(g, (n0, n1 - n0)))
+            interleave(engine, joint_part(g, SEN + n0, SEN + n1), *j_planes(g, (n0, n1 - n0)))
 
-        def j_piece(g, cols, engine, tag=None, part=None):
+        def j_piece(g, cols, engine, part=None):
             if (g, cols) not in j_grp:
-                if tag is not None:
-                    tile = keep.tile([P, cols[1], 4], BF16, name=tag, align_bytes=64)
-                elif cols[1] == REST[1]:
+                if cols[1] == REST[1]:
                     tile = work.tile([P, cols[1], 4], BF16, name="j_rest", bufs=REST_BUFS, align_bytes=64)
                 else:
                     tile = work.tile([P, cols[1], 4], BF16, name="j_grp", bufs=PIECE_BUFS, align_bytes=64)
                 j_grp[g, cols] = tile[:]
             part = part or cols
             n0 = part[0] - cols[0]
-            interleave(engine, j_grp[g, cols][:, n0:n0 + part[1], :], j_planes(g, part))
+            interleave(engine, j_grp[g, cols][:, n0:n0 + part[1], :], *j_planes(g, part))
 
         def hand_out(g, cols, codes, scales):
             for n0, w in FIELD_BANKS:
@@ -427,23 +427,28 @@ def tile_meg_forward_whitened_d3_kernel(tc, g_bytes, g_scale, j_in, gain_in, e_i
         quant_forward(4, MID)
         joint_quant(7)
         forward(7, WIDE)
-        j_piece(4, LAST, "scalar", tag="hand")
+        hand = keep.tile([P, 4 * REST[1]], BF16, name="hand", align_bytes=64)
+        hand = hand[:].rearrange("p (n t) -> p n t", t=4)
+        j_grp[4, LAST] = hand[:, MID[1]:, :]
+        j_piece(4, LAST, "scalar")
         j_quant(4, LAST)
         j_quant(5, REST)
         forward(5, MID)
         forward(5, LAST)
         forward(4, LAST)
-        j_piece(0, LAST, "gpsimd", tag="hand")
-        for g in (0, 7, 6, 1):
+        j_grp[0, REST] = hand
+        j_piece(0, REST, "scalar", part=(REST[0], REST[1] - POOL_COLS))
+        j_piece(0, REST, "gpsimd", part=(TIM - POOL_COLS, POOL_COLS))
+        for g in (7, 6, 1):
             j_piece(g, MID, "scalar")
         record(WIDE, WIDE, range(4))
-        quant_forward(0, MID)
-        quant_forward(0, LAST)
         quant_forward(7, MID)
+        quant_forward(0, REST)
         quant_forward(6, MID)
+        b_interleave(WIDE, "scalar", 0, SCALAR_B)
         for g in (7, 6, 1):
             j_piece(g, LAST, "scalar")
-        b_interleave(WIDE, "vector")
+        b_interleave(WIDE, "vector", SCALAR_B, WIDE[1])
         quant_forward(1, MID)
         whiten(WIDE, (0, 1, 2, 3))
         for i in range(4):

from contextlib import ExitStack

import concourse.mybir as mybir
from concourse.masks import make_identity

SRC, SEN, TIM = 4096, 512, 1024
FLOPS = 2 * SRC * SEN * TIM + 2 * SEN * SEN * TIM

F32 = mybir.dt.float32
BF16 = mybir.dt.bfloat16
U32 = mybir.dt.uint32
U8 = mybir.dt.uint8
FP8 = mybir.dt.float8_e4m3fn
FP8X4 = mybir.dt.float8_e4m3fn_x4
MULT = mybir.AluOpType.mult
ADD = mybir.AluOpType.add
COPY = mybir.ActivationFunctionType.Copy

P = 128
PASSES = SRC // 512
FINAL = PASSES - 1
WIDE, MID, LAST_A, LAST_B = (0, 512), (512, 256), (768, 128), (896, 128)
LAST = (768, 256)
REST = (512, 512)
ROUTED = (0, 2, 3, 4, 5, 6)
PLANE_GAP, PAIR_GAP = 20, 20
JOINT_COLS = SEN + 512
JOINT_BUFS, WIDENED_BUFS, PIECE_BUFS, REST_BUFS = 4, 4, 4, 2
FIELD_BANKS = {WIDE: (0, 1, 2, 3), MID: (4, 5), LAST: (6, 7)}
SPLIT_PLANE = 256
SPLIT_LOADS = (0, 1)
POOL_COLS = 352
SCALAR_B = 96


def tile_meg_forward_whitened_d3_kernel(tc, g_bytes, g_scale, j_in, gain_in, e_in, v_in, out):
    nc = tc.nc

    with ExitStack() as ctx:
        keep = ctx.enter_context(tc.tile_pool(name="keep", bufs=1))
        work = ctx.enter_context(tc.tile_pool(name="work", bufs=3))
        psum = ctx.enter_context(tc.psum_pool(name="psum", bufs=1))
        ctx.enter_context(tc.manual_schedule())


        gs_view = g_scale.rearrange("(g p t) o -> p g (t o)", p=P, t=4)
        gb_view = g_bytes.rearrange("(g p t) s -> g p t s", p=P, t=4)
        j_view = j_in.rearrange("(g p t) n -> g p t n", p=P, t=4)
        e_view = e_in.rearrange("(p u) n -> p u n", u=4)
        g_raw, g_sc, j_raw, noise = {}, {}, {}, []

        def load_scales(g0, g1):
            tile = keep.tile([P, g1 - g0, 8], F32, name="g_sc%d" % g0)
            queue = nc.scalar if g0 < 1 else nc.sync
            queue.dma_start(out=tile[:, :, :4], in_=gs_view[:, g0:g1, :])
            for g in range(g0, g1):
                g_sc[g] = tile[:, g - g0, :4]

        def load_g(g):
            g_raw[g] = keep.tile([P, 4, SEN], U8, name="g_raw%d" % g, align_bytes=64)
            for t0, t1 in ((0, 2), (2, 4)) if g in SPLIT_LOADS else ((0, 4),):
                nc.sync.dma_start(out=g_raw[g][:, t0:t1, :], in_=gb_view[g][:, t0:t1, :])

        def load_j(g, n0, n1):
            name = "j_raw%d_%d" % (g, n0)
            if n1 - n0 == TIM:
                tile = keep.tile([P, 2, 2 * TIM + PAIR_GAP], BF16, name=name, align_bytes=64)
                nc.sync.dma_start(out=tile[:, :, :2 * TIM], in_=j_view[g].rearrange("p (h e) n -> p h (e n)", h=2))
                planes = tile[:, :, :2 * TIM].rearrange("p h (e n) -> p h e n", e=2)
            else:
                tile = keep.tile([P, 4, n1 - n0 + PLANE_GAP], BF16, name=name, align_bytes=64)
                nc.sync.dma_start(out=tile[:, :, :n1 - n0], in_=j_view[g][:, :, n0:n1])
                planes = tile[:, :, :n1 - n0].rearrange("p (h e) n -> p h e n", e=2)
            j_raw.setdefault(g, []).append((n0, n1, planes, "c e h i" if n1 - n0 == TIM else "c h e i"))

        def j_planes(g, cols):
            first, width = cols
            for n0, n1, planes, walk in j_raw[g]:
                if n0 <= first and first + width <= n1:
                    return planes[:, :, :, first - n0:first - n0 + width], walk
            raise ValueError("columns not loaded")

        def load_e(n0, n1):
            tile = keep.tile([P, 4, n1 - n0], BF16, name="noise%d" % n0, align_bytes=64)
            nc.sync.dma_start(out=tile[:], in_=e_view[:, :, n0:n1])
            noise.append((n0, n1, tile))

        v_raw = keep.tile([P, 4, SEN], BF16, name="v_raw", align_bytes=64)
        gain = keep.tile([P, 4], BF16, name="gain")

        def load_v():
            nc.sync.dma_start(out=v_raw[:], in_=v_in.rearrange("(p b) s -> p b s", b=4))

        def load_gain():
            nc.sync.dma_start(out=gain[:], in_=gain_in.rearrange("(p u) -> p u", u=4))

        half = WIDE[1]
        load_scales(0, 3)
        zeros = keep.tile([P, P], F32, name="zeros")
        nc.vector.memset(zeros[:], 0.0)
        ident_b = keep.tile([P, P], BF16, name="ident_b")
        make_identity(nc, ident_b[:])
        ident = keep.tile([P, P], F32, name="ident")
        nc.scalar.activation(out=ident[:], in_=zeros[:], func=COPY)
        make_identity(nc, ident[:], nomemset=True)
        load_g(0)
        load_g(1)
        load_g(2)
        load_j(0, 0, half)
        load_scales(3, 5)
        load_g(3)
        for g in range(1, 5):
            if g > 1:
                load_scales(g + 3, g + 4)
            load_g(g + 3)
            load_j(g, 0, half if g == 1 else TIM)
        load_j(5, 0, TIM)
        load_v()
        load_j(6, 0, half)
        load_j(7, 0, TIM)
        load_j(0, half, TIM)
        load_gain()
        load_e(0, half)
        load_j(6, half, TIM)
        load_j(1, half, TIM)
        load_e(half, TIM)

        def quantize(name, grouped, width):
            codes = keep.tile([P, width], U32, name="codes_" + name, align_bytes=64)
            scales = keep.tile([P, width], U8, name="scales_" + name, align_bytes=64)
            nc.vector.quantize_mx(
                out=codes[:].bitcast(FP8X4), scales=scales[:], in_=grouped.rearrange("p n t -> p (n t)")
            )
            return codes, scales

        def interleave(engine, grouped, planes, walk="c h e i"):
            if engine == "gpsimd":
                nc.gpsimd.tensor_scalar(
                    out=grouped.rearrange("p n (h e) -> p n h e", e=2),
                    in0=planes.rearrange("p h e n -> p n h e"),
                    scalar1=1.0,
                    scalar2=0.0,
                    op0=MULT,
                    op1=ADD,
                )
                return
            dst = grouped.rearrange("p (c i) (h e) -> p " + walk, i=2, e=2)
            src = planes.rearrange("p h e (c i) -> p " + walk, i=2)
            if engine == "scalar":
                nc.scalar.copy(out=dst, in_=src)
            else:
                nc.vector.tensor_copy(out=dst, in_=src)

        joint = {}

        def joint_part(g, n0, n1):
            if g not in joint:
                joint[g] = work.tile([P, 4 * JOINT_COLS], BF16, name="joint", bufs=JOINT_BUFS, align_bytes=64)
            return joint[g][:, 4 * n0:4 * n1].rearrange("p (n t) -> p n t", t=4)

        def g_grouped(g):
            return joint_part({0: 0, 1: "alone"}.get(g, g - 1), 0, SEN)

        g_wide, g_mx, g_psum = {}, {}, {}

        def widen(g, t, on_vector, n0=0, n1=SEN):
            if g not in g_wide:
                g_wide[g] = work.tile([P, 4, SEN], BF16, name="g_wide", bufs=WIDENED_BUFS, align_bytes=64)
            scale = g_sc[g][:, t:t + 1]
            src = g_raw[g][:, t, n0:n1].bitcast(FP8)
            if on_vector:
                nc.vector.tensor_scalar(out=g_wide[g][:, t, n0:n1], in0=src, scalar1=scale, scalar2=None, op0=MULT)
            else:
                nc.scalar.activation(out=g_wide[g][:, t, n0:n1], in_=src, func=COPY, scale=scale)

        def widen_pass(g, on_scalar=()):
            for t in range(4):
                widen(g, t, on_vector=t not in on_scalar)

        def g_interleave(g):
            nc.vector.tensor_copy(
                out=g_grouped(g).rearrange("p (u c i) t -> p c u t i", u=4, i=2),
                in_=g_wide[g][:].rearrange("p t (c i u) -> p c u t i", u=4, i=2),
            )

        def g_route(g, planes_first=False):
            bank = 4 + 2 * (ROUTED.index(g) % 2)
            for q in range(2):
                g_psum[g, q] = psum.tile([P, 4, 64, 4], BF16, name="bank%d" % (bank + q))
            for step in range(4):
                q, t0 = (step % 2, 2 * (step // 2)) if planes_first else (step // 2, 2 * (step % 2))
                nc.tensor.matmul(
                    out=g_psum[g, q][:, :, :, t0:t0 + 2].rearrange("p u m t -> p t m u"),
                    lhsT=ident_b[:],
                    rhs=g_wide[g][:, t0:t0 + 2, 256 * q:256 * (q + 1)].rearrange("p t (m u) -> p t m u", u=4),
                    start=True,
                    stop=True,
                )

        def g_fetch(g, halves=(0, 1)):
            dst = g_grouped(g).rearrange("p (u m) t -> p u (m t)", u=4).bitcast(F32)
            for q in halves:
                nc.scalar.copy(
                    out=dst[:, :, 128 * q:128 * (q + 1)],
                    in_=g_psum[g, q][:].rearrange("p u m t -> p u (m t)").bitcast(F32),
                )

        j_grp, j_mx, field = {}, {}, {}

        def j_joint(g, engine, n0=0, n1=WIDE[1]):
            interleave(engine, joint_part(g, SEN + n0, SEN + n1), *j_planes(g, (n0, n1 - n0)))

        def j_piece(g, cols, engine, part=None):
            if (g, cols) not in j_grp:
                if cols[1] == REST[1]:
                    tile = work.tile([P, cols[1], 4], BF16, name="j_rest", bufs=REST_BUFS, align_bytes=64)
                else:
                    tile = work.tile([P, cols[1], 4], BF16, name="j_grp", bufs=PIECE_BUFS, align_bytes=64)
                j_grp[g, cols] = tile[:]
            part = part or cols
            n0 = part[0] - cols[0]
            interleave(engine, j_grp[g, cols][:, n0:n0 + part[1], :], *j_planes(g, part))

        def hand_out(g, cols, codes, scales):
            for n0, w in FIELD_BANKS:
                if cols[0] <= n0 and n0 + w <= cols[0] + cols[1]:
                    j_mx[g, (n0, w)] = codes[:, n0 - cols[0]:n0 - cols[0] + w], scales[:, n0 - cols[0]:n0 - cols[0] + w]

        def j_quant(g, cols):
            codes, scales = quantize("j%d_%d" % (cols[0], g), j_grp[g, cols], cols[1])
            hand_out(g, cols, codes, scales)

        def joint_quant(g):
            codes, scales = quantize("joint%d" % g, joint_part(g, 0, SEN + WIDE[1]), SEN + WIDE[1])
            hand_out(g, WIDE, codes[:, SEN:], scales[:, SEN:])
            g_mx[g + 1 if g else 0] = codes[:, :SEN], scales[:, :SEN]

        def joint_mid_quant(g):
            codes, scales = quantize("mid%d" % g, joint_part(g, SEN + MID[0], SEN + MID[0] + MID[1]), MID[1])
            hand_out(g, MID, codes, scales)

        def bank_tiles(banks, width):
            per_bank = 4 // len(banks)
            tiles = []
            for b in banks:
                tile = psum.tile([P, per_bank, width], F32, name="bank%d" % b)
                tiles.append(tile)
            return tiles, per_bank

        passes_done = {}

        def forward(g, cols):
            if cols not in passes_done:
                passes_done[cols] = []
                field[cols] = bank_tiles(FIELD_BANKS[cols], cols[1])
            passes_done[cols].append(g)
            tiles, per_bank = field[cols]
            codes, scales = j_mx[g, cols]
            for u in range(4):
                nc.tensor.matmul_mx(
                    out=tiles[u // per_bank][:, u % per_bank, :],
                    lhsT=g_mx[g][0][:, u * P:(u + 1) * P].bitcast(FP8X4),
                    lhsT_scale=g_mx[g][1][:, u * P:(u + 1) * P],
                    rhs=codes.bitcast(FP8X4),
                    rhs_scale=scales,
                    start=(len(passes_done[cols]) == 1 and u % per_bank == 0),
                    stop=(len(passes_done[cols]) == PASSES and u % per_bank == per_bank - 1),
                )

        def forward_all(g, cols):
            for stretch in FIELD_BANKS:
                if cols[0] <= stretch[0] and stretch[0] + stretch[1] <= cols[0] + cols[1]:
                    forward(g, stretch)

        def quant_forward(g, cols):
            j_quant(g, cols)
            forward_all(g, cols)

        v_psum = []

        def v_turn():
            words = v_raw[:].rearrange("p b s -> p (b s)").bitcast(F32)
            for h in range(2):
                turned = psum.tile([P, 2, 2, P], F32, name="bank%d" % (6 + h))
                v_psum.append(turned)
                for b in range(2):
                    for w in range(2):
                        w0 = (2 * h + b) * 256
                        nc.tensor.transpose(turned[:, b, w, :], words[:, w0 + w:w0 + 256:2], ident[:])

        def v_fetch():
            for h in range(2):
                dst = g_grouped(PASSES).rearrange("p n t -> p (n t)").bitcast(F32)[:, 512 * h:512 * (h + 1)]
                nc.scalar.copy(
                    out=dst.rearrange("p (b r w) -> p b r w", b=2, w=2),
                    in_=v_psum[h][:].rearrange("p b w r -> p b r w"),
                )

        b_planes, b_grp, b_mx, white = {}, {}, {}, {}

        def record(cols, stretch, planes):
            first, width = cols
            if cols not in b_planes:
                b_planes[cols] = work.tile(
                    [P, 4, width + PLANE_GAP], BF16, name="g_wide", bufs=WIDENED_BUFS, align_bytes=64
                )
            tiles, per_bank = field[stretch]
            n0 = first - stretch[0]
            e0, e_tile = [(a, tile) for a, b, tile in noise if a <= first < b][0]
            for u in planes:
                nc.vector.scalar_tensor_tensor(
                    out=b_planes[cols][:, u, :width],
                    in0=tiles[u // per_bank][:, u % per_bank, n0:n0 + width],
                    scalar=gain[:, u:u + 1],
                    in1=e_tile[:, u, first - e0:first - e0 + width],
                    op0=MULT,
                    op1=ADD,
                )

        def b_interleave(cols, engine, n0=0, n1=None):
            n1 = n1 or cols[1]
            if cols not in b_grp:
                b_grp[cols] = work.tile([P, cols[1], 4], BF16, name="joint", bufs=JOINT_BUFS, align_bytes=64)
            planes = b_planes[cols][:, :, n0:n1].rearrange("p (h e) n -> p h e n", e=2)
            interleave(engine, b_grp[cols][:, n0:n1, :], planes)

        def b_quant(cols, n0=0, n1=None):
            n1 = n1 or cols[1]
            if cols not in b_mx:
                codes = keep.tile([P, cols[1]], U32, name="codes_b%d" % cols[0], align_bytes=64)
                scales = keep.tile([P, cols[1]], U8, name="scales_b%d" % cols[0], align_bytes=64)
                b_mx[cols] = codes, scales
            codes, scales = b_mx[cols]
            nc.vector.quantize_mx(
                out=codes[:, n0:n1].bitcast(FP8X4),
                scales=scales[:, n0:n1],
                in_=b_grp[cols][:, n0:n1, :].rearrange("p n t -> p (n t)"),
            )

        def whiten(cols, banks):
            if cols not in b_mx:
                b_quant(cols)
            codes, scales = b_mx[cols]
            v_mx = g_mx[PASSES]
            white[cols] = bank_tiles(banks, cols[1])
            tiles, per_bank = white[cols]
            for b in range(4):
                nc.tensor.matmul_mx(
                    out=tiles[b // per_bank][:, b % per_bank, :],
                    lhsT=v_mx[0][:, b * P:(b + 1) * P].bitcast(FP8X4),
                    lhsT_scale=v_mx[1][:, b * P:(b + 1) * P],
                    rhs=codes[:].bitcast(FP8X4),
                    rhs_scale=scales[:],
                    start=True,
                    stop=True,
                )

        out_view = out.rearrange("(p b) n -> p b n", b=4)
        spent = ["j_raw%d_0" % g for g in range(PASSES)] + ["v_raw", "noise0", "g_raw0", "g_raw1"]

        def store(cols, i, on_scalar):
            first, width = cols
            tiles, per_bank = white[cols]
            rows = per_bank * len(on_scalar)
            y = keep.tile([P, rows, width], F32, name=spent.pop(0), align_bytes=64)
            for k, scalar in enumerate(on_scalar):
                part = y[:, k * per_bank:(k + 1) * per_bank, :]
                if scalar:
                    nc.scalar.copy(out=part, in_=tiles[i + k][:])
                else:
                    nc.vector.tensor_copy(out=part, in_=tiles[i + k][:])
            nc.sync.dma_start(out=out_view[:, i * per_bank:i * per_bank + rows, first:first + width], in_=y[:])

        widen_pass(0, on_scalar=(1, 3))
        g_route(0)
        widen_pass(1, on_scalar=(3,))
        widen(2, 0, on_vector=True)
        g_interleave(1)
        for t in range(1, 4):
            widen(2, t, on_vector=False)
        g_fetch(0)
        g_route(2, planes_first=True)
        j_joint(0, "vector")
        widen_pass(3, on_scalar=(2, 3))
        g_route(3, planes_first=True)
        for q in range(2):
            widen(4, q, True, 0, SEN if q == 0 else SPLIT_PLANE)
            if q:
                widen(4, q, False, SPLIT_PLANE, SEN)
            g_fetch(2, (q,))
            widen(4, 2 + q, on_vector=False)
        joint_quant(0)

        for g in range(1, 5):
            if g + 3 in ROUTED:
                g_route(g + 3)
            forward(g - 1, WIDE)
            g_fetch(g + 2)
            if g + 4 < PASSES:
                widen_pass(g + 4, on_scalar=range(4))
            j_joint(g, "vector")
            if g == 1:
                g_mx[1] = quantize("g1", g_grouped(1), SEN)
            if g - 1 in (2, 3):
                j_quant(g - 1, REST)
            if g in (2, 3):
                j_piece(g, REST, "vector")
            if g == 4:
                forward(2, MID)
                v_turn()
            joint_quant(g)
        forward(4, WIDE)
        g_interleave(FINAL)
        j_joint(5, "scalar")
        v_fetch()
        j_joint(6, "vector")
        forward(3, MID)
        joint_quant(5)
        forward(2, LAST)
        forward(5, WIDE)
        j_piece(4, MID, "scalar")
        j_joint(7, "scalar")
        joint_quant(6)
        forward(3, LAST)
        forward(6, WIDE)
        j_piece(5, REST, "vector")
        quant_forward(4, MID)
        joint_quant(7)
        forward(7, WIDE)
        hand = keep.tile([P, 4 * REST[1]], BF16, name="hand", align_bytes=64)
        hand = hand[:].rearrange("p (n t) -> p n t", t=4)
        j_grp[4, LAST] = hand[:, MID[1]:, :]
        j_piece(4, LAST, "scalar")
        j_quant(4, LAST)
        j_quant(5, REST)
        forward(5, MID)
        forward(5, LAST)
        forward(4, LAST)
        j_grp[0, REST] = hand
        j_piece(0, REST, "scalar", part=(REST[0], REST[1] - POOL_COLS))
        j_piece(0, REST, "gpsimd", part=(TIM - POOL_COLS, POOL_COLS))
        for g in (7, 6, 1):
            j_piece(g, MID, "scalar")
        record(WIDE, WIDE, range(4))
        quant_forward(7, MID)
        quant_forward(0, REST)
        quant_forward(6, MID)
        b_interleave(WIDE, "scalar", 0, SCALAR_B)
        for g in (7, 6, 1):
            j_piece(g, LAST, "scalar")
        b_interleave(WIDE, "vector", SCALAR_B, WIDE[1])
        quant_forward(1, MID)
        whiten(WIDE, (0, 1, 2, 3))
        for i in range(4):
            store(WIDE, i, (True,))
        quant_forward(7, LAST)
        record(MID, MID, (0, 1))
        quant_forward(6, LAST)
        record(MID, MID, (2, 3))
        quant_forward(1, LAST)
        b_interleave(MID, "vector", 0, 128)
        b_interleave(MID, "vector", 128, 256)
        b_quant(MID, 0, 128)
        b_quant(MID, 128, 256)
        whiten(MID, (4, 5))
        for i in range(2):
            store(MID, i, (True,))
        record(LAST_A, LAST, range(4))
        record(LAST_B, LAST, (0, 1))
        b_interleave(LAST_A, "vector")
        record(LAST_B, LAST, (2, 3))
        whiten(LAST_A, (0, 1))
        b_interleave(LAST_B, "vector", 0, 64)
        b_interleave(LAST_B, "vector", 64, 128)
        b_quant(LAST_B, 0, 64)
        b_quant(LAST_B, 64, 128)
        whiten(LAST_B, (2, 3, 4, 5))
        for i in range(2):
            store(LAST_A, i, (i == 0,))
        for i in (0, 2):
            store(LAST_B, i, (True, False))
